import numpy as np, ml_dtypes
CORES = [40,64,80,88,96,104,120,144]
N = 8
BF = ml_dtypes.bfloat16
def gentries(a):
    return np.ascontiguousarray(a.reshape(8, 16, -1).transpose(0, 2, 1)).reshape(8, -1)
def gtable(e):
    e = np.asarray(e); return np.ascontiguousarray(e.reshape(8, -1, 16).transpose(0, 2, 1)).reshape(128, -1).astype(np.int32)
def f(rng, *shape):
    return (rng.standard_normal(shape, dtype=np.float32) * np.exp2(rng.integers(-2, 3, shape[:-1] + (1,)))).astype(BF)
def wide(rng, *shape):
    v = f(rng, *shape).astype(np.float32); k = shape[:-2] + (1, shape[-1])
    return (v * np.exp2(rng.integers(-6, 7, k)) * (rng.random(k) > 0.0625)).astype(BF)
V, G, S, P, RO, VO = 1024, 256, 256, 2, 3, 9
def parts(rng):
    sd = (rng.random((N, 8, V)) < 0.3 + 0.4 * rng.random((N, 8, 1))).astype(np.int64)
    nr = rng.integers(0, S, (N, 8, V)); hs = np.ascontiguousarray(np.argsort(rng.random((N, 8, V)), axis=-1)[..., :S])
    tl = rng.integers(0, V, (N, 8, 16, V)); tl = np.where(rng.random(tl.shape) < 0.2, V + rng.integers(0, G, tl.shape), tl)
    u = 0.6 * rng.standard_normal((N, 8, 16, V)) + np.where(sd == 0, 0.5, -0.5)[:, :, None, :]
    c = 0.5 * rng.standard_normal((N, 8, 16, S)); lean = 0.4 * rng.choice(np.array([-1.0, -0.5, 0.0, 0.5, 1.0]), (N, 8, 1, S))
    w = np.stack([c + lean + 0.3 * rng.standard_normal(c.shape), c - lean + 0.3 * rng.standard_normal(c.shape)], axis=-1)
    th = rng.integers(0, 48, (N, 8, 16, 1)) * 0.015625
    return sd, nr, hs, tl, u, w, th
def pack(sd, nr, hs, tl, u, w, th):
    def cut(a, n): return np.where(np.abs(a) < 2.0 ** -20, 0.0, np.clip(a, -2.0, 2.0)).reshape(N, 128, n).astype(np.float32).astype(BF)
    return {"tl": np.ascontiguousarray(tl.reshape(N, 128, V)).astype(np.int32), "u0": cut(u, V), "w0": cut(w, 2 * S), "sd": sd.astype(np.int32), "nr": nr.astype(np.int32),
            "hs": hs.astype(np.int32), "th": th.reshape(N, 128, 1).astype(np.float32)}
def still(rng, p, r, g, up, fine):
    sd, nr, hs, tl, u, w, th = p
    a1 = rng.integers(-48, 49, (16, 1)) * 0.015625; gap = rng.integers(1, 65, (16, 1)) * 0.015625; sign = 1.0 if up else -1.0; a0 = a1 + sign * gap
    tl[r, g] = tl[r, g] % V; u[r, g] = np.where(sd[r, g] == 0, a0, a1)
    n = rng.choice(np.array([0, 1, VO - 1, VO - 1, VO, VO, 15, 16]), S); m = np.argsort(rng.random((16, S)), axis=0) < n
    w[r, g, :, :, 0] = a0 + sign * np.where(m, 0.0078125, 0.0); w[r, g, :, :, 1] = a1
    th[r, g] = gap + (0.0078125 - 0.000244140625 if fine else 0.0)
def hang(rng, p, r, g, up):
    sd, nr, hs, tl, u, w, th = p; z = 0 if up else 1
    kind = rng.permutation(np.arange(16) % 3)[:, None]; m = 1 + rng.integers(1, 64, (16, 1)) * 0.0078125; j = rng.integers(1, 17, (16, 1)) * 0.0078125
    base = np.where(kind == 0, -2.0 ** -20 - 2.0 ** -27, np.where(kind == 1, m, (2 * rng.integers(64, 128, (16, 1)) + 1) * 2.0 ** -17))
    at = np.where(kind == 1, m + j, m); dif = (at - base).astype(np.float32)
    th[r, g] = np.where(kind == 0, dif, np.nextafter(dif, np.float32(0)))
    o = np.argsort(rng.random((16, S)), axis=0); step = rng.integers(1, 33, (16, S)) * 0.0078125
    w[r, g, :, :, z] = at + np.where(o < VO - 1, step, np.where(o == VO - 1, 0.0, -step)); w[r, g, :, :, 1 - z] = base
    sd[r, g] = 1 - z; tl[r, g] = tl[r, g] % V; u[r, g] = base
def full(rng, p, r, g, c):
    sd, nr, hs, tl, u, w, th = p; E = S // 2; z = int(rng.integers(0, 2))
    v = np.arange(V)
    if c in (1, 3, 6): v = np.roll(v, E - G)
    if c in (4, 7): v = rng.permutation(V)
    to = np.zeros(S, np.int64); to[0::2] = rng.permutation(v[:E]); to[1::2] = rng.permutation(v[E:S]); sd[r, g, to] = 1 - z
    if c < 2: to[S - 2] = to[0]
    k = np.arange(16)[:, None]; k0 = rng.integers(0, 4, S); own = rng.integers(0, V, (16, S)); gh = V + rng.integers(0, G, (16, S))
    nm = np.where(k < k0, gh, np.where(k == k0, to, own))
    if c in (2, 3, 4): nm[:, 1::2] = gh[:, 1::2]
    tl[r, g][:, hs[r, g]] = nm
    h = 1.25 if z == 0 else -1.25
    u[r, g] = np.where(sd[r, g] == 0, h, -h) + 0.25 * (2 * rng.random((16, V)) - 1)
    w[r, g] = np.array([h, -h]) + 0.25 * (2 * rng.random((16, S, 2)) - 1)
    th[r, g] = rng.integers(0, 33, (16, 1)) * 0.015625
def setup_inputs(rng):
    return pack(*parts(rng))
def setup_inputs_spread(rng):
    sd, nr, hs, tl, u, w, th = parts(rng)
    u = wide(rng, N, 128, V).astype(np.float64).reshape(N, 8, 16, V) * 0.0625
    w = wide(rng, N, 128, 2 * S).astype(np.float64).reshape(N, 8, 16, S, 2) * 0.0625
    b = rng.integers(0, 3, (N, 8, 1, S, 1)); z = np.array([1.0, -1.0])
    w = np.where(b == 0, w, np.where(b == 1, np.abs(w) * z, -np.abs(w) * z))
    th = np.exp2(rng.integers(-10, 2, (N, 8, 16, 1))) * (rng.random((N, 8, 16, 1)) > 0.125)
    return pack(sd, nr, hs, tl, u, w, th)
def setup_inputs_ends(rng):
    sd, nr, hs, tl, u, w, th = parts(rng)
    def ends(shape, hi, share): return np.where(rng.random(shape) < share, hi * rng.integers(0, 2, shape), rng.integers(0, hi + 1, shape))
    nr = ends((N, 8, V), S - 1, 0.75); hs = ends((N, 8, S), V - 1, 0.75); tl = ends((N, 8, 16, V), V + G - 1, 0.75)
    u = np.where(rng.random((N, 8, 1, V)) < 0.5, 4.0 * rng.integers(0, 2, (N, 8, 1, V)) - 2, 4.0 * rng.integers(0, 2, (N, 8, 16, V)) - 2)
    z = np.array([2.0, -2.0]); b = rng.integers(0, 4, (N, 8, 1, S, 1)); free = 4.0 * rng.integers(0, 2, (N, 8, 16, S, 2)) - 2
    n = VO - rng.integers(0, 2, (N, 8, 1, S)); m = (np.argsort(rng.random((N, 8, 16, S)), axis=2) < n)[..., None]
    w = np.where(b == 0, z, np.where(b == 1, -z, np.where(b == 2, free, np.where(m, z, -2.0))))
    th = 2.0 * rng.integers(0, 2, (N, 8, 16, 1))
    tl = np.where(tl == G - 1, G - 2, np.where(tl == V - 1, V - 2, tl)); hs = np.where(hs == G - 1, G - 2, hs)
    for g in range(8):
        far = 2.0 if g % 2 == 0 else -2.0
        sd[:, g, G - 1] = 0; u[:, g, :, G - 1] = far; tl[:, g, :, G - 1] = G - 1
        if g in (0, 7):
            for v in (0, V - 1): sd[:, g, v] = 0; u[:, g, :, v] = far; tl[:, g, :, v] = V + G - 1
    return pack(sd, nr, hs, tl, u, w, th)
def setup_inputs_corners(rng):
    p = parts(rng); sd, nr, hs, tl, u, w, th = p
    for r in range(N):
        o = rng.permutation(8)
        for g in range(8):
            c = int(o[g])
            if c < 2: sd[r, g] = c
            elif c == 2: tl[r, g] = V + tl[r, g] % G
            elif c == 3: tl[r, g] = np.arange(V)
            elif c == 4:
                tl[r, g] = rng.choice(np.array([0, V - 1, V, V + G - 1]), (16, V)); hs[r, g] = np.where(rng.random(S) < 0.5, rng.choice(np.array([0, V - 1]), S), hs[r, g])
            elif c == 5:
                hs[r, g, 0::2] = int(rng.integers(0, V)); hs[r, g, 1::4] = V - 1; hs[r, g, 3::4] = 0; nr[r, g] = rng.choice(np.array([0, S - 1]), V)
            elif c == 6:
                own = rng.integers(0, V, (16, V)); gh = V + rng.integers(0, G, (16, V)); k = np.arange(16)[:, None]; v = np.arange(V)
                tl[r, g] = np.where(k == np.where(v % 2 == 0, 15, 0), own, gh)
            else: still(rng, p, r, g, r % 2 == 0, False)
    return pack(*p)
def setup_inputs_crowd(rng):
    p = parts(rng); sd, nr, hs, tl, u, w, th = p; most = rng.permutation(N)[:N // 2]
    for r in range(N):
        o = rng.permutation(8)
        for g in range(8):
            c = int(o[g])
            if r in most:
                full(rng, p, r, g, c); continue
            if c > 3: continue
            z = int(rng.integers(0, 2)); q = 1 + rng.permutation(V - 2)[:16]
            if c == 0: q[0] = V - 1
            if c == 1: q[0] = 0
            sd[r, g, q] = 1 - z; tl[r, g] = q[:, None]
            if c == 1:
                for j in (0, 1): tl[r, g, :, hs[r, g, 2 * int(rng.integers(0, S // 2)) + j]] = rng.integers(0, V, 16)
            if c == 2: tl[r, g] = q[(np.arange(16)[:, None] + np.arange(V) % 3) % 16]
            if c == 3: tl[r, g] = np.where(rng.random(V) < 0.5, rng.integers(0, V, (16, V)), tl[r, g])
            h = 1.25 if z == 0 else -1.25
            u[r, g] = np.where(sd[r, g] == 0, h, -h) + 0.25 * (2 * rng.random((16, V)) - 1)
            w[r, g] = np.array([h, -h]) + 0.25 * (2 * rng.random((16, S, 2)) - 1)
            th[r, g] = rng.integers(0, 33, (16, 1)) * 0.015625
    return pack(*p)
def setup_inputs_calm(rng):
    p = parts(rng)
    for r in range(N):
        o = rng.permutation(8)
        for g in range(8):
            c = int(o[g])
            if c < 4: still(rng, p, r, g, c % 2 == 0, c > 1)
            elif c < 6: hang(rng, p, r, g, c == 4)
    return pack(*p)
def check_inputs(d):
    bad = []
    for k, lo, hi in (("tl", 0, V + G - 1), ("u0", -2, 2), ("w0", -2, 2), ("sd", 0, 1), ("nr", 0, S - 1), ("hs", 0, V - 1), ("th", 0, 2)):
        a = np.asarray(d[k]).astype(np.float64)
        if not (np.min(a) >= lo and np.max(a) <= hi): bad.append("range of " + k)
        if k in ("u0", "w0", "th") and np.any((a != 0) & (np.abs(a) < 2.0 ** -20)): bad.append("least size of " + k)
    return bad
def tree(q):
    for h in (8, 4, 2, 1): q = q[..., :h, :] + q[..., h:, :]
    return q[..., 0, :]
def ext(a):
    b = np.roll(a, -1, axis=0)
    return np.concatenate([a, b[..., :G // 2], np.roll(b, -1, axis=1)[..., G // 2:G]], axis=-1)
def reference(tl, u0, w0, sd, nr, hs, th):
    t = tl.astype(np.int64).reshape(N, 8, 16, V); u = np.array(u0.astype(np.float32).reshape(N, 8, 16, V)); w = np.array(w0.astype(np.float32).reshape(N, 8, 16, S, 2))
    side = sd.astype(np.int64); near = nr.astype(np.int64); host = hs.astype(np.int64); lim = th.astype(np.float32).reshape(N, 8, 16, 1); c = np.float32(0.015625)
    for rnd in range(RO):
        view = [ext(np.where((side == z)[:, :, None, :], u, np.take_along_axis(w[..., z], near[:, :, None, :], 3))) for z in (0, 1)]
        es = ext(side)
        v = np.arange(rnd % P, V, P); ix = t[..., v] + (V + G) * side[..., v][:, :, None, :]
        x = np.take_along_axis(np.concatenate(view, axis=3), ix.reshape(N, 8, 1, -1), 3).reshape(N, 8, 16, 16, len(v))
        d = x - u[..., v][..., None, :]; nu = u.copy(); nu[..., v] = u[..., v] + tree(d * np.abs(d)) * c
        s = np.arange(rnd % 2, S, 2); name = np.take_along_axis(t, host[..., s][:, :, None, :], 3)
        flat = name.reshape(N, 8, -1); e = np.take_along_axis(es, flat, 2).reshape(name.shape)
        x = np.take_along_axis(np.where((es == 0)[:, :, None, :], view[0], view[1]), flat[:, :, None, :], 3).reshape(N, 8, 16, 16, len(s))
        new = []
        for z in (0, 1):
            old = w[..., z][..., s]; d = np.where((e == z)[:, :, None], x - old[..., None, :], np.float32(0))
            new.append(old + tree(d * np.abs(d)) * c)
        diff = new[0] - new[1]
        up = np.count_nonzero(diff > lim, axis=2) >= VO; dn = np.count_nonzero(diff < -lim, axis=2) >= VO
        sg = np.where(up, 0, 1); fit = (up | dn)[:, :, None] & (name < V) & (e == 1 - sg[:, :, None])
        k = np.argmax(fit, axis=2); ok = np.any(fit, axis=2)
        claim = np.where(ok, np.take_along_axis(name, k[:, :, None], 2)[:, :, 0], V)
        a, b, i = np.nonzero(ok); first = np.full((N, 8, V + 1), S, np.int64); np.minimum.at(first, (a, b, claim[a, b, i]), i)
        a, b, i = np.nonzero(ok & (np.take_along_axis(first, claim, 2) == np.arange(len(s))))
        n = claim[a, b, i]; z = sg[a, b, i]
        w[..., s, 0] = new[0]; w[..., s, 1] = new[1]; u = nu
        u[a, b, :, n] = w[a, b, :, s[i], z]; side[a, b, n] = z; near[a, b, n] = s[i]; host[a, b, s[i]] = n
    return {"yu": u.reshape(N, 128, V), "ys": w.reshape(N, 128, 2 * S), "yc": (2 * near + side).astype(np.float32), "yh": host.astype(np.float32)}

@@ -1,0 +1,762 @@
+from concourse.bass import DstId, RemoteDMATransfer
+from concourse.mybir import AluOpType, AxisListType, ActivationFunctionType
+
+AL = AluOpType
+AF = ActivationFunctionType
+F32, BF, I32, U16 = "float32", "bfloat16", "int32", "uint16"
+
+ALL = (0, 1, 2, 3)
+CFG = [
+    {'pe': [ALL, ALL, ALL, ALL], 'x': 'aaaaaaav', 'e': 'av', 'us': 'vv', 'xs': 'aa', 'long': [0, -1, 1, 2, 0], 'first': 0, 'gv': 'vv', 'rv': 'aavvvv', 'm': 'vaaav', 'sb': [5, 5, 4, 4, 4, 5]},
+    {'pe': [(), (), (), ()], 'x': 'aaaaaaaa', 'e': 'aa', 'us': 'aa', 'xs': '', 'long': [2, -1, 2, 2, 0], 'first': 0, 'gv': 'aa', 'rv': 'vaaavv', 'm': 'aavva', 'sb': [4, 4, 5, 4, 4, 6]},
+    {'pe': [(2, 3), (), (), ()], 'x': 'aaaaaaaa', 'e': 'aa', 'us': 'aa', 'xs': '', 'long': [2, 0, 2, 1, 2], 'first': 0, 'gv': 'av', 'rv': 'avavav', 'm': 'aaava', 'sb': [6, 6, 5, 4, 4, 5]},
+]
+
+OU, OW = 128, 1152
+OK_ = (128, 1280, 2432)
+ON, OS, OG = 3584, 4736, 5760
+
+SCRATCH = {
+    "TL": ("sbuf", [128, 1024], I32), "TL2": ("sbuf", [128, 1024], F32),
+    "UB": ("sbuf", [128, 1536], BF), "UW": ("sbuf", [128, 1664], F32),
+    "SN": ("sbuf", [128, 6016], BF),
+    "VW0": ("sbuf", [128, 2560], BF), "VW1": ("sbuf", [128, 2560], F32), "VW2": ("sbuf", [128, 2560], F32),
+    "SV0": ("sbuf", [128, 256], BF), "SV1": ("sbuf", [128, 256], F32), "SV2": ("sbuf", [128, 256], F32),
+    "SS": ("sbuf", [128, 384], BF), "SG": ("sbuf", [128, 512], BF),
+    "SBI": ("sbuf", [128, 128], I32), "SBB": ("sbuf", [128, 128], BF),
+    "HI": ("sbuf", [128, 16], I32), "HF": ("sbuf", [128, 16], F32), "HL": ("sbuf", [128, 24], U16),
+    "TH": ("sbuf", [128, 4], F32), "NTH": ("sbuf", [128, 4], F32),
+    "PI": ("sbuf", [128, 4], I32), "PC": ("sbuf", [128, 4], F32),
+    "PM": ("sbuf", [128, 128], F32), "J": ("sbuf", [128, 128], F32), "MH": ("sbuf", [128, 128], F32), "ML": ("sbuf", [128, 128], F32),
+    "IDF": ("sbuf", [128, 128], F32), "NIDF": ("sbuf", [128, 128], F32), "IDB": ("sbuf", [128, 128], BF), "NIDB": ("sbuf", [128, 128], BF),
+    "IDS": ("sbuf", [128, 128], BF), "SHF": ("sbuf", [128, 128], F32), "SHB": ("sbuf", [128, 128], BF),
+    "ONB": ("sbuf", [128, 128], BF), "ONF": ("sbuf", [128, 128], F32), "TRM": ("sbuf", [128, 128], BF),
+    "TMP": ("sbuf", [128, 512], F32), "SC": ("sbuf", [128, 16], F32),
+    "SEL": ("sbuf", [128, 2048], BF), "BC": ("sbuf", [128, 2048], BF),
+    "DG": ("sbuf", [128, 128], F32), "RS": ("sbuf", [128, 128], F32), "JK": ("sbuf", [128, 128], F32),
+    "J4": ("sbuf", [128, 256], F32), "J4B": ("sbuf", [128, 256], BF), "ZB": ("sbuf", [128, 128], BF),
+    "RG": ("sbuf", [128, 128], F32), "VC": ("sbuf", [128, 192], F32), "CC": ("sbuf", [128, 16], F32),
+    "IX": ("sbuf", [128, 1536], U16), "LV": ("sbuf", [128, 384], U16), "LA": ("sbuf", [128, 128], F32), "LM": ("sbuf", [128, 128], F32),
+    "NM2": ("sbuf", [128, 384], F32), "NMU": ("sbuf", [128, 384], U16), "OWN": ("sbuf", [128, 384], F32),
+    "E": ("sbuf", [128, 2048], BF), "XF": ("sbuf", [128, 256], F32), "XU": ("sbuf", [128, 256], U16),
+    "FIT": ("sbuf", [128, 256], BF), "FF": ("sbuf", [128, 256], F32), "CL": ("sbuf", [128, 256], F32),
+    "XS": ("sbuf", [128, 2048], F32), "US": ("sbuf", [128, 2048], F32), "XSB": ("sbuf", [128, 2048], BF), "USB": ("sbuf", [128, 2048], BF),
+    "Q0": ("sbuf", [128, 2048], F32), "Q1": ("sbuf", [128, 2048], F32),
+    "XA": ("sbuf", [128, 2048], F32), "XB": ("sbuf", [128, 2048], F32), "XC": ("sbuf", [128, 2048], F32),
+    "XH0": ("sbuf", [128, 2048], BF), "XH1": ("sbuf", [128, 2048], BF), "XH2": ("sbuf", [128, 2048], BF),
+    "DA": ("sbuf", [128, 2048], F32), "DB": ("sbuf", [128, 2048], F32), "DC": ("sbuf", [128, 2048], F32),
+    "TB": ("sbuf", [128, 1152], F32),
+    "DD": ("sbuf", [128, 128], F32), "VB": ("sbuf", [128, 256], BF), "MM": ("sbuf", [128, 128], F32), "MV": ("sbuf", [128, 256], F32),
+    "AS": ("sbuf", [128, 128], BF), "KEY": ("sbuf", [128, 128], F32), "KD": ("sbuf", [128, 128], F32), "KS": ("sbuf", [128, 128], F32),
+    "AB": ("sbuf", [128, 1024], F32), "SM": ("sbuf", [128, 96], F32), "LU": ("sbuf", [128, 24], U16), "YC": ("sbuf", [128, 128], F32),
+}
+for _b in range(8):
+    SCRATCH["P%d" % _b] = ("psum", [128, 512], F32)
+
+SEMAPHORES = (["ev", "ea", "et", "eg", "rl"] + ["d%d" % i for i in range(24)] + ["arr%d" % i for i in range(6)] + ["rin%d" % i for i in range(6)])
+ESEM = {"v": "ev", "a": "ea", "t": "et", "g": "eg"}
+
+CY, PECY, GA, SCAT, LAT_X, LAT_S, SLACK = 1.0, 0.5, 1.55, 3.8, 150.0, 90.0, 30.0
+COMM = 1.2
+BOOST, LOOK, TOL, FAR = 10000.0, 200.0, 50.0, 3000.0
+
+
+def R(name, lo, hi, step=1):
+    return (name, lo, hi, step)
+
+
+def IND(win, off):
+    return ("#ind", win, off)
+
+
+def _n(r):
+    if r[0] == "#ind":
+        return 16 * _n(r[2])
+    return (r[2] - r[1] + r[3] - 1) // r[3]
+
+
+def _psum(r):
+    return r[0] != "#ind" and SCRATCH[r[0]][0] == "psum"
+
+
+def _two(r):
+    return SCRATCH[r[0]][2] in (BF, U16)
+
+
+def _flat(rs):
+    out = []
+    for r in rs:
+        if isinstance(r, tuple):
+            out += [r[1], r[2]] if r[0] == "#ind" else [r]
+    return out
+
+
+def build():
+    ops = []
+    nsem = [0]
+    up = [0.0]
+
+    def add(eng, fn, wr, rd, cost, done=None, sem=None, after=()):
+        w, r = [], _flat(rd)
+        for o in wr:
+            if o[0] == "#ind":
+                w.append(o[1]); r.append(o[2])
+            else:
+                w.append(o)
+        ops.append({"e": eng, "fn": fn, "w": w, "r": r, "c": cost, "done": cost if done is None else done, "sem": sem, "after": list(after), "up": up[0]})
+        return len(ops) - 1
+
+    def vcost(out, a, b=None):
+        if out[0] == "#ind":
+            return 50 + SCAT * CY * _n(out)
+        if a[0] == "#ind":
+            return 50 + GA * CY * _n(a)
+        n = _n(out)
+        if b is not None:
+            n = n if (_psum(a) or _psum(b)) else 2 * n
+        elif _two(out) and _two(a):
+            n = n / 2
+        return CY * max(64, n)
+
+    def tt(out, a, b, op):
+        return add("v", lambda q, A: q.tensor_tensor(A(out), A(a), A(b), op), [out], [a, b], vcost(out, a, b))
+
+    def ts(out, a, s1, op0, s2=None, op1=None):
+        if op1 is None:
+            fn = lambda q, A: q.tensor_scalar(A(out), A(a), A(s1), None, op0)
+        else:
+            fn = lambda q, A: q.tensor_scalar(A(out), A(a), A(s1), A(s2), op0, op1)
+        return add("v", fn, [out], [a, s1, s2], vcost(out, a))
+
+    def cp(out, a):
+        return add("v", lambda q, A: q.tensor_copy(A(out), A(a)), [out], [a], vcost(out, a))
+
+    def fill(out, x):
+        return add("v", lambda q, A: q.memset(A(out), x), [out], [], CY * max(64, _n(out) / (2 if _two(out) else 1)))
+
+    def act(out, a, f, bias=0.0, scale=1.0):
+        c = 65 + GA * CY * _n(a) if a[0] == "#ind" else CY * max(64, _n(a))
+        return add("a", lambda q, A: q.activation(A(out), A(a), f, bias=A(bias), scale=A(scale)), [out], [a, bias, scale], c)
+
+    def move(eng, out, a, scale=None):
+        if eng == "a":
+            return act(out, a, AF.Identity, 0.0, 1.0 if scale is None else scale)
+        return cp(out, a) if scale is None else ts(out, a, scale, AL.mult)
+
+    def mm(items):
+        def fn(q, A):
+            for o, l, r, st, sp in items:
+                ins = q.matmul(A(o), A(l), A(r), st, sp)
+            return ins
+        c = sum(PECY * max(64, _n(r)) * (1 if _two(r) else 4) for o, l, r, st, sp in items)
+        return add("t", fn, [i[0] for i in items], [i[1] for i in items] + [i[2] for i in items], c)
+
+    def group(parts):
+        return [(o, l, r, i == 0, i == len(parts) - 1) for i, (o, l, r) in enumerate(parts)]
+
+    def iota(out, pattern, base, cm):
+        if SCRATCH[out[0]][2] == I32:
+            fn = lambda q, A: q.iota(A(out), pattern, base, cm)
+        else:
+            fn = lambda q, A: q.iota(A(out), pattern, base, cm, allow_small_or_imprecise_dtypes=True)
+        return add("g", fn, [out], [], 130 + 2 * CY * _n(out))
+
+    def dma(eng, pairs, wr, rd, nbytes, after=(), rows=128):
+        s = "d%d" % nsem[0]; nsem[0] += 1
+        def fn(q, A):
+            for o, i in pairs:
+                q.dma_start(o(A), i(A)).then_inc(A(("#sem", s)), 16)
+        return add(eng, fn, wr, rd, (1000 if eng == "g" else 70) * len(pairs), 2000 + nbytes / 150 + rows * 3, (s, 16 * len(pairs)), after)
+
+    def load(eng, out, name, nbytes, after=()):
+        return dma(eng, [(lambda A: A(out), lambda A: A(("#hbm", name))[:])], [out], [], nbytes, after)
+
+    def send(m, srcs, dsts, lat):
+        s = "d%d" % nsem[0]; nsem[0] += 1
+        i = add("g", ("send", m, srcs, dsts, s), [], srcs, 700, 2500, (s, "#sent"))
+        add("x", None, dsts, [], 0, lat * COMM - 2500, ("arr%d" % m, "#arr"), [i])
+        return i
+
+    P = lambda b, lo=0, hi=512, st=1: R("P%d" % b, lo, hi, st)
+    whole = lambda n: R(n, 0, SCRATCH[n][1][1])
+    col = lambda n, j: R(n, j, j + 1)
+    blk = lambda n, i: R(n, 128 * i, 128 * i + 128)
+
+    up[0] = 50000.0
+    load("s", R("SBI", 0, 64), "sd", 32768)
+    load("s", R("SBI", 64, 128), "nr", 32768)
+    load("a", R("UB", 1024, 1536), "w0", 131072)
+    load("a", R("UB", 0, 1024), "u0", 393216)
+    up[0] = 40000.0
+    load("s", whole("TL"), "tl", 900000)
+    up[0] = 0.0
+    load("s", col("TH", 0), "th", 512)
+    dma("s", [(lambda A, c=c: A(R("HI", 2 * c, 2 * c + 2)), lambda A, c=c: A(("#hbm", "hs"))[:, 32 * c:32 * c + 32]) for c in range(8)],
+        [whole("HI")], [], 500000, rows=1024)
+
+    iota(col("PI", 0), [[0, 1]], 0, 1)
+    iota(whole("MH"), [[1, 8], [0, 16]], 0, 0)
+    iota(whole("J"), [[1, 128]], 0, 0)
+    iota(whole("PM"), [[1, 128]], 0, -1)
+    iota(R("RG", 0, 64), [[-256, 4], [0, 16]], 0, 0)
+    iota(whole("ML"), [[0, 8], [1, 16]], 0, 0)
+    ts(col("PI", 1), col("PI", 0), 15, AL.bitwise_and)
+    ts(col("PI", 2), col("PI", 0), 4, AL.arith_shift_right)
+    cp(R("PC", 1, 3), R("PI", 1, 3))
+    lane, grp = col("PC", 1), col("PC", 2)
+    ts(whole("ONB"), whole("MH"), grp, AL.is_equal)
+    ts(whole("SC"), R("J", 0, 16), lane, AL.is_equal)
+    ts(whole("IDB"), whole("PM"), 0.0, AL.is_equal)
+    for i in range(16):
+        act(blk("BC", i), whole("ONB"), AF.Identity, 0.0, col("SC", i))
+        ts(blk("SEL", i), whole("IDB"), col("SC", i), AL.mult)
+    ts(R("VC", 0, 64), R("J", 0, 64), 16.0, AL.mult, lane, AL.add)
+    tt(R("RG", 64, 128), R("VC", 0, 64), R("RG", 0, 64), AL.add)
+    ts(R("VC", 64, 128), R("RG", 64, 128), 1024.0, AL.add)
+    ts(R("VC", 128, 192), R("RG", 64, 128), -1025.0, AL.add)
+    ts(blk("TMP", 0), whole("PM"), -16.0, AL.is_equal)
+    ts(blk("TMP", 1), whole("PM"), 112.0, AL.is_equal)
+    tt(whole("SHB"), blk("TMP", 0), blk("TMP", 1), AL.add)
+    act(whole("SHF"), whole("SHB"), AF.Identity)
+    act(whole("IDF"), whole("IDB"), AF.Identity)
+    act(whole("NIDB"), whole("IDB"), AF.Identity, 0.0, -1.0)
+    if any(CFG[t]["xs"] or any(CFG[t]["pe"]) for t in (1, 2)):
+        act(whole("NIDF"), whole("IDB"), AF.Identity, 0.0, -1.0)
+    act(whole("IDS"), whole("IDB"), AF.Identity, 0.0, 1.0 / 2048)
+    act(whole("ONF"), whole("ONB"), AF.Identity)
+    ts(blk("TMP", 2), whole("PM"), 0.0, AL.is_gt, -8192.0, AL.mult)
+    ts(blk("TMP", 3), whole("PM"), 0.0, AL.is_ge, 4096.0, AL.mult)
+    tt(blk("TMP", 2), blk("TMP", 2), blk("TMP", 3), AL.add)
+    tt(whole("TRM"), blk("TMP", 2), whole("ONB"), AL.mult)
+    ts(whole("DG"), whole("ML"), lane, AL.is_equal)
+    ts(whole("RS"), whole("ML"), 0.0, AL.not_equal)
+    act(whole("JK"), whole("J"), AF.Identity, 0.0, 1.0 / 256)
+    for par in (0, 1):
+        ts(blk("J4", par), whole("J"), 4.0, AL.mult, 2.0 * par, AL.add)
+    act(whole("J4B"), whole("J4"), AF.Identity)
+    fill(whole("ZB"), 0.0)
+    j0 = R("VC", 0, 8)
+    ts(R("CC", 0, 8), j0, 1.0 + 1.0 / 256, AL.mult, -127.0, AL.add)
+    ts(R("CC", 8, 16), j0, 1.0 / 256, AL.mult, 1.0, AL.add)
+    for t in range(3):
+        fill(R("SN", OK_[t] + 256 + t % 2, OK_[t] + 1024, 2), 0.015625)
+    ts(col("NTH", 0), col("TH", 0), -1.0, AL.mult)
+
+    ts(R("SBB", 0, 64), R("SBI", 0, 64), 2048.0, AL.mult)
+    ts(R("SBB", 64, 128), R("SBI", 64, 128), 2.0, AL.mult)
+
+    def spread(bank, src, dst, i0, i1, eng):
+        mm([(P(bank, 64 * (i - i0), 64 * (i - i0) + 64), blk("BC", i), R("SBB", src, src + 64), True, True) for i in range(i0, i1)])
+        move(eng, R("SN", dst + 64 * i0, dst + 64 * i1), P(bank, 0, 64 * (i1 - i0)))
+
+    def lists(t, c0, c1, bank):
+        n = c1 - c0
+        mm(group([(P(bank, 64, 64 + n), blk("SEL", i), R("SN", OS + 16 * c0 + i, OS + 16 * c1, 16)) for i in range(16)]))
+        mm(group([(P(bank, 0, n), blk("SEL", i), R("SN", ON + 16 * c0 + i, ON + 16 * c1, 16)) for i in range(16)]))
+        a = R("LA", c0, c1)
+        tt(a, P(bank, 0, n), R("RG", c0, c1), AL.add)
+        tt(P(bank, 128, 128 + n), a, P(bank, 64, 64 + n), AL.add)
+        tt(P(bank, 192, 192 + n), a, P(bank, 64, 64 + n), AL.subtract)
+        for z in (0, 1):
+            tt(R("LM", 64 * z + c0, 64 * z + c1), P(bank, 128 + 64 * z, 128 + 64 * z + n), R("VC", 64 + 64 * z + c0, 64 + 64 * z + c1), AL.max)
+        for z in (0, 1):
+            o = 128 * t + 64 * z
+            ts(R("LV", o + c0, o + c1), R("LM", 64 * z + c0, 64 * z + c1), (-1024.0, 1025.0)[z], AL.add)
+
+    def views(t, c0, c1, engs):
+        lo = 256 * (c0 // 16)
+        win = R("UB", lo, 1536) if t == 0 else R("UW", OU + lo, 1664)
+        if engs[0] != engs[1]:
+            views(t, c0, (c0 + c1) // 2, 2 * engs[0])
+            views(t, (c0 + c1) // 2, c1, 2 * engs[1])
+            return
+        for z in (0, 1):
+            o = 128 * t + 64 * z
+            move(engs[z], R("VW%d" % t, 32 * c0 + z, 32 * c1, 2), IND(win, R("LV", o + c0, o + c1)))
+
+    def send_sides(t, bank):
+        mm([(P(bank, 0, 128), whole("SHB"), R("SN", OS + 128, OS + 256), True, True)])
+        move("a", blk("SS", t), P(bank, 0, 128))
+        name, o = ("SN", OG) if t == 0 else ("SG", 256 * (t - 1))
+        return send(2 * t, [R("SN", OS, OS + 128), blk("SS", t)], [R(name, o, o + 128), R(name, o + 128, o + 256)], 5000)
+
+    def send_views(t, bank):
+        vw, sv = "VW%d" % t, "SV%d" % t
+        mm([(P(bank, 0, 256), whole("SHB" if t == 0 else "SHF"), R(vw, 256, 512), True, True)])
+        move("a", whole(sv), P(bank, 0, 256))
+        return send(2 * t + 1, [R(vw, 0, 256), whole(sv)], [R(vw, 2048, 2304), R(vw, 2304, 2560)], 6000 if t == 0 else 8000)
+
+    def node_lists(t, bank):
+        par = t % 2
+        mm(group([(P(bank), whole("IDF"), R("TL2", par, 1024, 2)), (P(bank), whole("IDS"), R("SN", OS + par, OS + 1024, 2))]))
+        cp(R("IX", 512 * t, 512 * t + 512), P(bank))
+
+    def names(t):
+        par = t % 2
+        cp(R("HL", 8 * t, 8 * t + 8), R("HF", par, 16, 2))
+        move("a", blk("NM2", t), IND(whole("TL2"), R("HL", 8 * t, 8 * t + 8)))
+        ts(blk("NMU", t), blk("NM2", t), 0.5, AL.mult)
+        ts(blk("OWN", t), blk("NM2", t), 2048.0, AL.is_lt)
+
+    spread(1, 0, OS, 0, 4, "a")
+    spread(2, 64, ON, 0, 4, "v")
+    send_sides(0, 7)
+    lists(0, 0, 16, 6)
+    views(0, 0, 16, "av")
+    last = send_views(0, 7)
+    spread(3, 0, OS, 4, 12, "a")
+    spread(4, 64, ON, 4, 12, "v")
+    spread(5, 0, OS, 12, 16, "a")
+    spread(0, 64, ON, 12, 16, "a")
+    lists(0, 16, 64, 1)
+    for c in (1, 2, 3):
+        views(0, 16 * c, 16 * c + 16, ("aa", "vv", "av")[c - 1])
+    ts(R("TL2", 0, 1024), whole("TL"), 2.0, AL.mult)
+    cp(whole("HF"), whole("HI"))
+    names(0)
+    node_lists(0, 2)
+    load("g", R("UW", OW, 1664), "w0", 262144, [last])
+    load("g", R("UW", OU, OW), "u0", 524288, [last])
+    names(1)
+
+    rot = {"a": 0, "s": 0, "x": 0, "tb": 0}
+
+    def nxt(k, n):
+        rot[k] += 1
+        return (rot[k] - 1) % n
+
+    def tree_a(D, b, u, long):
+        lo = 128 if long > 0 else 0
+        if long >= 0:
+            mm([(P(b, lo, 512), whole("IDF"), R(D, 512 * u + lo, 512 * u + 512), u == 0, False)])
+        elif u == 2:
+            tt(P(b), P(b), R(D, 1024, 1536), AL.add)
+
+    def tree(D, b, dst, keep, long, scale_on="v"):
+        o = 384 * nxt("tb", 3)
+        idf = whole("IDF")
+        lo = 128 if long > 0 else 0
+        hi = 512 if long == 2 else 256
+        if long >= 0:
+            mm([(P(b, lo, hi), idf, R(D, 1536 + lo, 1536 + hi), False, True)])
+        else:
+            tt(P(b, 0, 256), P(b, 0, 256), R(D, 1536, 1792), AL.add)
+        if long == 2:
+            move("a", R("TB", o, o + 256), P(b, 256, 512))
+        else:
+            tt(R("TB", o, o + 256), P(b, 256, 512), R(D, 1792, 2048), AL.add)
+        tt(R("TB", o + 256, o + 384), P(b, 128, 256), R("TB", o + 128, o + 256), AL.add)
+        if long > 0:
+            mm(group([(P(b, 0, 128), idf, x) for x in (blk(D, 0), blk(D, 8), blk(D, 12), R("TB", o, o + 128), R("TB", o + 256, o + 384))]))
+        else:
+            tt(P(b, 0, 128), P(b, 0, 128), R("TB", o, o + 128), AL.add)
+            tt(P(b, 0, 128), P(b, 0, 128), R("TB", o + 256, o + 384), AL.add)
+        if keep is None:
+            move(scale_on, P(b, 128, 256), P(b, 0, 128), 0.015625)
+        else:
+            tt(P(b, 128, 256), P(b, 0, 128), keep, AL.mult)
+        tt(dst, P(b, 128, 256), dst, AL.add)
+
+    def abank(t):
+        return (1, 2, 3, 0)[nxt("a", 4)] if t == 0 else 1 + nxt("a", 3)
+
+    def nodes(t, c):
+        par = t % 2
+        x = nxt("x", 3)
+        X = ("XH%d" % x) if t == 0 else ("XA", "XB", "XC")[x]
+        D = ("DA", "DB", "DC")[x]
+        for h in (0, 1):
+            o = 512 * t + 128 * c + 64 * h
+            move(CFG[t]["x"][2 * c + h], R(X, 1024 * h, 1024 * h + 1024), IND(whole("VW%d" % t), R("IX", o, o + 64)))
+        long = CFG[t]["long"][c]
+        sb = CFG[t]["sb"][c]
+        for u in (0, 2, 1, 3):
+            stay = u == 1 or (u == 0 and long < 0)
+            b = sb if (u == 0 and long < 0) else abank(t)
+            du = R(D, 512 * u, 512 * u + 512)
+            if u in CFG[t]["pe"][c]:
+                un = R("UB", 256 * c, 256 * c + 256, 2) if t == 0 else R("UW", OU + 256 * c + par, OU + 256 * c + 256, 2)
+                items = []
+                for kk in range(4):
+                    o = P(b, 128 * kk, 128 * kk + 128)
+                    items += group([(o, whole("IDB" if t == 0 else "IDF"), R(X, 4 * u + kk, 2048, 16)), (o, whole("NIDB" if t == 0 else "NIDF"), un)])
+                    if t > 0 or kk == 3:
+                        mm(items)
+                        items = []
+                act(du, P(b), AF.Abs)
+            else:
+                for k in range(4 * u, 4 * u + 4):
+                    tt(blk(D, k), R(X, k, 2048, 16), P(0, 128 * c, 128 * c + 128), AL.subtract)
+                act(P(b), du, AF.Abs)
+            tt(P(b) if stay else du, P(b), du, AL.mult)
+            if u == 1:
+                b1 = b
+            elif u == 3:
+                tt(du, P(b1), du, AL.add)
+            else:
+                tree_a(D, sb, u, long)
+        return D, sb
+
+    def nodes_end(t, c, D):
+        par = t % 2
+        tree(D[0], D[1], R("UW", OU + 256 * c + par, OU + 256 * c + 256, 2),
+             R("SN", OK_[t] + 256 * c + par, OK_[t] + 256 * c + 256, 2) if c else None, CFG[t]["long"][c], CFG[t]["m"][1])
+
+    def shock_front(t):
+        par = t % 2
+        if t > 0:
+            move("a", R("SN", OG, OG + 256), R("SG", 256 * (t - 1), 256 * t))
+        for h in (0, 1):
+            o = 128 * t + 64 * h
+            move(CFG[t]["e"][h], R("E", 1024 * h, 1024 * h + 1024), IND(R("SN", OS, OS + 1280), R("NMU", o, o + 64)), 1.0 / 2048)
+        e = P(6, 0, 128)
+        mm(group([(e, blk("SEL", k), R("E", k, 2048, 16)) for k in range(16)]))
+        tt(blk("XF", 1), e, blk("J4", par), AL.add)
+        tt(blk("XF", 0), e, blk("NM2", t), AL.add)
+        cp(blk("XU", 1), blk("XF", 1))
+        cp(blk("XU", 0), blk("XF", 0))
+        tt(blk("FIT", 0), blk("OWN", t), e, AL.mult)
+        tt(blk("FIT", 1), blk("OWN", t), e, AL.is_gt)
+        mm(group([(P(7, 0, 256), whole("TRM"), whole("FIT")), (P(7, 0, 128), whole("IDF"), blk("NM2", t)), (P(7, 128, 256), whole("IDF"), blk("NM2", t))]))
+        act(whole("FF"), P(7, 0, 256), AF.Relu, col("NTH", 1), 0.5)
+        mm(group([(P(7, 256, 512), whole("ONF"), whole("FF")), (P(7, 256, 384), whole("IDF"), whole("JK")), (P(7, 384, 512), whole("IDF"), whole("JK"))]))
+        move("a", whole("CL"), P(7, 256, 512))
+
+    def shock_main(t):
+        par = t % 2
+        cf = CFG[t]
+        xs, us = ("XSB", "USB") if t == 0 else ("XS", "US")
+        for h in (0, 1):
+            lx, lu, part = R("XU", 64 * h, 64 * h + 64), R("XU", 128 + 64 * h, 192 + 64 * h), (1024 * h, 1024 * h + 1024)
+            up[0] = BOOST
+            move(cf["us"][h], R(us, *part), IND(R("UB", 1024, 1536) if t == 0 else R("UW", OW, 1664), lu))
+            up[0] = 0.0
+            if cf["xs"]:
+                move(cf["xs"][h], R(xs, *part), IND(whole("VW%d" % t), lx))
+            else:
+                tt(R("XS", *part), IND(whole("VW%d" % t), lx), R("US", *part), AL.subtract)
+        sb = cf["sb"][4:6]
+        long = cf["long"][4]
+        for u in (0, 2, 1, 3):
+            b = abank(t)
+            q0, q1 = R("Q0", 512 * u, 512 * u + 512), R("Q1", 512 * u, 512 * u + 512)
+            if cf["xs"]:
+                items = []
+                for kk in range(4):
+                    o = P(b, 128 * kk, 128 * kk + 128)
+                    items += group([(o, whole("IDB" if t == 0 else "IDF"), R(xs, 4 * u + kk, 2048, 16)), (o, whole("NIDB" if t == 0 else "NIDF"), R(us, 4 * u + kk, 2048, 16))])
+                mm(items)
+                act(q0, P(b), AF.Abs)
+                tt(P(b), P(b), q0, AL.mult)
+            else:
+                for kk in range(4):
+                    act(P(b, 128 * kk, 128 * kk + 128), R("XS", 4 * u + kk, 2048, 16), AF.Abs)
+                for kk in range(4):
+                    o = P(b, 128 * kk, 128 * kk + 128)
+                    tt(o, o, R("XS", 4 * u + kk, 2048, 16), AL.mult)
+            for kk in range(4):
+                tt(blk("Q1", 4 * u + kk), P(b, 128 * kk, 128 * kk + 128), R("E", 4 * u + kk, 2048, 16), AL.mult)
+            tt(P(b) if u == 1 else q0, P(b), q1, AL.subtract)
+            if u == 1:
+                b1 = b
+            elif u == 3:
+                tt(q1, R("Q1", 512, 1024), q1, AL.add)
+                tt(q0, P(b1), q0, AL.add)
+            else:
+                tree_a("Q1", sb[1], u, long)
+                tree_a("Q0", sb[0], u, long)
+        for z in (1, 0):
+            tree("Q%d" % z, sb[z], R("UW", OW + 2 * par + z, 1664, 4), None, long, cf["m"][0])
+
+    def claims(t):
+        par = t % 2
+        w = [R("UW", OW + 2 * par + z, 1664, 4) for z in (0, 1)]
+        tt(whole("DD"), w[0], w[1], AL.subtract)
+        ts(blk("VB", 0), whole("DD"), col("TH", 0), AL.is_gt)
+        ts(blk("VB", 1), whole("DD"), col("NTH", 0), AL.is_lt)
+        mm([(P(6, 0, 256), whole("ONB"), whole("VB"), True, True)])
+        ts(P(6, 0, 256), P(6, 0, 256), 9.0, AL.is_ge)
+        tt(P(6, 256, 384), P(6, 0, 128), blk("CL", 0), AL.mult)
+        tt(whole("MM"), P(6, 128, 256), blk("CL", 1), AL.mult)
+        tt(whole("KEY"), P(6, 256, 384), whole("MM"), AL.add)
+        tt(whole("KD"), whole("KEY"), whole("DG"), AL.mult)
+        add("v", lambda q, A: q.tensor_tensor_scan(A(whole("KS")), A(whole("RS")), A(whole("KD")), 0.0, AL.mult, AL.add),
+            [whole("KS")], [whole("RS"), whole("KD")], 128 * CY)
+        kw = R("KS", 15, 128, 16)
+        sm = lambda i: R("SM", 8 * i, 8 * i + 8)
+        ts(sm(0), kw, -1.0, AL.mult, 0.25, AL.add)
+        for c in range(7, -1, -1):
+            a = R("AB", 128 * c, 128 * c + 16 * c + 16)
+            act(a, R("KEY", 0, 16 * c + 16), AF.Abs, col("SM", c))
+            if CFG[t]["m"][4] == "a":
+                add("a", lambda q, A, a=a, c=c: q.activation(A(a), A(a), AF.Relu, bias=A(col("NTH", 2)), scale=-1.0, accum_out=A(col("SM", 8 + c))),
+                    [a, col("SM", 8 + c)], [a, col("NTH", 2)], 20 + CY * max(64, 16 * c + 16))
+            else:
+                add("v", lambda q, A, a=a, c=c: q.tensor_reduce(A(col("SM", 8 + c)), A(a), AxisListType.X, AL.min),
+                    [col("SM", 8 + c)], [a], CY * max(64, 16 * c + 16))
+        for z in (0, 1):
+            tt(blk("MV", z), P(6, 128 * z, 128 * z + 128), w[z], AL.mult)
+        move(CFG[t]["m"][2], whole("AS"), P(6, 128, 256), 2048.0)
+        ts(sm(2), kw, 1.0, AL.is_ge)
+        tt(sm(3), kw, R("CC", 0, 8), AL.subtract)
+        tt(sm(4), sm(3), sm(2), AL.mult)
+        if CFG[t]["m"][4] == "a":
+            ts(sm(5), sm(1), 0.001, AL.is_lt)
+        else:
+            ts(sm(5), sm(1), 0.25, AL.is_ge)
+        tt(sm(6), sm(5), sm(4), AL.mult)
+        tt(sm(7), sm(6), j0, AL.add)
+        lu = R("LU", 8 * t, 8 * t + 8)
+        cp(lu, sm(7))
+        cp(IND(R("SN", OS - 128, OS + 1024), lu), whole("AS"))
+        cp(IND(R("SN", ON - 128, ON + 1024), lu), blk("J4B", par))
+        tt(IND(R("UW", 0, OW), lu), blk("MV", 0), blk("MV", 1), AL.add)
+        cp(IND(R("SN", OK_[t] - 128, OK_[t] + 1024), lu), whole("ZB"))
+        h = R("HF", par, 16, 2)
+        tt(sm(8), kw, R("CC", 8, 16), AL.subtract)
+        tt(sm(9), sm(8), h, AL.subtract)
+        tt(sm(10), sm(5), sm(2), AL.mult)
+        tt(sm(11), sm(10), sm(9), AL.mult)
+        tt(h, h, sm(11), AL.add)
+
+    def store(name, src, lo, hi):
+        dma("s", [(lambda A: A(("#hbm", name))[:, lo:hi], lambda A: A(src))], [], [src], 512 * (hi - lo))
+
+    fill(col("NTH", 1), -2047.0)
+    fill(col("NTH", 2), 0.25)
+    for t in range(3):
+        par = t % 2
+        if t > 0:
+            if CFG[t]["m"][3] == "a":
+                move("a", P(0), R("UW", OU + par, OW, 2))
+            else:
+                mm([(P(0), whole("IDF"), R("UW", OU + par, OW, 2), True, True)])
+        up[0] = BOOST
+        shock_front(t)
+        up[0] = 0.0
+        if CFG[t]["first"]:
+            nodes_end(t, 0, nodes(t, 0))
+            shock_main(t)
+        else:
+            shock_main(t)
+            nodes_end(t, 0, nodes(t, 0))
+        D = nodes(t, 3)
+        claims(t)
+        if t < 2:
+            send_sides(t + 1, 7)
+            lists(t + 1, 0, 64, 6)
+            views(t + 1, 0, 16, CFG[t]["gv"])
+            send_views(t + 1, 7)
+            node_lists(t + 1, 6)
+            if t == 0:
+                names(2)
+        else:
+            store("ys", R("UW", OW, 1664), 0, 512)
+            store("yu", R("UW", OU, OU + 256), 0, 256)
+            mm(group([(P(7, 0, 64), blk("SEL", i), R("SN", ON + 64 * i, ON + 64 * i + 64)) for i in range(16)])
+               + group([(P(7, 64, 128), blk("SEL", i), R("SN", OS + 64 * i, OS + 64 * i + 64)) for i in range(16)]))
+            move("a", R("YC", 64, 128), P(7, 64, 128), 1.0 / 2048)
+            tt(R("YC", 0, 64), P(7, 0, 64), R("YC", 64, 128), AL.add)
+            dma("s", [(lambda A: A(("#hbm", "yc"))[:], lambda A: A(R("YC", 0, 64)))], [], [R("YC", 0, 64)], 32768)
+            dma("s", [(lambda A, c=c: A(("#hbm", "yh"))[:, 32 * c:32 * c + 32], lambda A, c=c: A(R("HF", 2 * c, 2 * c + 2))) for c in range(8)],
+                [], [whole("HF")], 8192, rows=1024)
+        for c in (3, 2, 1):
+            if c < 3:
+                D = nodes(t, c)
+            nodes_end(t, c, D)
+            if t < 2:
+                views(t + 1, 16 * c, 16 * c + 16, CFG[t]["rv"][6 - 2 * c:8 - 2 * c])
+            else:
+                store("yu", R("UW", OU + 256 * c, OU + 256 * c + 256), 256 * c, 256 * c + 256)
+    return ops
+
+
+def schedule(ops):
+    n = len(ops)
+    seen = {}
+    for i, o in enumerate(ops):
+        deps = set()
+        for kind in ("r", "w"):
+            for r in o[kind]:
+                ps = _psum(r)
+                for j, k2, lo, hi in seen.get(r[0], ()):
+                    if ps and ops[j]["e"] != o["e"]:
+                        deps.add(j)
+                    elif (kind == "w" or k2 == "w") and lo < r[2] and r[1] < hi:
+                        deps.add(j)
+        for kind in ("r", "w"):
+            for r in o[kind]:
+                seen.setdefault(r[0], []).append((i, kind, r[1], r[2]))
+        o["deps"] = deps
+        o["all"] = deps | set(o["after"])
+    succ = [[] for _ in range(n)]
+    for i, o in enumerate(ops):
+        for j in o["all"]:
+            succ[j].append(i)
+
+    def lat(j, i):
+        if ops[j]["e"] == ops[i]["e"] and ops[j]["sem"] is None:
+            return 0.0 if ops[j]["e"] == "t" else LAT_S
+        return LAT_X
+    prio = [0.0] * n
+    for i in range(n - 1, -1, -1):
+        prio[i] = ops[i]["done"] + max([prio[k] + lat(i, k) for k in succ[i]], default=0.0)
+    left = [len(o["all"]) for o in ops]
+    ready = [0.0] * n
+    cand = {e: [] for e in "vatgsx"}
+    free = {e: 0.0 for e in "vatgsx"}
+    order = {e: [] for e in "vatgsx"}
+    for i in range(n):
+        if left[i] == 0:
+            cand[ops[i]["e"]].append(i)
+    end = [0.0] * n
+    for _ in range(n):
+        best = None
+        for e in "xvatgs":
+            if cand[e]:
+                t0 = max(free[e], min(ready[i] for i in cand[e]))
+                if best is None or t0 < best[0]:
+                    best = (t0, e)
+        t0, e = best
+        key = lambda k: (prio[k] + ops[k]["up"], -k)
+        i = max((k for k in cand[e] if ready[k] <= t0 + LOOK), key=key)
+        if ready[i] > t0 + SLACK:
+            now = [k for k in cand[e] if ready[k] <= t0 + SLACK]
+            short = [k for k in now if ops[k]["c"] <= ready[i] - t0 + TOL]
+            if short:
+                i = max(short, key=key)
+            elif key(i)[0] - key(max(now, key=key))[0] < FAR:
+                i = max(now, key=key)
+        cand[e].remove(i)
+        st = max(free[e], ready[i])
+        free[e] = st + ops[i]["c"]
+        end[i] = st + ops[i]["done"]
+        ops[i]["st"] = st
+        ops[i]["seq"] = _
+        order[e].append(i)
+        for k in succ[i]:
+            ready[k] = max(ready[k], end[i] + lat(i, k))
+            left[k] -= 1
+            if left[k] == 0:
+                cand[ops[k]["e"]].append(k)
+    count = {}
+    for e in "vatg":
+        c = 0
+        for i in order[e]:
+            if ops[i]["sem"] is None:
+                c += 1
+                ops[i]["sig"] = (ESEM[e], c)
+        count[ESEM[e]] = c
+    for o in ops:
+        if o["sem"] is not None:
+            o["sig"] = o["sem"]
+            count[o["sem"][0]] = o["sem"][1]
+    for e in "vatgs":
+        had = {}
+        for i in order[e]:
+            need = {}
+            for j in ops[i]["deps"]:
+                if e == "t" and ops[j]["e"] == "t":
+                    continue
+                s, v = ops[j]["sig"]
+                if isinstance(v, str):
+                    if s not in had:
+                        need[s] = v
+                elif v > had.get(s, 0) and v > need.get(s, 0):
+                    need[s] = v
+            had.update(need)
+            ops[i]["waits"] = sorted(need.items())
+    return order, count, max(end)
+
+
+_PLAN = {}
+
+
+def plan():
+    if not _PLAN:
+        ops = build()
+        order, count, total = schedule(ops)
+        _PLAN.update(ops=ops, order=order, count=count, total=total)
+    return _PLAN
+
+
+def route(T, topo, src, dst):
+    if topo.may_write(src, dst):
+        return [dst, dst]
+    ok = [c for c in topo.cores_of(src) if c != src and T.rank_of(c) is None and topo.may_write(c, dst)]
+    ok.sort(key=lambda c: topo.die(c) != topo.die(src))
+    return ok[:2]
+
+
+def bits(engines):
+    return sum(1 << e for e in engines)
+
+
+def rank_program(g, core, T, topo):
+    pl = plan()
+    ops = pl["ops"]
+    cores = list(T.cores)
+    n = len(cores)
+
+    def A(x):
+        if not isinstance(x, tuple):
+            return x
+        if x[0] == "#ind":
+            return A(x[1]).indirect(A(x[2]))
+        if x[0] == "#sem":
+            return T.sem[x[1]]
+        if x[0] == "#hbm":
+            return T[x[1]]
+        if x[3] == 1:
+            return T[x[0]][:, x[1]:x[2]]
+        return T[x[0]][:, x[1]:x[2]:x[3]]
+
+    rank = T.rank_of(core)
+    if rank is None:
+        for r in range(n):
+            src, dst = cores[r], cores[(r - 1) % n]
+            hops = route(T, topo, src, dst)
+            if core in hops:
+                half = hops.index(core)
+                eng = topo.engines(core, dst)
+                rid, pid = topo.addr(dst, core)
+                sent = 0
+                for i in pl["order"]["g"]:
+                    fn = ops[i]["fn"]
+                    if isinstance(fn, tuple):
+                        m, d = fn[1], fn[3][half]
+                        g.wait_ge(T.sem["rin%d" % m], HOP1)
+                        g.remote_dma(A(d), A(d), T.sem["arr%d" % m], T.sem["rl"], pid, rid, bits(eng))
+                        sent += len(eng)
+                g.wait_ge(T.sem["rl"], sent)
+        return
+
+    dst, src = cores[(rank - 1) % n], cores[(rank + 1) % n]
+    hops = route(T, topo, core, dst)
+    back = route(T, topo, src, core)
+    val = {"#sent": 2 * HOP1, "#arr": sum(HOP1 if h == core else len(topo.engines(h, core)) for h in back)}
+    queue = {"v": g.vector, "a": g.scalar, "t": g.tensor, "g": g, "s": g.sync}
+    for e in "sagtv":
+        q = queue[e]
+        for i in pl["order"][e]:
+            o = ops[i]
+            for s, v in o["waits"]:
+                q.wait_ge(T.sem[s], val.get(v, v))
+            if isinstance(o["fn"], tuple):
+                m, srcs, dsts, s = o["fn"][1:]
+                tr = []
+                for half in (0, 1):
+                    rid, pid = topo.addr(hops[half], core)
+                    eng = topo.engines(core, hops[half])[HOP1 * half:HOP1 * half + HOP1]
+                    tr.append(RemoteDMATransfer(dst_ids=[DstId(rid=rid, pnc=pid)], dma_engine_mask=bits(eng),
+                                                remote_sem=T.sem[("arr%d" if hops[half] == dst else "rin%d") % m], src=A(srcs[half]), dst=A(dsts[half])))
+                g.remote_dma_fused(tr, local_sem=T.sem[s])
+            elif o["sem"] is None:
+                o["fn"](q, A).then_inc(T.sem[o["sig"][0]], 1)
+            else:
+                o["fn"](q, A)
+    for s, v in sorted(pl["count"].items()):
+        g.wait_ge(T.sem[s], val.get(v, v))
+
+
+HOP1 = 4

@@ -5,20 +5,21 @@ AL = AluOpType
 AF = ActivationFunctionType
 F32, BF, I32, U16 = "float32", "bfloat16", "int32", "uint16"
 
-ALL = (0, 1, 2, 3)
 CFG = [
-    {'pe': [ALL, ALL, ALL, ALL], 'x': 'aaaaaaav', 'e': 'av', 'us': 'vv', 'xs': 'aa', 'long': [0, -1, 1, 2, 0], 'first': 0, 'gv': 'vv', 'rv': 'aavvvv', 'm': 'vaaav', 'sb': [5, 5, 4, 4, 4, 5]},
-    {'pe': [(), (), (), ()], 'x': 'aaaaaaaa', 'e': 'aa', 'us': 'aa', 'xs': '', 'long': [2, -1, 2, 2, 0], 'first': 0, 'gv': 'aa', 'rv': 'vaaavv', 'm': 'aavva', 'sb': [4, 4, 5, 4, 4, 6]},
-    {'pe': [(2, 3), (), (), ()], 'x': 'aaaaaaaa', 'e': 'aa', 'us': 'aa', 'xs': '', 'long': [2, 0, 2, 1, 2], 'first': 0, 'gv': 'av', 'rv': 'avavav', 'm': 'aaava', 'sb': [6, 6, 5, 4, 4, 5]},
+    {'tree': [12, 12, -1, 0, 0], 'xs': 1, 'q0': 0, 'early': (0,), 'red': 'a', 'up': [15000, 5000, 1000, 2000, 10000, 40000, 2000], 'sub': ['pppp', 'pppp', 'pppp', 'pppp'], 'rel': 5000, 'one': 2, 'split': 1},
+    {'tree': [11, 1, 12, -1, 0], 'xs': 0, 'q0': 0, 'early': (0,), 'red': 'v', 'up': [0, 5000, 5000, 0, 30000, 10000, 2000], 'sub': ['dddd', 'ffvv', 'ppdd', 'pfpf'], 'rel': 20000, 'one': 0, 'split': 1},
+    {'tree': [11, -1, 2, 12, 2], 'xs': 0, 'q0': 0, 'early': (0, 1), 'red': 'a', 'up': [2000, 2000, 20000, 20000, 40000, 2000, 15000], 'sub': ['ffdd', 'fffv', 'dpdp', 'dddd'], 'rel': 5000, 'one': 0, 'split': 0},
 ]
 
-OU, OW = 128, 1152
+OW, OE, OU, OH = 0, 512, 640, 1664
 OK_ = (128, 1280, 2432)
 ON, OS, OG = 3584, 4736, 5760
 
 SCRATCH = {
     "TL": ("sbuf", [128, 1024], I32), "TL2": ("sbuf", [128, 1024], F32),
-    "UB": ("sbuf", [128, 1536], BF), "UW": ("sbuf", [128, 1664], F32),
+    "UB": ("sbuf", [128, 1920], BF), "UW": ("sbuf", [128, 1920], F32),
+    "U1": ("sbuf", [128, 4, 512], F32), "U2": ("sbuf", [128, 4, 512], F32), "TT": ("sbuf", [128, 1024], F32), "LT": ("sbuf", [128, 896], F32), "SL": ("sbuf", [128, 64], BF),
+    "SO0": ("sbuf", [128, 128], BF), "SO": ("sbuf", [128, 256], F32), "GO": ("sbuf", [128, 256], F32),
     "SN": ("sbuf", [128, 6016], BF),
     "VW0": ("sbuf", [128, 2560], BF), "VW1": ("sbuf", [128, 2560], F32), "VW2": ("sbuf", [128, 2560], F32),
     "SV0": ("sbuf", [128, 256], BF), "SV1": ("sbuf", [128, 256], F32), "SV2": ("sbuf", [128, 256], F32),
@@ -33,32 +34,47 @@ SCRATCH = {
     "ONB": ("sbuf", [128, 128], BF), "ONF": ("sbuf", [128, 128], F32), "TRM": ("sbuf", [128, 128], BF),
     "TMP": ("sbuf", [128, 512], F32), "SC": ("sbuf", [128, 16], F32),
     "SEL": ("sbuf", [128, 2048], BF), "BC": ("sbuf", [128, 2048], BF),
-    "DG": ("sbuf", [128, 128], F32), "RS": ("sbuf", [128, 128], F32), "JK": ("sbuf", [128, 128], F32),
+    "DG": ("sbuf", [128, 128], F32), "RS": ("sbuf", [128, 128], F32), "JK": ("sbuf", [128, 128], BF),
     "J4": ("sbuf", [128, 256], F32), "J4B": ("sbuf", [128, 256], BF), "ZB": ("sbuf", [128, 128], BF),
-    "RG": ("sbuf", [128, 128], F32), "VC": ("sbuf", [128, 192], F32), "CC": ("sbuf", [128, 16], F32),
+    "VC": ("sbuf", [128, 192], F32), "CC": ("sbuf", [128, 16], F32),
     "IX": ("sbuf", [128, 1536], U16), "LV": ("sbuf", [128, 384], U16), "LA": ("sbuf", [128, 128], F32), "LM": ("sbuf", [128, 128], F32),
     "NM2": ("sbuf", [128, 384], F32), "NMU": ("sbuf", [128, 384], U16), "OWN": ("sbuf", [128, 384], F32),
     "E": ("sbuf", [128, 2048], BF), "XF": ("sbuf", [128, 256], F32), "XU": ("sbuf", [128, 256], U16),
     "FIT": ("sbuf", [128, 256], BF), "FF": ("sbuf", [128, 256], F32), "CL": ("sbuf", [128, 256], F32),
-    "XS": ("sbuf", [128, 2048], F32), "US": ("sbuf", [128, 2048], F32), "XSB": ("sbuf", [128, 2048], BF), "USB": ("sbuf", [128, 2048], BF),
-    "Q0": ("sbuf", [128, 2048], F32), "Q1": ("sbuf", [128, 2048], F32),
-    "XA": ("sbuf", [128, 2048], F32), "XB": ("sbuf", [128, 2048], F32), "XC": ("sbuf", [128, 2048], F32),
-    "XH0": ("sbuf", [128, 2048], BF), "XH1": ("sbuf", [128, 2048], BF), "XH2": ("sbuf", [128, 2048], BF),
-    "DA": ("sbuf", [128, 2048], F32), "DB": ("sbuf", [128, 2048], F32), "DC": ("sbuf", [128, 2048], F32),
-    "TB": ("sbuf", [128, 1152], F32),
-    "DD": ("sbuf", [128, 128], F32), "VB": ("sbuf", [128, 256], BF), "MM": ("sbuf", [128, 128], F32), "MV": ("sbuf", [128, 256], F32),
-    "AS": ("sbuf", [128, 128], BF), "KEY": ("sbuf", [128, 128], F32), "KD": ("sbuf", [128, 128], F32), "KS": ("sbuf", [128, 128], F32),
-    "AB": ("sbuf", [128, 1024], F32), "SM": ("sbuf", [128, 96], F32), "LU": ("sbuf", [128, 24], U16), "YC": ("sbuf", [128, 128], F32),
+    "VB": ("sbuf", [128, 256], BF), "MM": ("sbuf", [128, 128], F32), "MV": ("sbuf", [128, 256], F32),
+    "AS": ("sbuf", [128, 128], BF), "KEY": ("sbuf", [128, 136], F32), "KD": ("sbuf", [128, 128], F32), "KS": ("sbuf", [128, 128], F32),
+    "AB": ("sbuf", [128, 1088], F32), "SM": ("sbuf", [128, 96], F32), "LU": ("sbuf", [128, 24], U16), "YC": ("sbuf", [128, 128], F32),
 }
-for _b in range(8):
-    SCRATCH["P%d" % _b] = ("psum", [128, 512], F32)
+POOLS = {"P": (8, "psum", 512, F32), "X": (4, "sbuf", 1024, F32), "Y": (2, "sbuf", 2048, F32), "H": (4, "sbuf", 2048, BF),
+         "D": (4, "sbuf", 2048, F32), "B": (4, "sbuf", 384, F32)}
+SCRATCH["Q"] = ("sbuf", [128, 2, 2048], F32)
+for _p, (_k, _w, _c, _d) in POOLS.items():
+    for _b in range(_k):
+        SCRATCH["%s%d" % (_p, _b)] = (_w, [128, 4, 16, 8] if _p == "P" else [128, _c], _d)
+PRE, POST = (0.015625, 0.015625, 1.0), (1.0, 1.0, 0.015625)
 
-SEMAPHORES = (["ev", "ea", "et", "eg", "rl"] + ["d%d" % i for i in range(24)] + ["arr%d" % i for i in range(6)] + ["rin%d" % i for i in range(6)])
+SEMAPHORES = (["ev", "ea", "et", "eg", "rl"] + ["d%d" % i for i in range(110)] + ["arr%d" % i for i in range(9)] + ["rin%d" % i for i in range(9)])
 ESEM = {"v": "ev", "a": "ea", "t": "et", "g": "eg"}
+HOP1 = 4
 
-CY, PECY, GA, SCAT, LAT_X, LAT_S, SLACK = 1.0, 0.5, 1.55, 3.8, 150.0, 90.0, 30.0
-COMM = 1.2
-BOOST, LOOK, TOL, FAR = 10000.0, 200.0, 50.0, 3000.0
+M = {"cy": 0.83 * 1.1, "fv": 30, "fa": 30, "pe": 0.45 * 1.1, "ga": 1.56, "sc": 3.8, "lx": 150.0, "ls": 90.0, "comm": 1.2,
+     "gi": 1000, "dl": 2000, "dr": 150.0, "ar": 200}
+S = {'slack': 30.0, 'boost': 10000, 'look': 200, 'tol': 300, 'far': 8000, 'th': 600, 'res': 0, 'far2': 1000000000.0, 'frac': 1.1, 'tn': -30000, 'uo': 300, 'so': 600, 'cn': 4, 'cs': 4, 'tn2': 30000, 'pass': 1, 'mix': 0.5, 'q': 1.0}
+
+
+def price(k, m):
+    cy = m["cy"]
+    if k[0] == "ns":
+        return k[1], k[2], 0.0
+    if k[0] == "comm":
+        return 0.0, k[1] * m["comm"] - 2500, 0.0
+    if k[0] == "dma":
+        return (m["gi"] if k[1] == "g" else 70) * k[2], m["dl"] + k[3] / m["dr"] + k[4] * 3, (k[3] / m["ar"] if k[4] == 512 else 0.0)
+    if k[0] == "acc":
+        return m["gi"], m["dl"] + k[1] / m["ar"], k[1] / m["ar"]
+    c = {"v": m["fv"] + cy * max(64, k[1]), "a": m["fa"] + cy * max(64, k[1]), "vg": 50 + m["ga"] * cy * k[1], "ag": 65 + m["ga"] * cy * k[1],
+         "vs": 50 + m["sc"] * cy * k[1], "t": m["pe"] * k[1], "g": 130 + 2 * cy * k[1]}[k[0]]
+    return c, c, 0.0
 
 
 def R(name, lo, hi, step=1):
@@ -72,15 +88,23 @@ def IND(win, off):
 def _n(r):
     if r[0] == "#ind":
         return 16 * _n(r[2])
+    if len(r) > 4:
+        return 32
     return (r[2] - r[1] + r[3] - 1) // r[3]
 
 
+def _kind(name):
+    if name[0] == "Q":
+        return SCRATCH["D0"]
+    return SCRATCH[name.split("#")[0] + "0" if "#" in name else name]
+
+
 def _psum(r):
-    return r[0] != "#ind" and SCRATCH[r[0]][0] == "psum"
+    return r[0] != "#ind" and _kind(r[0])[0] == "psum"
 
 
 def _two(r):
-    return SCRATCH[r[0]][2] in (BF, U16)
+    return _kind(r[0])[2] in (BF, U16)
 
 
 def _flat(rs):
@@ -95,28 +119,34 @@ def build():
     ops = []
     nsem = [0]
     up = [0.0]
+    ntile = [0]
 
-    def add(eng, fn, wr, rd, cost, done=None, sem=None, after=()):
+    def tile(pool, kind=""):
+        ntile[0] += 1
+        return "%s#%d%s" % (pool, ntile[0], kind)
+
+    def add(eng, fn, wr, rd, cost, sem=None, after=(), hold=()):
         w, r = [], _flat(rd)
         for o in wr:
             if o[0] == "#ind":
                 w.append(o[1]); r.append(o[2])
             else:
                 w.append(o)
-        ops.append({"e": eng, "fn": fn, "w": w, "r": r, "c": cost, "done": cost if done is None else done, "sem": sem, "after": list(after), "up": up[0]})
+        tiles = sorted(set([x[0] for x in w + r if "#" in x[0]] + list(hold)))
+        ops.append({"e": eng, "fn": fn, "w": w, "r": r, "k": cost, "sem": sem, "after": list(after), "up": up[0], "tiles": tiles})
         return len(ops) - 1
 
     def vcost(out, a, b=None):
         if out[0] == "#ind":
-            return 50 + SCAT * CY * _n(out)
+            return ("vs", _n(out))
         if a[0] == "#ind":
-            return 50 + GA * CY * _n(a)
+            return ("vg", _n(a))
         n = _n(out)
         if b is not None:
             n = n if (_psum(a) or _psum(b)) else 2 * n
         elif _two(out) and _two(a):
             n = n / 2
-        return CY * max(64, n)
+        return ("v", n)
 
     def tt(out, a, b, op):
         return add("v", lambda q, A: q.tensor_tensor(A(out), A(a), A(b), op), [out], [a, b], vcost(out, a, b))
@@ -132,23 +162,28 @@ def build():
         return add("v", lambda q, A: q.tensor_copy(A(out), A(a)), [out], [a], vcost(out, a))
 
     def fill(out, x):
-        return add("v", lambda q, A: q.memset(A(out), x), [out], [], CY * max(64, _n(out) / (2 if _two(out) else 1)))
+        return add("v", lambda q, A: q.memset(A(out), x), [out], [], ("v", _n(out) / (2 if _two(out) else 1)))
+
+    def acost(a):
+        return ("ag", _n(a)) if a[0] == "#ind" else ("a", _n(a))
 
     def act(out, a, f, bias=0.0, scale=1.0):
-        c = 65 + GA * CY * _n(a) if a[0] == "#ind" else CY * max(64, _n(a))
-        return add("a", lambda q, A: q.activation(A(out), A(a), f, bias=A(bias), scale=A(scale)), [out], [a, bias, scale], c)
+        return add("a", lambda q, A: q.activation(A(out), A(a), f, bias=A(bias), scale=A(scale)), [out], [a, bias, scale], acost(a))
 
-    def move(eng, out, a, scale=None):
-        if eng == "a":
-            return act(out, a, AF.Identity, 0.0, 1.0 if scale is None else scale)
-        return cp(out, a) if scale is None else ts(out, a, scale, AL.mult)
+    def move(out, a, scale=None, hold=()):
+        fa = lambda q, A: q.activation(A(out), A(a), AF.Identity, bias=0.0, scale=A(1.0 if scale is None else scale))
+        if scale is None:
+            fv = lambda q, A: q.tensor_copy(A(out), A(a))
+        else:
+            fv = lambda q, A: q.tensor_scalar(A(out), A(a), A(scale), None, AL.mult)
+        return add("f", {"a": fa, "v": fv}, [out], [a, scale], {"a": acost(a), "v": vcost(out, a)}, hold=hold)
 
     def mm(items):
         def fn(q, A):
             for o, l, r, st, sp in items:
                 ins = q.matmul(A(o), A(l), A(r), st, sp)
             return ins
-        c = sum(PECY * max(64, _n(r)) * (1 if _two(r) else 4) for o, l, r, st, sp in items)
+        c = ("t", sum(max(64, _n(r)) * (1 if _two(r) else 4) for o, l, r, st, sp in items), len(items))
         return add("t", fn, [i[0] for i in items], [i[1] for i in items] + [i[2] for i in items], c)
 
     def group(parts):
@@ -159,34 +194,49 @@ def build():
             fn = lambda q, A: q.iota(A(out), pattern, base, cm)
         else:
             fn = lambda q, A: q.iota(A(out), pattern, base, cm, allow_small_or_imprecise_dtypes=True)
-        return add("g", fn, [out], [], 130 + 2 * CY * _n(out))
+        return add("g", fn, [out], [], ("g", _n(out)))
+
+    def select(out, a, pattern, base, cm):
+        return add("g", lambda q, A: q.affine_select(A(out), A(a), pattern, AL.is_equal, 0.0, base, cm), [out], [a], ("g", _n(out) + 24))
 
     def dma(eng, pairs, wr, rd, nbytes, after=(), rows=128):
         s = "d%d" % nsem[0]; nsem[0] += 1
         def fn(q, A):
             for o, i in pairs:
                 q.dma_start(o(A), i(A)).then_inc(A(("#sem", s)), 16)
-        return add(eng, fn, wr, rd, (1000 if eng == "g" else 70) * len(pairs), 2000 + nbytes / 150 + rows * 3, (s, 16 * len(pairs)), after)
+        return add(eng, fn, wr, rd, ("dma", eng, len(pairs), nbytes, rows), (s, 16 * len(pairs)), after)
+
+    def acc(D, lo, hi, far, other=None):
+        s = "d%d" % nsem[0]; nsem[0] += 1
+        name = D[0] if len(D) == 1 else "QQ"
+        out, a = R(name, lo, hi), R(other or name, lo + far, hi + far)
+        fn = lambda q, A: q.dma_start(A(out), A(a), accum_op=AL.add).then_inc(A(("#sem", s)), 16)
+        w = [R(x, lo, hi) for x in D]
+        return add("g", fn, w, w + [R(other or x, lo + far, hi + far) for x in D], ("acc", 512 * (hi - lo) * len(D), 128 * len(D)), (s, 16))
 
     def load(eng, out, name, nbytes, after=()):
         return dma(eng, [(lambda A: A(out), lambda A: A(("#hbm", name))[:])], [out], [], nbytes, after)
 
     def send(m, srcs, dsts, lat):
         s = "d%d" % nsem[0]; nsem[0] += 1
-        i = add("g", ("send", m, srcs, dsts, s), [], srcs, 700, 2500, (s, "#sent"))
-        add("x", None, dsts, [], 0, lat * COMM - 2500, ("arr%d" % m, "#arr"), [i])
+        i = add("g", ("send", m, srcs, dsts, s), [], srcs, ("ns", 700, 2500), (s, "#sent"))
+        add("x", None, dsts, [], ("comm", lat), ("arr%d" % m, "#arr"), [i])
         return i
 
-    P = lambda b, lo=0, hi=512, st=1: R("P%d" % b, lo, hi, st)
-    whole = lambda n: R(n, 0, SCRATCH[n][1][1])
+    P = lambda b, lo=0, hi=512, st=1: R(b, lo, hi, st)
+    byname = lambda b, k: (b, 0, 512, 1, k)
+    whole = lambda n: R(n, 0, _kind(n)[1][1])
     col = lambda n, j: R(n, j, j + 1)
     blk = lambda n, i: R(n, 128 * i, 128 * i + 128)
+    idf, idb = whole("IDF"), whole("IDB")
+    BOOST = S["boost"]
 
     up[0] = 50000.0
     load("s", R("SBI", 0, 64), "sd", 32768)
     load("s", R("SBI", 64, 128), "nr", 32768)
-    load("a", R("UB", 1024, 1536), "w0", 131072)
-    load("a", R("UB", 0, 1024), "u0", 393216)
+    dma("a", [(lambda A: A(R("UB", OU, OU + 256)), lambda A: A(("#hbm", "u0"))[:, 0:256])], [R("UB", OU, OU + 256)], [], 65536)
+    load("a", R("UB", OW, OE), "w0", 196608)
+    dma("a", [(lambda A: A(R("UB", OU + 256, OH)), lambda A: A(("#hbm", "u0"))[:, 256:1024])], [R("UB", OU + 256, OH)], [], 393216)
     up[0] = 40000.0
     load("s", whole("TL"), "tl", 900000)
     up[0] = 0.0
@@ -198,7 +248,6 @@ def build():
     iota(whole("MH"), [[1, 8], [0, 16]], 0, 0)
     iota(whole("J"), [[1, 128]], 0, 0)
     iota(whole("PM"), [[1, 128]], 0, -1)
-    iota(R("RG", 0, 64), [[-256, 4], [0, 16]], 0, 0)
     iota(whole("ML"), [[0, 8], [1, 16]], 0, 0)
     ts(col("PI", 1), col("PI", 0), 15, AL.bitwise_and)
     ts(col("PI", 2), col("PI", 0), 4, AL.arith_shift_right)
@@ -206,436 +255,649 @@ def build():
     lane, grp = col("PC", 1), col("PC", 2)
     ts(whole("ONB"), whole("MH"), grp, AL.is_equal)
     ts(whole("SC"), R("J", 0, 16), lane, AL.is_equal)
-    ts(whole("IDB"), whole("PM"), 0.0, AL.is_equal)
+    ts(idb, whole("PM"), 0.0, AL.is_equal)
     for i in range(16):
-        act(blk("BC", i), whole("ONB"), AF.Identity, 0.0, col("SC", i))
-        ts(blk("SEL", i), whole("IDB"), col("SC", i), AL.mult)
+        move(blk("BC", i), whole("ONB"), col("SC", i))
+        ts(blk("SEL", i), idb, col("SC", i), AL.mult)
     ts(R("VC", 0, 64), R("J", 0, 64), 16.0, AL.mult, lane, AL.add)
-    tt(R("RG", 64, 128), R("VC", 0, 64), R("RG", 0, 64), AL.add)
-    ts(R("VC", 64, 128), R("RG", 64, 128), 1024.0, AL.add)
-    ts(R("VC", 128, 192), R("RG", 64, 128), -1025.0, AL.add)
+    ts(R("VC", 64, 128), R("VC", 0, 64), float(OU), AL.add)
+    ts(R("VC", 128, 192), R("VC", 0, 64), OU - 2049.0, AL.add)
     ts(blk("TMP", 0), whole("PM"), -16.0, AL.is_equal)
     ts(blk("TMP", 1), whole("PM"), 112.0, AL.is_equal)
     tt(whole("SHB"), blk("TMP", 0), blk("TMP", 1), AL.add)
-    act(whole("SHF"), whole("SHB"), AF.Identity)
-    act(whole("IDF"), whole("IDB"), AF.Identity)
-    act(whole("NIDB"), whole("IDB"), AF.Identity, 0.0, -1.0)
-    if any(CFG[t]["xs"] or any(CFG[t]["pe"]) for t in (1, 2)):
-        act(whole("NIDF"), whole("IDB"), AF.Identity, 0.0, -1.0)
-    act(whole("IDS"), whole("IDB"), AF.Identity, 0.0, 1.0 / 2048)
-    act(whole("ONF"), whole("ONB"), AF.Identity)
+    move(whole("SHF"), whole("SHB"))
+    move(idf, idb)
+    move(whole("NIDB"), idb, -1.0)
+    move(whole("NIDF"), idb, -1.0)
+    move(whole("IDS"), idb, 1.0 / 2048)
+    move(whole("ONF"), whole("ONB"))
     ts(blk("TMP", 2), whole("PM"), 0.0, AL.is_gt, -8192.0, AL.mult)
     ts(blk("TMP", 3), whole("PM"), 0.0, AL.is_ge, 4096.0, AL.mult)
     tt(blk("TMP", 2), blk("TMP", 2), blk("TMP", 3), AL.add)
     tt(whole("TRM"), blk("TMP", 2), whole("ONB"), AL.mult)
     ts(whole("DG"), whole("ML"), lane, AL.is_equal)
     ts(whole("RS"), whole("ML"), 0.0, AL.not_equal)
-    act(whole("JK"), whole("J"), AF.Identity, 0.0, 1.0 / 256)
+    move(whole("JK"), whole("J"), 1.0 / 256)
     for par in (0, 1):
         ts(blk("J4", par), whole("J"), 4.0, AL.mult, 2.0 * par, AL.add)
-    act(whole("J4B"), whole("J4"), AF.Identity)
+    move(whole("J4B"), whole("J4"))
     fill(whole("ZB"), 0.0)
     j0 = R("VC", 0, 8)
     ts(R("CC", 0, 8), j0, 1.0 + 1.0 / 256, AL.mult, -127.0, AL.add)
     ts(R("CC", 8, 16), j0, 1.0 / 256, AL.mult, 1.0, AL.add)
+    late = [[c for c in (1, 2, 3) if c not in CFG[t]["early"]] for t in range(3)]
     for t in range(3):
-        fill(R("SN", OK_[t] + 256 + t % 2, OK_[t] + 1024, 2), 0.015625)
+        if late[t]:
+            fill(R("SN", OK_[t] + 256 * min(late[t]) + t % 2, OK_[t] + 256 * max(late[t]) + 256, 2), POST[t])
     ts(col("NTH", 0), col("TH", 0), -1.0, AL.mult)
+    for name in ("UB", "UW"):
+        fill(R(name, OE, OU), 0.0)
+    fill(col("KEY", 7), -0.002)
+    fill(col("NTH", 1), -2047.0)
+    fill(col("NTH", 2), 0.25)
 
     ts(R("SBB", 0, 64), R("SBI", 0, 64), 2048.0, AL.mult)
     ts(R("SBB", 64, 128), R("SBI", 64, 128), 2.0, AL.mult)
 
-    def spread(bank, src, dst, i0, i1, eng):
-        mm([(P(bank, 64 * (i - i0), 64 * (i - i0) + 64), blk("BC", i), R("SBB", src, src + 64), True, True) for i in range(i0, i1)])
-        move(eng, R("SN", dst + 64 * i0, dst + 64 * i1), P(bank, 0, 64 * (i1 - i0)))
+    def spread(src, dst, i0, i1):
+        b = tile("P")
+        mm([(P(b, 64 * (i - i0), 64 * (i - i0) + 64), blk("BC", i), R("SBB", src, src + 64), True, True) for i in range(i0, i1)])
+        move(R("SN", dst + 64 * i0, dst + 64 * i1), P(b, 0, 64 * (i1 - i0)))
 
-    def lists(t, c0, c1, bank):
+    def lists(t, c0, c1):
         n = c1 - c0
-        mm(group([(P(bank, 64, 64 + n), blk("SEL", i), R("SN", OS + 16 * c0 + i, OS + 16 * c1, 16)) for i in range(16)]))
-        mm(group([(P(bank, 0, n), blk("SEL", i), R("SN", ON + 16 * c0 + i, ON + 16 * c1, 16)) for i in range(16)]))
-        a = R("LA", c0, c1)
-        tt(a, P(bank, 0, n), R("RG", c0, c1), AL.add)
-        tt(P(bank, 128, 128 + n), a, P(bank, 64, 64 + n), AL.add)
-        tt(P(bank, 192, 192 + n), a, P(bank, 64, 64 + n), AL.subtract)
+        b = tile("P")
+        mm(group([(P(b, 64, 64 + n), blk("SEL", i), R("SN", OS + 16 * c0 + i, OS + 16 * c1, 16)) for i in range(16)]))
+        mm(group([(P(b, 0, n), blk("SEL", i), R("SN", ON + 16 * c0 + i, ON + 16 * c1, 16)) for i in range(16)]))
         for z in (0, 1):
-            tt(R("LM", 64 * z + c0, 64 * z + c1), P(bank, 128 + 64 * z, 128 + 64 * z + n), R("VC", 64 + 64 * z + c0, 64 + 64 * z + c1), AL.max)
+            tt(R("LA", 64 * z + c0, 64 * z + c1), R("VC", 64 + 64 * z + c0, 64 + 64 * z + c1), P(b, 64, 64 + n), (AL.subtract, AL.add)[z])
         for z in (0, 1):
-            o = 128 * t + 64 * z
-            ts(R("LV", o + c0, o + c1), R("LM", 64 * z + c0, 64 * z + c1), (-1024.0, 1025.0)[z], AL.add)
-
-    def views(t, c0, c1, engs):
-        lo = 256 * (c0 // 16)
-        win = R("UB", lo, 1536) if t == 0 else R("UW", OU + lo, 1664)
-        if engs[0] != engs[1]:
-            views(t, c0, (c0 + c1) // 2, 2 * engs[0])
-            views(t, (c0 + c1) // 2, c1, 2 * engs[1])
-            return
+            tt(R("LM", 64 * z + c0, 64 * z + c1), P(b, 0, n), R("LA", 64 * z + c0, 64 * z + c1), AL.max)
         for z in (0, 1):
             o = 128 * t + 64 * z
-            move(engs[z], R("VW%d" % t, 32 * c0 + z, 32 * c1, 2), IND(win, R("LV", o + c0, o + c1)))
+            ts(R("LV", o + c0, o + c1), R("LM", 64 * z + c0, 64 * z + c1), float(z), AL.add)
 
-    def send_sides(t, bank):
-        mm([(P(bank, 0, 128), whole("SHB"), R("SN", OS + 128, OS + 256), True, True)])
-        move("a", blk("SS", t), P(bank, 0, 128))
+    def views(t, c):
+        win = R("UB" if t == 0 else "UW", 0, OU + 256 * c + 256)
+        for z in (0, 1):
+            o = 128 * t + 64 * z + 16 * c
+            move(R("VW%d" % t, 512 * c + z, 512 * c + 512, 2), IND(win, R("LV", o, o + 16)))
+
+    def send_sides(t):
+        b = tile("P")
+        mm([(P(b, 0, 128), whole("SHB"), R("SN", OS + 128, OS + 256), True, True)])
+        move(blk("SS", t), P(b, 0, 128))
         name, o = ("SN", OG) if t == 0 else ("SG", 256 * (t - 1))
-        return send(2 * t, [R("SN", OS, OS + 128), blk("SS", t)], [R(name, o, o + 128), R(name, o + 128, o + 256)], 5000)
+        return send(3 * t, [R("SN", OS, OS + 128), blk("SS", t)], [R(name, o, o + 128), R(name, o + 128, o + 256)], 5000)
 
-    def send_views(t, bank):
+    def send_own(t):
+        b = tile("P")
+        u, so, land, o = (("UB", whole("SO0"), "UB", OH), ("UW", blk("SO", 0), "UW", OH), ("UW", blk("SO", 1), "GO", 0))[t]
+        mm([(P(b, 0, 128), whole("SHB" if t == 0 else "SHF"), R(u, OU + 128, OU + 256), True, True)])
+        move(so, P(b, 0, 128))
+        return send(3 * t + 1, [R(u, OU, OU + 128), so], [R(land, o, o + 128), R(land, o + 128, o + 256)], 5000 if t == 0 else 6000)
+
+    def send_views(t):
         vw, sv = "VW%d" % t, "SV%d" % t
-        mm([(P(bank, 0, 256), whole("SHB" if t == 0 else "SHF"), R(vw, 256, 512), True, True)])
-        move("a", whole(sv), P(bank, 0, 256))
-        return send(2 * t + 1, [R(vw, 0, 256), whole(sv)], [R(vw, 2048, 2304), R(vw, 2304, 2560)], 6000 if t == 0 else 8000)
+        b = tile("P")
+        mm([(P(b, 0, 256), whole("SHB" if t == 0 else "SHF"), R(vw, 256, 512), True, True)])
+        move(whole(sv), P(b, 0, 256))
+        return send(3 * t + 2, [R(vw, 0, 256), whole(sv)], [R(vw, 2048, 2304), R(vw, 2304, 2560)], 6000 if t == 0 else 8000)
 
-    def node_lists(t, bank):
+    def node_lists(t):
         par = t % 2
-        mm(group([(P(bank), whole("IDF"), R("TL2", par, 1024, 2)), (P(bank), whole("IDS"), R("SN", OS + par, OS + 1024, 2))]))
-        cp(R("IX", 512 * t, 512 * t + 512), P(bank))
+        b = tile("P")
+        if t == 0:
+            mm(group([(P(b), idf, R("TL2", par, 1024, 2)), (P(b), whole("IDS"), R("SN", OS + par, OS + 1024, 2))]))
+        else:
+            b2, sl = tile("P"), R("SL", 32 * par, 32 * par + 32)
+            mm(group([(P(b2, 0, 32), blk("SEL", i), R("SN", OS + par + 2 * i, OS + 1024, 32)) for i in range(16)]))
+            move(sl, P(b2, 0, 32))
+            mm(group([(P(b), idf, R("TT", 512 * par, 512 * par + 512))] + [(byname(b, k), whole("IDS"), sl) for k in range(16)]))
+        cp(R("IX", 512 * t, 512 * t + 512), P(b))
+
+    def turned_names(par, gate):
+        y = "VW2"
+        if par:
+            add("v", lambda q, A: q.transpose(A(R(y, 0, 1024)), A(whole("TL2"))), [R(y, 0, 1024)], [whole("TL2")], ("v", 1024))
+            ops[iota(blk("LT", 6), [[0, 128]], 1, 0)]["after"].append(last)
+            for p in (1, 0):
+                select(blk("LT", 4 + p), blk("LT", 6), [[-32, 4], [0, 2], [-2, 16]], -p, 1)
+                for a in (0, 1):
+                    select(blk("LT", 2 * p + a), blk("LT", 4 + p), [[0, 4], [1, 2], [0, 16]], -a, 0)
+        b = tile("P")
+        for k0 in range(0, 16, 2):
+            i = mm([x for k in (k0, k0 + 1) for x in group([(byname(b, k), blk("LT", 2 * par + a), R(y, 16 * a + k, 1024, 32)) for a in (0, 1)])])
+            ops[i]["after"] += gate
+        move(R("TT", 512 * par, 512 * par + 512), P(b))
+
+    def copies(t):
+        name, src = "U%d" % t, R("UW", OU + t % 2, OH, 2)
+        part = lambda lo, hi: [R(name, 512 * c + lo, 512 * c + hi) for c in range(4)]
+        add("a", lambda q, A: q.activation(A(("#all", name, 0, 128)), A(src), AF.Identity, bias=0.0, scale=-1.0), part(0, 128), [src], ("a", 512))
+        for w in (128, 256):
+            dma("s", [(lambda A, w=w: A(("#all", name, w, 2 * w)), lambda A, w=w: A(("#all", name, 0, w)))], part(w, 2 * w), part(0, w), 2048 * w, rows=512)
 
     def names(t):
         par = t % 2
         cp(R("HL", 8 * t, 8 * t + 8), R("HF", par, 16, 2))
-        move("a", blk("NM2", t), IND(whole("TL2"), R("HL", 8 * t, 8 * t + 8)))
+        move(blk("NM2", t), IND(whole("TL2"), R("HL", 8 * t, 8 * t + 8)))
         ts(blk("NMU", t), blk("NM2", t), 0.5, AL.mult)
-        ts(blk("OWN", t), blk("NM2", t), 2048.0, AL.is_lt)
+        ts(blk("OWN", t), blk("NM2", t), 2048.0, AL.is_lt, -1.0, AL.mult)
 
-    spread(1, 0, OS, 0, 4, "a")
-    spread(2, 64, ON, 0, 4, "v")
-    send_sides(0, 7)
-    lists(0, 0, 16, 6)
-    views(0, 0, 16, "av")
-    last = send_views(0, 7)
-    spread(3, 0, OS, 4, 12, "a")
-    spread(4, 64, ON, 4, 12, "v")
-    spread(5, 0, OS, 12, 16, "a")
-    spread(0, 64, ON, 12, 16, "a")
-    lists(0, 16, 64, 1)
+    spread(0, OS, 0, 4)
+    spread(64, ON, 0, 4)
+    send_sides(0)
+    send_own(0)
+    lists(0, 0, 16)
+    views(0, 0)
+    last = send_views(0)
+    spread(0, OS, 4, 12)
+    spread(64, ON, 4, 12)
+    spread(0, OS, 12, 16)
+    spread(64, ON, 12, 16)
+    lists(0, 16, 64)
     for c in (1, 2, 3):
-        views(0, 16 * c, 16 * c + 16, ("aa", "vv", "av")[c - 1])
-    ts(R("TL2", 0, 1024), whole("TL"), 2.0, AL.mult)
+        views(0, c)
+    move(R("TL2", 0, 1024), whole("TL"), 2.0) if False else ts(R("TL2", 0, 1024), whole("TL"), 2.0, AL.mult)
     cp(whole("HF"), whole("HI"))
     names(0)
-    node_lists(0, 2)
-    load("g", R("UW", OW, 1664), "w0", 262144, [last])
-    load("g", R("UW", OU, OW), "u0", 524288, [last])
+    node_lists(0)
+    load("g", R("UW", OW, OE), "w0", 262144, [last])
+    load("g", R("UW", OU, OH), "u0", 524288, [last])
     names(1)
-
-    rot = {"a": 0, "s": 0, "x": 0, "tb": 0}
-
-    def nxt(k, n):
-        rot[k] += 1
-        return (rot[k] - 1) % n
+    up[0] = S["tn"]
+    turned_names(1, [])
 
     def tree_a(D, b, u, long):
         lo = 128 if long > 0 else 0
         if long >= 0:
-            mm([(P(b, lo, 512), whole("IDF"), R(D, 512 * u + lo, 512 * u + 512), u == 0, False)])
+            mm([(P(b, lo, 512), idf, R(D, 512 * u + lo, 512 * u + 512), u == 0, False)])
         elif u == 2:
             tt(P(b), P(b), R(D, 1024, 1536), AL.add)
 
-    def tree(D, b, dst, keep, long, scale_on="v"):
-        o = 384 * nxt("tb", 3)
-        idf = whole("IDF")
-        lo = 128 if long > 0 else 0
-        hi = 512 if long == 2 else 256
-        if long >= 0:
-            mm([(P(b, lo, hi), idf, R(D, 1536 + lo, 1536 + hi), False, True)])
+    VA = (-1, 0, 1, 2, 21)
+
+    def levels(D, long, u, split):
+        if u == 2 and (split or long == 21):
+            acc(D, 0, 512, 1024)
+        if u == 3 and long != 21:
+            acc(D, 512, 1024, 1024) if split else acc(D, 0, 1024, 1024)
+            for lv in range(1, long - 10):
+                acc(D, 0, 1024 >> lv, 1024 >> lv)
+
+    def tree(D, b, dst, keep, long, scale, gate=()):
+        B = tile("B")
+        tb = lambda lo, hi: R(B, lo, hi)
+        if long > 10:
+            b = tile("P")
+            if long == 21:
+                mm(group([(P(b, 256, 512), idf, R(D, 256, 512)), (P(b, 256, 512), idf, R(D, 1792, 2048))]))
+                move(tb(0, 256), P(b, 256, 512))
+                mm(group([(P(b, 128, 256), idf, blk(D, 1)), (P(b, 128, 256), idf, blk(D, 13))]))
+                tt(tb(256, 384), P(b, 128, 256), tb(128, 256), AL.add)
+                fin = [blk(D, 0), blk(D, 12), tb(0, 128), tb(256, 384)]
+            elif long == 11:
+                mm(group([(P(b, 256, 512), idf, R(D, 256, 512)), (P(b, 256, 512), idf, R(D, 768, 1024))]))
+                move(tb(0, 256), P(b, 256, 512))
+                mm(group([(P(b, 128, 256), idf, blk(D, 1)), (P(b, 128, 256), idf, blk(D, 5))]))
+                tt(tb(256, 384), P(b, 128, 256), tb(128, 256), AL.add)
+                fin = [blk(D, 0), blk(D, 4), tb(0, 128), tb(256, 384)]
+            elif long == 12:
+                mm(group([(P(b, 128, 256), idf, blk(D, 1)), (P(b, 128, 256), idf, blk(D, 3))]))
+                move(tb(0, 128), P(b, 128, 256))
+                fin = [blk(D, 0), blk(D, 2), tb(0, 128)]
+            else:
+                fin = [blk(D, 0), blk(D, 1)]
+            if gate and long != 13:
+                b = tile("P")
+            i = mm(group([(P(b, 0, 128), idf, x) for x in fin]))
+            ops[i]["after"] += list(gate)
         else:
-            tt(P(b, 0, 256), P(b, 0, 256), R(D, 1536, 1792), AL.add)
-        if long == 2:
-            move("a", R("TB", o, o + 256), P(b, 256, 512))
-        else:
-            tt(R("TB", o, o + 256), P(b, 256, 512), R(D, 1792, 2048), AL.add)
-        tt(R("TB", o + 256, o + 384), P(b, 128, 256), R("TB", o + 128, o + 256), AL.add)
-        if long > 0:
-            mm(group([(P(b, 0, 128), idf, x) for x in (blk(D, 0), blk(D, 8), blk(D, 12), R("TB", o, o + 128), R("TB", o + 256, o + 384))]))
-        else:
-            tt(P(b, 0, 128), P(b, 0, 128), R("TB", o, o + 128), AL.add)
-            tt(P(b, 0, 128), P(b, 0, 128), R("TB", o + 256, o + 384), AL.add)
+            lo = 128 if long > 0 else 0
+            hi = 512 if long == 2 else 256
+            if long >= 0:
+                mm([(P(b, lo, hi), idf, R(D, 1536 + lo, 1536 + hi), False, True)])
+            else:
+                tt(P(b, 0, 256), P(b, 0, 256), R(D, 1536, 1792), AL.add)
+            if long == 2:
+                move(tb(0, 256), P(b, 256, 512))
+            else:
+                tt(tb(0, 256), P(b, 256, 512), R(D, 1792, 2048), AL.add)
+            tt(tb(256, 384), P(b, 128, 256), tb(128, 256), AL.add)
+            if long > 0:
+                if gate:
+                    b = tile("P")
+                i = mm(group([(P(b, 0, 128), idf, x) for x in (blk(D, 0), blk(D, 8), blk(D, 12), tb(0, 128), tb(256, 384))]))
+                ops[i]["after"] += list(gate)
+            else:
+                tt(P(b, 0, 128), P(b, 0, 128), tb(0, 128), AL.add)
+                tt(P(b, 0, 128), P(b, 0, 128), tb(256, 384), AL.add)
+        if keep is None and abs(scale) == 1.0:
+            tt(dst, dst, P(b, 0, 128), AL.add if scale > 0 else AL.subtract)
+            return
         if keep is None:
-            move(scale_on, P(b, 128, 256), P(b, 0, 128), 0.015625)
+            move(P(b, 128, 256), P(b, 0, 128), scale)
         else:
             tt(P(b, 128, 256), P(b, 0, 128), keep, AL.mult)
         tt(dst, P(b, 128, 256), dst, AL.add)
 
-    def abank(t):
-        return (1, 2, 3, 0)[nxt("a", 4)] if t == 0 else 1 + nxt("a", 3)
-
     def nodes(t, c):
         par = t % 2
-        x = nxt("x", 3)
-        X = ("XH%d" % x) if t == 0 else ("XA", "XB", "XC")[x]
-        D = ("DA", "DB", "DC")[x]
-        for h in (0, 1):
-            o = 512 * t + 128 * c + 64 * h
-            move(CFG[t]["x"][2 * c + h], R(X, 1024 * h, 1024 * h + 1024), IND(whole("VW%d" % t), R("IX", o, o + 64)))
-        long = CFG[t]["long"][c]
-        sb = CFG[t]["sb"][c]
+        D = tile("D")
+        vw, o = whole("VW%d" % t), 512 * t + 128 * c
+        mode = CFG[t]["sub"][c]
+        xu = {}
+        if t == 0:
+            X = tile("H")
+            for h in (0, 1):
+                move(R(X, 1024 * h, 1024 * h + 1024), IND(vw, R("IX", o + 64 * h, o + 64 * h + 64)), hold=[D])
+        else:
+            u = 0
+            while u < 4:
+                if mode[u] == "f":
+                    u += 1
+                    continue
+                w = 2 if u < 3 and mode[u + 1] != "f" and (mode[u] == "d") == (mode[u + 1] == "d") and c >= CFG[t]["one"] else 1
+                X, x0 = (D, 512 * u) if mode[u] == "d" else (tile("X"), 0)
+                i = move(R(X, x0, x0 + 512 * w), IND(vw, R("IX", o + 32 * u, o + 32 * (u + w))), hold=[D])
+                for j in range(w):
+                    xu[u + j] = R(X, x0 + 512 * j, x0 + 512 * j + 512)
+                u += w
+        long = CFG[t]["tree"][c]
+        old = R("U%d" % t, 512 * c, 512 * c + 512)
+        if "v" in mode:
+            pu = tile("P")
+            j = mm([(P(pu), idf, old, True, True)])
+            ops[j]["after"].append(i)
+        sb = tile("P") if long < 10 else None
         for u in (0, 2, 1, 3):
-            stay = u == 1 or (u == 0 and long < 0)
-            b = sb if (u == 0 and long < 0) else abank(t)
+            up[0] = CFG[t]["up"][c] + S["uo"] * (3, 1, 2, 0)[u]
+            stay = long in VA and (u == 1 or (u == 0 and long < 0))
+            b = sb if (u == 0 and long < 0) else tile("P", "n")
             du = R(D, 512 * u, 512 * u + 512)
-            if u in CFG[t]["pe"][c]:
-                un = R("UB", 256 * c, 256 * c + 256, 2) if t == 0 else R("UW", OU + 256 * c + par, OU + 256 * c + 256, 2)
-                items = []
-                for kk in range(4):
-                    o = P(b, 128 * kk, 128 * kk + 128)
-                    items += group([(o, whole("IDB" if t == 0 else "IDF"), R(X, 4 * u + kk, 2048, 16)), (o, whole("NIDB" if t == 0 else "NIDF"), un)])
-                    if t > 0 or kk == 3:
-                        mm(items)
-                        items = []
-                act(du, P(b), AF.Abs)
+            if t == 0:
+                un = R("UB", OU + 256 * c, OU + 256 * c + 256, 2)
+                mm([x for kk in range(4) for x in group([(P(b, 128 * kk, 128 * kk + 128), idb, R(X, 4 * u + kk, 2048, 16)),
+                                                         (P(b, 128 * kk, 128 * kk + 128), whole("NIDB"), un)])])
+            elif mode[u] == "p":
+                for x in range(0, 512, 128):
+                    mm(group([(P(b, x, x + 128), idf, R(xu[u][0], xu[u][1] + x, xu[u][1] + x + 128)),
+                              (P(b, x, x + 128), idf, R(old[0], old[1], old[1] + 128))]))
+            elif mode[u] == "v":
+                tt(du, xu[u], P(pu), AL.add)
+            elif mode[u] == "d":
+                acc([D], 512 * u, 512 * u + 512, 512 * (c - u), old[0])
             else:
-                for k in range(4 * u, 4 * u + 4):
-                    tt(blk(D, k), R(X, k, 2048, 16), P(0, 128 * c, 128 * c + 128), AL.subtract)
-                act(P(b), du, AF.Abs)
+                tt(du, IND(vw, R("IX", o + 32 * u, o + 32 * u + 32)), old, AL.add)
+            if mode[u] == "p":
+                up[0] += CFG[t]["rel"]
+                act(du, P(b), AF.Abs, 0.0, PRE[t])
+            else:
+                act(P(b), du, AF.Abs, 0.0, PRE[t])
             tt(P(b) if stay else du, P(b), du, AL.mult)
+            up[0] = CFG[t]["up"][c]
+            if long > 10:
+                levels([D], long, u, CFG[t]["split"])
+            if long not in VA:
+                continue
             if u == 1:
                 b1 = b
             elif u == 3:
                 tt(du, P(b1), du, AL.add)
-            else:
+            elif long < 10:
                 tree_a(D, sb, u, long)
         return D, sb
 
-    def nodes_end(t, c, D):
+    def nodes_end(t, c, D, gate):
         par = t % 2
-        tree(D[0], D[1], R("UW", OU + 256 * c + par, OU + 256 * c + 256, 2),
-             R("SN", OK_[t] + 256 * c + par, OK_[t] + 256 * c + 256, 2) if c else None, CFG[t]["long"][c], CFG[t]["m"][1])
+        keep = R("SN", OK_[t] + 256 * c + par, OK_[t] + 256 * c + 256, 2) if c in late[t] else None
+        tree(D[0], D[1], R("UW", OU + 256 * c + par, OU + 256 * c + 256, 2), keep, CFG[t]["tree"][c], POST[t], gate)
 
     def shock_front(t):
         par = t % 2
         if t > 0:
-            move("a", R("SN", OG, OG + 256), R("SG", 256 * (t - 1), 256 * t))
+            move(R("SN", OG, OG + 256), R("SG", 256 * (t - 1), 256 * t))
         for h in (0, 1):
             o = 128 * t + 64 * h
-            move(CFG[t]["e"][h], R("E", 1024 * h, 1024 * h + 1024), IND(R("SN", OS, OS + 1280), R("NMU", o, o + 64)), 1.0 / 2048)
-        e = P(6, 0, 128)
+            move(R("E", 1024 * h, 1024 * h + 1024), IND(R("SN", OS, OS + 1280), R("NMU", o, o + 64)), -1.0 / 2048)
+        e = P(tile("P"), 0, 128)
         mm(group([(e, blk("SEL", k), R("E", k, 2048, 16)) for k in range(16)]))
-        tt(blk("XF", 1), e, blk("J4", par), AL.add)
-        tt(blk("XF", 0), e, blk("NM2", t), AL.add)
+        tt(blk("XF", 1), blk("J4", par), e, AL.subtract)
         cp(blk("XU", 1), blk("XF", 1))
-        cp(blk("XU", 0), blk("XF", 0))
         tt(blk("FIT", 0), blk("OWN", t), e, AL.mult)
-        tt(blk("FIT", 1), blk("OWN", t), e, AL.is_gt)
-        mm(group([(P(7, 0, 256), whole("TRM"), whole("FIT")), (P(7, 0, 128), whole("IDF"), blk("NM2", t)), (P(7, 128, 256), whole("IDF"), blk("NM2", t))]))
-        act(whole("FF"), P(7, 0, 256), AF.Relu, col("NTH", 1), 0.5)
-        mm(group([(P(7, 256, 512), whole("ONF"), whole("FF")), (P(7, 256, 384), whole("IDF"), whole("JK")), (P(7, 384, 512), whole("IDF"), whole("JK"))]))
-        move("a", whole("CL"), P(7, 256, 512))
+        tt(blk("FIT", 1), blk("OWN", t), e, AL.is_lt)
+        up[0] = CFG[t]["up"][5]
+        b = tile("P")
+        mm(group([(P(b, 0, 256), whole("TRM"), whole("FIT")), (P(b, 0, 128), idf, blk("NM2", t)), (P(b, 128, 256), idf, blk("NM2", t))]))
+        act(whole("FF"), P(b, 0, 256), AF.Relu, col("NTH", 1), 0.5)
+        mm(group([(P(b, 256, 512), whole("ONF"), whole("FF")), (P(b, 256, 384), idb, whole("JK")), (P(b, 384, 512), idb, whole("JK"))]))
+        move(whole("CL"), P(b, 256, 512))
 
     def shock_main(t):
         par = t % 2
         cf = CFG[t]
-        xs, us = ("XSB", "USB") if t == 0 else ("XS", "US")
+        pool = "H" if t == 0 and cf["xs"] else "Y"
+        xs, us, Q = tile(pool), tile(pool), ["Q0", "Q1"]
+        u_ = "UB" if t == 0 else "UW"
+        up[0] = cf["up"][4]
+        if t == 2:
+            move(R("UW", OH, OH + 256), whole("GO"))
         for h in (0, 1):
-            lx, lu, part = R("XU", 64 * h, 64 * h + 64), R("XU", 128 + 64 * h, 192 + 64 * h), (1024 * h, 1024 * h + 1024)
-            up[0] = BOOST
-            move(cf["us"][h], R(us, *part), IND(R("UB", 1024, 1536) if t == 0 else R("UW", OW, 1664), lu))
-            up[0] = 0.0
+            o = 128 * t + 64 * h
+            move(R(us, 1024 * h, 1024 * h + 1024), IND(R(u_, OU, OH + 256), R("NMU", o, o + 64)), hold=[xs])
+        for h in (0, 1):
+            lu, part = R("XU", 128 + 64 * h, 192 + 64 * h), (1024 * h, 1024 * h + 1024)
             if cf["xs"]:
-                move(cf["xs"][h], R(xs, *part), IND(whole("VW%d" % t), lx))
+                move(R(xs, *part), IND(R(u_, OW, OE), lu))
             else:
-                tt(R("XS", *part), IND(whole("VW%d" % t), lx), R("US", *part), AL.subtract)
-        sb = cf["sb"][4:6]
-        long = cf["long"][4]
+                tt(R(xs, *part), IND(R(u_, OW, OE), lu), R(us, *part), AL.subtract)
+        long = cf["tree"][4]
+        sb = [tile("P"), tile("P")] if long < 10 else [None, None]
+        pos, neg = ("IDB", "NIDB") if t == 0 else ("IDF", "NIDF")
         for u in (0, 2, 1, 3):
-            b = abank(t)
-            q0, q1 = R("Q0", 512 * u, 512 * u + 512), R("Q1", 512 * u, 512 * u + 512)
+            up[0] = cf["up"][4] + S["so"] * (3, 1, 2, 0)[u]
+            b = tile("P", "s")
+            q0, q1 = R(Q[0], 512 * u, 512 * u + 512), R(Q[1], 512 * u, 512 * u + 512)
             if cf["xs"]:
                 items = []
                 for kk in range(4):
                     o = P(b, 128 * kk, 128 * kk + 128)
-                    items += group([(o, whole("IDB" if t == 0 else "IDF"), R(xs, 4 * u + kk, 2048, 16)), (o, whole("NIDB" if t == 0 else "NIDF"), R(us, 4 * u + kk, 2048, 16))])
+                    items += group([(o, whole(pos), R(xs, 4 * u + kk, 2048, 16)), (o, whole(neg), R(us, 4 * u + kk, 2048, 16))])
                 mm(items)
-                act(q0, P(b), AF.Abs)
-                tt(P(b), P(b), q0, AL.mult)
+                act(q0, P(b), AF.Abs, 0.0, PRE[t])
+                tt(q0 if cf["q0"] else P(b), P(b), q0, AL.mult)
             else:
                 for kk in range(4):
-                    act(P(b, 128 * kk, 128 * kk + 128), R("XS", 4 * u + kk, 2048, 16), AF.Abs)
+                    act(P(b, 128 * kk, 128 * kk + 128), R(xs, 4 * u + kk, 2048, 16), AF.Abs, 0.0, PRE[t])
                 for kk in range(4):
                     o = P(b, 128 * kk, 128 * kk + 128)
-                    tt(o, o, R("XS", 4 * u + kk, 2048, 16), AL.mult)
+                    tt(blk(Q[0], 4 * u + kk) if cf["q0"] else o, o, R(xs, 4 * u + kk, 2048, 16), AL.mult)
+            if cf["q0"]:
+                b = tile("P")
+                mm([(P(b, 128 * kk, 128 * kk + 128), idb, R("E", 4 * u + kk, 2048, 16), True, True) for kk in range(4)])
+                tt(q1, P(b), q0, AL.mult)
+                if u == 3:
+                    acc([Q[0]], 0, 2048, 0, Q[1])
+                    levels(Q, long, u, False)
+                continue
             for kk in range(4):
-                tt(blk("Q1", 4 * u + kk), P(b, 128 * kk, 128 * kk + 128), R("E", 4 * u + kk, 2048, 16), AL.mult)
-            tt(P(b) if u == 1 else q0, P(b), q1, AL.subtract)
+                tt(blk(Q[1], 4 * u + kk), P(b, 128 * kk, 128 * kk + 128), R("E", 4 * u + kk, 2048, 16), AL.mult)
+            tt(P(b) if (u == 1 and long in VA) else q0, P(b), q1, AL.add)
+            if long > 10:
+                levels(Q, long, u, cf["split"])
+            if long not in VA:
+                continue
             if u == 1:
                 b1 = b
             elif u == 3:
-                tt(q1, R("Q1", 512, 1024), q1, AL.add)
+                tt(q1, R(Q[1], 512, 1024), q1, AL.add)
                 tt(q0, P(b1), q0, AL.add)
-            else:
-                tree_a("Q1", sb[1], u, long)
-                tree_a("Q0", sb[0], u, long)
+            elif long < 10:
+                tree_a(Q[1], sb[1], u, long)
+                tree_a(Q[0], sb[0], u, long)
         for z in (1, 0):
-            tree("Q%d" % z, sb[z], R("UW", OW + 2 * par + z, 1664, 4), None, long, cf["m"][0])
+            tree(Q[z], sb[z], R("UW", OW + 2 * par + z, OE, 4), None, long, (-POST[t], POST[t])[z])
+        up[0] = 0.0
 
     def claims(t):
         par = t % 2
-        w = [R("UW", OW + 2 * par + z, 1664, 4) for z in (0, 1)]
-        tt(whole("DD"), w[0], w[1], AL.subtract)
-        ts(blk("VB", 0), whole("DD"), col("TH", 0), AL.is_gt)
-        ts(blk("VB", 1), whole("DD"), col("NTH", 0), AL.is_lt)
-        mm([(P(6, 0, 256), whole("ONB"), whole("VB"), True, True)])
-        ts(P(6, 0, 256), P(6, 0, 256), 9.0, AL.is_ge)
-        tt(P(6, 256, 384), P(6, 0, 128), blk("CL", 0), AL.mult)
-        tt(whole("MM"), P(6, 128, 256), blk("CL", 1), AL.mult)
-        tt(whole("KEY"), P(6, 256, 384), whole("MM"), AL.add)
-        tt(whole("KD"), whole("KEY"), whole("DG"), AL.mult)
+        w = [R("UW", OW + 2 * par + z, OE, 4) for z in (0, 1)]
+        b = tile("P")
+        mm(group([(P(b, 0, 128), idf, w[0]), (P(b, 0, 128), whole("NIDF"), w[1])]))
+        ts(blk("VB", 0), P(b, 0, 128), col("TH", 0), AL.is_gt)
+        ts(blk("VB", 1), P(b, 0, 128), col("NTH", 0), AL.is_lt)
+        mm([(P(b, 0, 256), whole("ONB"), whole("VB"), True, True)])
+        ts(P(b, 0, 256), P(b, 0, 256), 9.0, AL.is_ge)
+        tt(P(b, 256, 384), P(b, 0, 128), blk("CL", 0), AL.mult)
+        tt(whole("MM"), P(b, 128, 256), blk("CL", 1), AL.mult)
+        tt(R("KEY", 8, 136), P(b, 256, 384), whole("MM"), AL.add)
+        tt(whole("KD"), R("KEY", 8, 136), whole("DG"), AL.mult)
         add("v", lambda q, A: q.tensor_tensor_scan(A(whole("KS")), A(whole("RS")), A(whole("KD")), 0.0, AL.mult, AL.add),
-            [whole("KS")], [whole("RS"), whole("KD")], 128 * CY)
+            [whole("KS")], [whole("RS"), whole("KD")], ("v", 128))
         kw = R("KS", 15, 128, 16)
         sm = lambda i: R("SM", 8 * i, 8 * i + 8)
         ts(sm(0), kw, -1.0, AL.mult, 0.25, AL.add)
         for c in range(7, -1, -1):
-            a = R("AB", 128 * c, 128 * c + 16 * c + 16)
-            act(a, R("KEY", 0, 16 * c + 16), AF.Abs, col("SM", c))
-            if CFG[t]["m"][4] == "a":
+            a = R("AB", 136 * c, 136 * c + 16 * c + 17)
+            act(a, R("KEY", 7, 16 * c + 24), AF.Abs, col("SM", c))
+            if CFG[t]["red"] == "a":
                 add("a", lambda q, A, a=a, c=c: q.activation(A(a), A(a), AF.Relu, bias=A(col("NTH", 2)), scale=-1.0, accum_out=A(col("SM", 8 + c))),
-                    [a, col("SM", 8 + c)], [a, col("NTH", 2)], 20 + CY * max(64, 16 * c + 16))
+                    [a, col("SM", 8 + c)], [a, col("NTH", 2)], ("a", 20 + max(64, 16 * c + 16)))
             else:
                 add("v", lambda q, A, a=a, c=c: q.tensor_reduce(A(col("SM", 8 + c)), A(a), AxisListType.X, AL.min),
-                    [col("SM", 8 + c)], [a], CY * max(64, 16 * c + 16))
+                    [col("SM", 8 + c)], [a], ("v", 16 * c + 16))
         for z in (0, 1):
-            tt(blk("MV", z), P(6, 128 * z, 128 * z + 128), w[z], AL.mult)
-        move(CFG[t]["m"][2], whole("AS"), P(6, 128, 256), 2048.0)
-        ts(sm(2), kw, 1.0, AL.is_ge)
-        tt(sm(3), kw, R("CC", 0, 8), AL.subtract)
-        tt(sm(4), sm(3), sm(2), AL.mult)
-        if CFG[t]["m"][4] == "a":
+            tt(blk("MV", z), P(b, 128 * z, 128 * z + 128), w[z], AL.mult)
+        move(whole("AS"), P(b, 128, 256), 2048.0)
+        tt(sm(4), kw, R("CC", 0, 8), AL.subtract)
+        if CFG[t]["red"] == "a":
             ts(sm(5), sm(1), 0.001, AL.is_lt)
         else:
             ts(sm(5), sm(1), 0.25, AL.is_ge)
         tt(sm(6), sm(5), sm(4), AL.mult)
         tt(sm(7), sm(6), j0, AL.add)
         lu = R("LU", 8 * t, 8 * t + 8)
-        cp(lu, sm(7))
+        i = cp(lu, sm(7))
         cp(IND(R("SN", OS - 128, OS + 1024), lu), whole("AS"))
         cp(IND(R("SN", ON - 128, ON + 1024), lu), blk("J4B", par))
-        tt(IND(R("UW", 0, OW), lu), blk("MV", 0), blk("MV", 1), AL.add)
-        cp(IND(R("SN", OK_[t] - 128, OK_[t] + 1024), lu), whole("ZB"))
+        tt(IND(R("UW", OE, OH), lu), blk("MV", 0), blk("MV", 1), AL.add)
+        if late[t]:
+            cp(IND(R("SN", OK_[t] - 128, OK_[t] + 1024), lu), whole("ZB"))
         h = R("HF", par, 16, 2)
         tt(sm(8), kw, R("CC", 8, 16), AL.subtract)
         tt(sm(9), sm(8), h, AL.subtract)
-        tt(sm(10), sm(5), sm(2), AL.mult)
-        tt(sm(11), sm(10), sm(9), AL.mult)
+        tt(sm(11), sm(5), sm(9), AL.mult)
         tt(h, h, sm(11), AL.add)
+        return i
 
     def store(name, src, lo, hi):
         dma("s", [(lambda A: A(("#hbm", name))[:, lo:hi], lambda A: A(src))], [], [src], 512 * (hi - lo))
 
-    fill(col("NTH", 1), -2047.0)
-    fill(col("NTH", 2), 0.25)
-    for t in range(3):
-        par = t % 2
-        if t > 0:
-            if CFG[t]["m"][3] == "a":
-                move("a", P(0), R("UW", OU + par, OW, 2))
-            else:
-                mm([(P(0), whole("IDF"), R("UW", OU + par, OW, 2), True, True)])
-        up[0] = BOOST
-        shock_front(t)
-        up[0] = 0.0
-        if CFG[t]["first"]:
-            nodes_end(t, 0, nodes(t, 0))
-            shock_main(t)
-        else:
-            shock_main(t)
-            nodes_end(t, 0, nodes(t, 0))
-        D = nodes(t, 3)
-        claims(t)
+    def done(t, c):
+        src = R("UW", OU + 256 * c, OU + 256 * c + 256)
         if t < 2:
-            send_sides(t + 1, 7)
-            lists(t + 1, 0, 64, 6)
-            views(t + 1, 0, 16, CFG[t]["gv"])
-            send_views(t + 1, 7)
-            node_lists(t + 1, 6)
+            views(t + 1, c)
+        else:
+            store("yu", src, 256 * c, 256 * c + 256)
+
+    for t in range(3):
+        up[0] = CFG[t]["up"][4] + BOOST
+        shock_front(t)
+        shock_main(t)
+        D = {}
+        for c in range(4):
+            up[0] = CFG[t]["up"][c]
+            D[c] = nodes(t, c)
+        for c in CFG[t]["early"]:
+            up[0] = CFG[t]["up"][c]
+            nodes_end(t, c, D[c], ())
+        up[0] = CFG[t]["up"][5]
+        gate = claims(t)
+        if t < 2:
+            send_sides(t + 1)
+            send_own(t + 1)
+            lists(t + 1, 0, 64)
+            done(t, 0)
+            sent = send_views(t + 1)
+            up[0] = CFG[t]["up"][6]
+            node_lists(t + 1)
+            copies(t + 1)
             if t == 0:
                 names(2)
+                up[0] = S["tn2"]
+                turned_names(0, [sent])
         else:
-            store("ys", R("UW", OW, 1664), 0, 512)
-            store("yu", R("UW", OU, OU + 256), 0, 256)
-            mm(group([(P(7, 0, 64), blk("SEL", i), R("SN", ON + 64 * i, ON + 64 * i + 64)) for i in range(16)])
-               + group([(P(7, 64, 128), blk("SEL", i), R("SN", OS + 64 * i, OS + 64 * i + 64)) for i in range(16)]))
-            move("a", R("YC", 64, 128), P(7, 64, 128), 1.0 / 2048)
-            tt(R("YC", 0, 64), P(7, 0, 64), R("YC", 64, 128), AL.add)
+            store("ys", R("UW", OW, OE), 0, 512)
+            done(t, 0)
+            b = tile("P")
+            mm(group([(P(b, 0, 64), blk("SEL", i), R("SN", ON + 64 * i, ON + 64 * i + 64)) for i in range(16)])
+               + group([(P(b, 64, 128), blk("SEL", i), R("SN", OS + 64 * i, OS + 64 * i + 64)) for i in range(16)]))
+            move(R("YC", 64, 128), P(b, 64, 128), 1.0 / 2048)
+            tt(R("YC", 0, 64), P(b, 0, 64), R("YC", 64, 128), AL.add)
             dma("s", [(lambda A: A(("#hbm", "yc"))[:], lambda A: A(R("YC", 0, 64)))], [], [R("YC", 0, 64)], 32768)
             dma("s", [(lambda A, c=c: A(("#hbm", "yh"))[:, 32 * c:32 * c + 32], lambda A, c=c: A(R("HF", 2 * c, 2 * c + 2))) for c in range(8)],
                 [], [whole("HF")], 8192, rows=1024)
-        for c in (3, 2, 1):
-            if c < 3:
-                D = nodes(t, c)
-            nodes_end(t, c, D)
-            if t < 2:
-                views(t + 1, 16 * c, 16 * c + 16, CFG[t]["rv"][6 - 2 * c:8 - 2 * c])
-            else:
-                store("yu", R("UW", OU + 256 * c, OU + 256 * c + 256), 256 * c, 256 * c + 256)
+        for c in (1, 2, 3):
+            up[0] = CFG[t]["up"][c]
+            if c in late[t]:
+                nodes_end(t, c, D[c], [gate])
+            done(t, c)
     return ops
 
 
-def schedule(ops):
+def schedule(ops, urge):
     n = len(ops)
     seen = {}
+    users = {}
     for i, o in enumerate(ops):
+        o["c"], o["done"], o["dm"] = price(o["k"]["a"] if o["e"] == "f" else o["k"], M)
         deps = set()
         for kind in ("r", "w"):
             for r in o[kind]:
                 ps = _psum(r)
-                for j, k2, lo, hi in seen.get(r[0], ()):
-                    if ps and ops[j]["e"] != o["e"]:
+                for j, k2, lo, hi, st in seen.get(r[0], ()):
+                    if ps and (ops[j]["e"] != o["e"] or o["e"] == "f"):
                         deps.add(j)
-                    elif (kind == "w" or k2 == "w") and lo < r[2] and r[1] < hi:
+                    elif (kind == "w" or k2 == "w") and lo < r[2] and r[1] < hi and (st != r[3] or (lo - r[1]) % st == 0):
                         deps.add(j)
         for kind in ("r", "w"):
             for r in o[kind]:
-                seen.setdefault(r[0], []).append((i, kind, r[1], r[2]))
+                seen.setdefault(r[0], []).append((i, kind, r[1], r[2], r[3]))
         o["deps"] = deps
         o["all"] = deps | set(o["after"])
+        for x in o["tiles"]:
+            users.setdefault(x, []).append(i)
     succ = [[] for _ in range(n)]
     for i, o in enumerate(ops):
         for j in o["all"]:
             succ[j].append(i)
 
-    def lat(j, i):
-        if ops[j]["e"] == ops[i]["e"] and ops[j]["sem"] is None:
-            return 0.0 if ops[j]["e"] == "t" else LAT_S
-        return LAT_X
+    def lat(ej, j, e):
+        if ej == e and ops[j]["sem"] is None:
+            return 0.0 if e == "t" else M["ls"]
+        return M["lx"]
     prio = [0.0] * n
     for i in range(n - 1, -1, -1):
-        prio[i] = ops[i]["done"] + max([prio[k] + lat(i, k) for k in succ[i]], default=0.0)
+        prio[i] = ops[i]["done"] + max([prio[k] + lat(ops[i]["e"], i, ops[k]["e"]) for k in succ[i]], default=0.0)
     left = [len(o["all"]) for o in ops]
     ready = [0.0] * n
-    cand = {e: [] for e in "vatgsx"}
-    free = {e: 0.0 for e in "vatgsx"}
+    cand = {e: [] for e in "vatgsxf"}
+    free = {e: 0.0 for e in "vatgsxd"}
     order = {e: [] for e in "vatgsx"}
     for i in range(n):
         if left[i] == 0:
             cand[ops[i]["e"]].append(i)
     end = [0.0] * n
-    for _ in range(n):
-        best = None
-        for e in "xvatgs":
-            if cand[e]:
-                t0 = max(free[e], min(ready[i] for i in cand[e]))
-                if best is None or t0 < best[0]:
-                    best = (t0, e)
-        t0, e = best
-        key = lambda k: (prio[k] + ops[k]["up"], -k)
-        i = max((k for k in cand[e] if ready[k] <= t0 + LOOK), key=key)
-        if ready[i] > t0 + SLACK:
-            now = [k for k in cand[e] if ready[k] <= t0 + SLACK]
-            short = [k for k in now if ops[k]["c"] <= ready[i] - t0 + TOL]
+    slot = {p: [None] * POOLS[p][0] for p in POOLS}
+    open_ = {x: len(u) for x, u in users.items()}
+    till = {x: 0.0 for x in users}
+    place = {}
+    if urge is None:
+        urge = [prio[k] + ops[k]["up"] for k in range(n)]
+    key = lambda k: (urge[k], -k)
+
+    memo = {}
+
+    def slots(p):
+        if p not in memo:
+            memo[p] = sorted((0.0 if x is None else till[x] + M["lx"], s) for s, x in enumerate(slot[p]) if x is None or open_[x] == 0)
+        return memo[p]
+
+    def when(k):
+        r = ready[k]
+        if not ops[k]["tiles"]:
+            return r
+        need = {}
+        for x in ops[k]["tiles"]:
+            if x not in place:
+                need[x[0]] = need.get(x[0], 0) + 1
+                if x[-1] in "ns" and sum(y is not None and y[-1] == x[-1] and open_[y] > 0 for y in slot["P"]) >= S["c" + x[-1]]:
+                    return None
+        for p, m in need.items():
+            f = slots(p)
+            if len(f) < m + (S["res"] if p == "P" and ops[k]["e"] == "t" and ops[k]["c"] > 800 else 0):
+                return None
+            r = max(r, f[m - 1][0])
+        return r
+
+    def choose(c, t0):
+        i = max((k for k in c if c[k] <= t0 + S["look"]), key=key)
+        if c[i] > t0 + S["slack"]:
+            now = [k for k in c if c[k] <= t0 + S["slack"]]
+            short = [k for k in now if ops[k]["c"] <= c[i] - t0 + S["tol"]]
             if short:
                 i = max(short, key=key)
-            elif key(i)[0] - key(max(now, key=key))[0] < FAR:
+            elif key(i)[0] - key(max(now, key=key))[0] < S["far"]:
                 i = max(now, key=key)
-        cand[e].remove(i)
-        st = max(free[e], ready[i])
-        free[e] = st + ops[i]["c"]
-        end[i] = st + ops[i]["done"]
-        ops[i]["st"] = st
-        ops[i]["seq"] = _
+        return i
+
+    def pick(e):
+        own = {k: when(k) for k in cand[e]}
+        own = {k: r for k, r in own.items() if r is not None}
+        if e in "va":
+            fl = {k: when(k) for k in cand["f"]}
+            fl = {k: r for k, r in fl.items() if r is not None}
+            if e == "a":
+                own.update(fl)
+            elif fl:
+                tf = max(free["v"], min(fl.values()))
+                to = max(free["v"], min(own.values())) if own else 1e18
+                busy = free["a"] - tf
+                now = {k: r for k, r in fl.items() if r <= tf + S["slack"]}
+                if busy > S["th"] or len(now) > 1:
+                    if len(now) > 1 and busy <= S["th"]:
+                        now.pop(max(now, key=key))
+                    k = max(now, key=key)
+                    if to - tf > S["frac"] * ops[k]["c"]:
+                        return tf, k
+                    mine = [j for j, r in own.items() if r <= to + S["slack"]]
+                    if busy > S["th"] and key(k)[0] - key(max(mine, key=key))[0] > S["far2"]:
+                        return tf, k
+        if not own:
+            return None
+        t0 = max(free[e], min(own.values()))
+        return t0, choose(own, t0)
+
+    for step in range(n):
+        best = None
+        for e in "xavtgs":
+            p = pick(e)
+            if p is not None and (best is None or p[0] < best[0]):
+                best = (p[0], p[1], e)
+        t0, i, e = best
+        o = ops[i]
+        st = max(free[e], when(i))
+        cand[o["e"]].remove(i)
+        if o["e"] == "f":
+            o["e"], o["fn"], o["k"] = e, o["fn"][e], o["k"][e]
+            o["c"], o["done"], o["dm"] = price(o["k"], M)
+        for x in o["tiles"]:
+            if x not in place:
+                s = slots(x[0])[0][1]
+                old = slot[x[0]][s]
+                slot[x[0]][s] = x
+                memo.clear()
+                place[x] = "%s%d" % (x[0], s)
+                if old is not None:
+                    for k in users[x]:
+                        ops[k]["deps"] = ops[k]["deps"] | set(users[old])
+                        ops[k]["all"] = ops[k]["all"] | set(users[old])
+                        ready[k] = max(ready[k], till[old] + M["lx"])
+        free[e] = st + o["c"]
+        end[i] = st + o["done"]
+        if o["dm"]:
+            end[i] = max(end[i], free["d"] + o["dm"])
+            free["d"] = end[i]
+        for x in o["tiles"]:
+            open_[x] -= 1
+            till[x] = max(till[x], end[i])
+        memo.clear()
+        o["st"] = st
+        o["seq"] = step
         order[e].append(i)
         for k in succ[i]:
-            ready[k] = max(ready[k], end[i] + lat(i, k))
+            ready[k] = max(ready[k], end[i] + lat(e, i, ops[k]["e"]))
             left[k] -= 1
             if left[k] == 0:
                 cand[ops[k]["e"]].append(k)
@@ -666,7 +928,7 @@ def schedule(ops):
                     need[s] = v
             had.update(need)
             ops[i]["waits"] = sorted(need.items())
-    return order, count, max(end)
+    return order, count, max(end), place
 
 
 _PLAN = {}
@@ -674,10 +936,29 @@ _PLAN = {}
 
 def plan():
     if not _PLAN:
-        ops = build()
-        order, count, total = schedule(ops)
-        _PLAN.update(ops=ops, order=order, count=count, total=total)
+        urge = None
+        for _ in range(S["pass"]):
+            ops = build()
+            order, count, total, place = schedule(ops, urge)
+            if total < _PLAN.get("total", 1e18):
+                _PLAN.update(ops=ops, order=order, count=count, total=total, place=place)
+            new = latest(ops, order)
+            urge = new if urge is None else [S["mix"] * a + (1 - S["mix"]) * b for a, b in zip(new, urge)]
     return _PLAN
+
+
+def latest(ops, order):
+    rest = [o["done"] for o in ops]
+    before = {}
+    for e in order:
+        before.update(zip(order[e][1:], order[e]))
+    for i in sorted(range(len(ops)), key=lambda k: -ops[k]["seq"]):
+        o = ops[i]
+        for j in o["all"]:
+            rest[j] = max(rest[j], rest[i] + ops[j]["done"] + (0.0 if o["e"] == ops[j]["e"] == "t" else M["lx"]))
+        if i in before and o["e"] != "x":
+            rest[before[i]] = max(rest[before[i]], rest[i] + S["q"] * ops[before[i]]["c"])
+    return rest
 
 
 def route(T, topo, src, dst):
@@ -692,11 +973,8 @@ def bits(engines):
     return sum(1 << e for e in engines)
 
 
-def rank_program(g, core, T, topo):
-    pl = plan()
-    ops = pl["ops"]
-    cores = list(T.cores)
-    n = len(cores)
+def binder(T, sem):
+    place = plan()["place"]
 
     def A(x):
         if not isinstance(x, tuple):
@@ -704,12 +982,36 @@ def rank_program(g, core, T, topo):
         if x[0] == "#ind":
             return A(x[1]).indirect(A(x[2]))
         if x[0] == "#sem":
-            return T.sem[x[1]]
+            return sem[x[1]] if sem is not None else None
         if x[0] == "#hbm":
             return T[x[1]]
+        if x[0] == "#all":
+            return T[x[1]][:, :, x[2]:x[3]]
+        if x[0] in ("U1", "U2"):
+            return T[x[0]][:, x[1] // 512, x[1] % 512:(x[2] - 1) % 512 + 1]
+        if x[0] == "QQ":
+            return T["Q"][:, :, x[1]:x[2]]
+        if x[0][0] == "Q":
+            return T["Q"][:, int(x[0][1]), x[1]:x[2]]
+        buf = T[place.get(x[0], x[0])]
+        if x[0][:2] == "P#":
+            if len(x) > 4:
+                return buf[:, :, x[4], :]
+            if x[1] % 128 == 0 and x[2] % 128 == 0:
+                return buf[:, x[1] // 128:x[2] // 128, :, :]
+            return buf[:, x[1] // 128, x[1] % 128 // 8:(x[2] - 1) % 128 // 8 + 1, :]
         if x[3] == 1:
-            return T[x[0]][:, x[1]:x[2]]
-        return T[x[0]][:, x[1]:x[2]:x[3]]
+            return buf[:, x[1]:x[2]]
+        return buf[:, x[1]:x[2]:x[3]]
+    return A
+
+
+def rank_program(g, core, T, topo):
+    pl = plan()
+    ops = pl["ops"]
+    cores = list(T.cores)
+    n = len(cores)
+    A = binder(T, T.sem)
 
     rank = T.rank_of(core)
     if rank is None:
@@ -757,6 +1059,3 @@ def rank_program(g, core, T, topo):
                 o["fn"](q, A)
     for s, v in sorted(pl["count"].items()):
         g.wait_ge(T.sem[s], val.get(v, v))
-
-
-HOP1 = 4

@@ -1,3 +1,4 @@
+import math
 from concourse.bass import DstId, RemoteDMATransfer
 from concourse.mybir import AluOpType, AxisListType, ActivationFunctionType
 
@@ -6,9 +7,12 @@ AF = ActivationFunctionType
 F32, BF, I32, U16 = "float32", "bfloat16", "int32", "uint16"
 
 CFG = [
-    {'tree': [12, 12, -1, 0, 0], 'xs': 1, 'q0': 0, 'early': (0,), 'red': 'a', 'up': [15000, 5000, 1000, 2000, 10000, 40000, 2000], 'sub': ['pppp', 'pppp', 'pppp', 'pppp'], 'rel': 5000, 'one': 2, 'split': 1},
-    {'tree': [11, 1, 12, -1, 0], 'xs': 0, 'q0': 0, 'early': (0,), 'red': 'v', 'up': [0, 5000, 5000, 0, 30000, 10000, 2000], 'sub': ['dddd', 'ffvv', 'ppdd', 'pfpf'], 'rel': 20000, 'one': 0, 'split': 1},
-    {'tree': [11, -1, 2, 12, 2], 'xs': 0, 'q0': 0, 'early': (0, 1), 'red': 'a', 'up': [2000, 2000, 20000, 20000, 40000, 2000, 15000], 'sub': ['ffdd', 'fffv', 'dpdp', 'dddd'], 'rel': 5000, 'one': 0, 'split': 0},
+    {'tree': [12, 12, -1, -1], 'xs': 1, 'q0': 0, 'early': (0,), 'red': 'v', 'up': [20000, 10000, 2000, 2000, 15000, 30000, 15000],
+     'sub': ['pppp', 'pppp', 'pppp', 'pppp'], 'rel': 10000, 'one': 4, 'split': 0, 'c1': 'v', 'vg': 3072, 'eh': 2, 'a4': 'vv'},
+    {'tree': [0, 12, -1, 0], 'xs': 3, 'q0': 0, 'early': (0,), 'red': 'v', 'up': [5000, 20000, 0, 5000, 30000, 20000, 5000],
+     'sub': ['ffdd', 'fddd', 'dddd', 'dddd'], 'rel': 0, 'one': 2, 'split': 1, 'c1': 'v', 'vg': 4096, 'eh': 2, 'a4': 'vv'},
+    {'tree': [-1, 12, 12, 0], 'xs': 3, 'q0': 0, 'early': (0, 1, 2, 3), 'red': 'a', 'up': [2000, 2000, 0, 2000, 5000, 5000, 0],
+     'sub': ['dpdp', 'dddd', 'ddff', 'ddff'], 'rel': 40000, 'one': 2, 'split': 1, 'c1': 'v', 'vg': 1024, 'eh': 2, 'a4': 'vv'},
 ]
 
 OW, OE, OU, OH = 0, 512, 640, 1664
@@ -43,11 +47,11 @@ SCRATCH = {
     "FIT": ("sbuf", [128, 256], BF), "FF": ("sbuf", [128, 256], F32), "CL": ("sbuf", [128, 256], F32),
     "VB": ("sbuf", [128, 256], BF), "MM": ("sbuf", [128, 128], F32), "MV": ("sbuf", [128, 256], F32),
     "AS": ("sbuf", [128, 128], BF), "KEY": ("sbuf", [128, 136], F32), "KD": ("sbuf", [128, 128], F32), "KS": ("sbuf", [128, 128], F32),
-    "AB": ("sbuf", [128, 1088], F32), "SM": ("sbuf", [128, 96], F32), "LU": ("sbuf", [128, 24], U16), "YC": ("sbuf", [128, 128], F32),
+    "AB": ("sbuf", [128, 1088], F32), "SM": ("sbuf", [128, 96], F32), "LU": ("sbuf", [128, 24], U16),
 }
 POOLS = {"P": (8, "psum", 512, F32), "X": (4, "sbuf", 1024, F32), "Y": (2, "sbuf", 2048, F32), "H": (4, "sbuf", 2048, BF),
-         "D": (4, "sbuf", 2048, F32), "B": (4, "sbuf", 384, F32)}
-SCRATCH["Q"] = ("sbuf", [128, 2, 2048], F32)
+         "D": (4, "sbuf", 2048, F32), "B": (5, "sbuf", 384, F32)}
+SCRATCH["Q"] = ("sbuf", [128, 2, 128, 16], F32)
 for _p, (_k, _w, _c, _d) in POOLS.items():
     for _b in range(_k):
         SCRATCH["%s%d" % (_p, _b)] = (_w, [128, 4, 16, 8] if _p == "P" else [128, _c], _d)
@@ -55,17 +59,20 @@ PRE, POST = (0.015625, 0.015625, 1.0), (1.0, 1.0, 0.015625)
 
 SEMAPHORES = (["ev", "ea", "et", "eg", "rl"] + ["d%d" % i for i in range(110)] + ["arr%d" % i for i in range(9)] + ["rin%d" % i for i in range(9)])
 ESEM = {"v": "ev", "a": "ea", "t": "et", "g": "eg"}
-HOP1 = 4
 
-M = {"cy": 0.83 * 1.1, "fv": 30, "fa": 30, "pe": 0.45 * 1.1, "ga": 1.56, "sc": 3.8, "lx": 150.0, "ls": 90.0, "comm": 1.2,
-     "gi": 1000, "dl": 2000, "dr": 150.0, "ar": 200}
-S = {'slack': 30.0, 'boost': 10000, 'look': 200, 'tol': 300, 'far': 8000, 'th': 600, 'res': 0, 'far2': 1000000000.0, 'frac': 1.1, 'tn': -30000, 'uo': 300, 'so': 600, 'cn': 4, 'cs': 4, 'tn2': 30000, 'pass': 1, 'mix': 0.5, 'q': 1.0}
+M = {"cy": 1.0, "fv": 33, "fa": 33, "pe": 0.6, "ga": 1.56, "sc": 3.8, "lx": 170.0, "ls": 100.0, "comm": 1.2,
+     "gi": 1000, "dl": 2000, "dr": 130, "ar": 200, "fm": 0}
+S = {'slack': 30.0, 'boost': 10000, 'look': 200, 'tol': 300, 'far': 1000, 'th': 1500, 'res': 0, 'far2': 8000, 'frac': 0.2, 'tn': -10000, 'uo': 1500,
+     'so': 1500, 'cn': 5, 'cs': 3, 'tn2': -10000, 'vg': 9999, 'hop': 6, 'iters': 24000, 'temp': 50, 'seed': 2}
+MODELS = [{"w": 0.4, "cy": 0.87, "pe": 0.47, "ar": 220, "lx": 170, "ls": 100},
+          {"w": 0.27, "cy": 1.22, "pe": 0.79, "ga": 1.9, "sc": 5.0, "comm": 1.2, "ar": 200, "lx": 150, "ls": 90, "fv": 40, "fa": 40},
+          {"w": 0.33, "cy": 1.05, "pe": 0.64, "ga": 1.2, "sc": 2.5, "comm": 1.3, "ar": 155, "gi": 1300, "dl": 2800, "lx": 220, "ls": 120}]
 
 
 def price(k, m):
     cy = m["cy"]
     if k[0] == "ns":
-        return k[1], k[2], 0.0
+        return k[1], k[2], 500.0
     if k[0] == "comm":
         return 0.0, k[1] * m["comm"] - 2500, 0.0
     if k[0] == "dma":
@@ -73,7 +80,7 @@ def price(k, m):
     if k[0] == "acc":
         return m["gi"], m["dl"] + k[1] / m["ar"], k[1] / m["ar"]
     c = {"v": m["fv"] + cy * max(64, k[1]), "a": m["fa"] + cy * max(64, k[1]), "vg": 50 + m["ga"] * cy * k[1], "ag": 65 + m["ga"] * cy * k[1],
-         "vs": 50 + m["sc"] * cy * k[1], "t": m["pe"] * k[1], "g": 130 + 2 * cy * k[1]}[k[0]]
+         "vs": 50 + m["sc"] * cy * k[1], "t": m["pe"] * k[1] + m["fm"] * k[-1], "g": 130 + 2 * cy * k[1]}[k[0]]
     return c, c, 0.0
 
 
@@ -89,7 +96,7 @@ def _n(r):
     if r[0] == "#ind":
         return 16 * _n(r[2])
     if len(r) > 4:
-        return 32
+        return 256 if r[0][0] == "Q" else 32
     return (r[2] - r[1] + r[3] - 1) // r[3]
 
 
@@ -120,6 +127,7 @@ def build():
     nsem = [0]
     up = [0.0]
     ntile = [0]
+    now = [3]
 
     def tile(pool, kind=""):
         ntile[0] += 1
@@ -133,7 +141,7 @@ def build():
             else:
                 w.append(o)
         tiles = sorted(set([x[0] for x in w + r if "#" in x[0]] + list(hold)))
-        ops.append({"e": eng, "fn": fn, "w": w, "r": r, "k": cost, "sem": sem, "after": list(after), "up": up[0], "tiles": tiles})
+        ops.append({"e": eng, "fn": fn, "w": w, "r": r, "k": cost, "sem": sem, "after": list(after), "up": up[0], "t": now[0], "tiles": tiles})
         return len(ops) - 1
 
     def vcost(out, a, b=None):
@@ -236,9 +244,10 @@ def build():
     load("s", R("SBI", 64, 128), "nr", 32768)
     dma("a", [(lambda A: A(R("UB", OU, OU + 256)), lambda A: A(("#hbm", "u0"))[:, 0:256])], [R("UB", OU, OU + 256)], [], 65536)
     load("a", R("UB", OW, OE), "w0", 196608)
-    dma("a", [(lambda A: A(R("UB", OU + 256, OH)), lambda A: A(("#hbm", "u0"))[:, 256:1024])], [R("UB", OU + 256, OH)], [], 393216)
+    up[0] = 45000.0
+    i = load("s", whole("TL"), "tl", 780000)
     up[0] = 40000.0
-    load("s", whole("TL"), "tl", 900000)
+    dma("s", [(lambda A: A(R("UB", OU + 256, OH)), lambda A: A(("#hbm", "u0"))[:, 256:1024])], [R("UB", OU + 256, OH)], [], 980000, [i])
     up[0] = 0.0
     load("s", col("TH", 0), "th", 512)
     dma("s", [(lambda A, c=c: A(R("HI", 2 * c, 2 * c + 2)), lambda A, c=c: A(("#hbm", "hs"))[:, 32 * c:32 * c + 32]) for c in range(8)],
@@ -258,7 +267,7 @@ def build():
     ts(idb, whole("PM"), 0.0, AL.is_equal)
     for i in range(16):
         move(blk("BC", i), whole("ONB"), col("SC", i))
-        ts(blk("SEL", i), idb, col("SC", i), AL.mult)
+        move(blk("SEL", i), idb, col("SC", i))
     ts(R("VC", 0, 64), R("J", 0, 64), 16.0, AL.mult, lane, AL.add)
     ts(R("VC", 64, 128), R("VC", 0, 64), float(OU), AL.add)
     ts(R("VC", 128, 192), R("VC", 0, 64), OU - 2049.0, AL.add)
@@ -426,22 +435,28 @@ def build():
             for lv in range(1, long - 10):
                 acc(D, 0, 1024 >> lv, 1024 >> lv)
 
-    def tree(D, b, dst, keep, long, scale, gate=()):
+    def tree(D, b, dst, keep, long, scale, c1, gate=()):
         B = tile("B")
         tb = lambda lo, hi: R(B, lo, hi)
         if long > 10:
             b = tile("P")
+
+            def third(parts):
+                if c1 == "a":
+                    mm(group([(P(b, 128, 256), idf, x) for x in parts + [tb(128, 256)]]))
+                    move(tb(256, 384), P(b, 128, 256))
+                else:
+                    mm(group([(P(b, 128, 256), idf, x) for x in parts]))
+                    tt(tb(256, 384), P(b, 128, 256), tb(128, 256), AL.add)
             if long == 21:
                 mm(group([(P(b, 256, 512), idf, R(D, 256, 512)), (P(b, 256, 512), idf, R(D, 1792, 2048))]))
                 move(tb(0, 256), P(b, 256, 512))
-                mm(group([(P(b, 128, 256), idf, blk(D, 1)), (P(b, 128, 256), idf, blk(D, 13))]))
-                tt(tb(256, 384), P(b, 128, 256), tb(128, 256), AL.add)
+                third([blk(D, 1), blk(D, 13)])
                 fin = [blk(D, 0), blk(D, 12), tb(0, 128), tb(256, 384)]
             elif long == 11:
                 mm(group([(P(b, 256, 512), idf, R(D, 256, 512)), (P(b, 256, 512), idf, R(D, 768, 1024))]))
                 move(tb(0, 256), P(b, 256, 512))
-                mm(group([(P(b, 128, 256), idf, blk(D, 1)), (P(b, 128, 256), idf, blk(D, 5))]))
-                tt(tb(256, 384), P(b, 128, 256), tb(128, 256), AL.add)
+                third([blk(D, 1), blk(D, 5)])
                 fin = [blk(D, 0), blk(D, 4), tb(0, 128), tb(256, 384)]
             elif long == 12:
                 mm(group([(P(b, 128, 256), idf, blk(D, 1)), (P(b, 128, 256), idf, blk(D, 3))]))
@@ -552,7 +567,7 @@ def build():
     def nodes_end(t, c, D, gate):
         par = t % 2
         keep = R("SN", OK_[t] + 256 * c + par, OK_[t] + 256 * c + 256, 2) if c in late[t] else None
-        tree(D[0], D[1], R("UW", OU + 256 * c + par, OU + 256 * c + 256, 2), keep, CFG[t]["tree"][c], POST[t], gate)
+        tree(D[0], D[1], R("UW", OU + 256 * c + par, OU + 256 * c + 256, 2), keep, CFG[t]["tree"][c], POST[t], CFG[t]["c1"], gate)
 
     def shock_front(t):
         par = t % 2
@@ -561,13 +576,17 @@ def build():
         for h in (0, 1):
             o = 128 * t + 64 * h
             move(R("E", 1024 * h, 1024 * h + 1024), IND(R("SN", OS, OS + 1280), R("NMU", o, o + 64)), -1.0 / 2048)
-        e = P(tile("P"), 0, 128)
-        mm(group([(e, blk("SEL", k), R("E", k, 2048, 16)) for k in range(16)]))
-        tt(blk("XF", 1), blk("J4", par), e, AL.subtract)
-        cp(blk("XU", 1), blk("XF", 1))
-        tt(blk("FIT", 0), blk("OWN", t), e, AL.mult)
-        tt(blk("FIT", 1), blk("OWN", t), e, AL.is_lt)
-        up[0] = CFG[t]["up"][5]
+        w = 128 // CFG[t]["eh"]
+        for x in range(0, 128, w):
+            e = P(tile("P"), 0, w)
+            part = lambda name, o: R(name, o + x, o + x + w)
+            up[0] = CFG[t]["up"][4] + BOOST
+            mm(group([(e, blk("SEL", k), R("E", 16 * x + k, 16 * (x + w), 16)) for k in range(16)]))
+            tt(part("XF", 128), part("J4", 128 * par), e, AL.subtract)
+            cp(part("XU", 128), part("XF", 128))
+            up[0] = CFG[t]["up"][5]
+            tt(part("FIT", 0), part("OWN", 128 * t), e, AL.mult)
+            tt(part("FIT", 128), part("OWN", 128 * t), e, AL.is_lt)
         b = tile("P")
         mm(group([(P(b, 0, 256), whole("TRM"), whole("FIT")), (P(b, 0, 128), idf, blk("NM2", t)), (P(b, 128, 256), idf, blk("NM2", t))]))
         act(whole("FF"), P(b, 0, 256), AF.Relu, col("NTH", 1), 0.5)
@@ -583,62 +602,79 @@ def build():
         up[0] = cf["up"][4]
         if t == 2:
             move(R("UW", OH, OH + 256), whole("GO"))
+        own = [IND(R(u_, OU, OH + 256), R("NMU", 128 * t + 64 * h, 128 * t + 64 * h + 64)) for h in (0, 1)]
+        cols = [IND(R(u_, OW, OE), R("XU", 128 + 64 * h, 192 + 64 * h)) for h in (0, 1)]
         for h in (0, 1):
-            o = 128 * t + 64 * h
-            move(R(us, 1024 * h, 1024 * h + 1024), IND(R(u_, OU, OH + 256), R("NMU", o, o + 64)), hold=[xs])
-        for h in (0, 1):
-            lu, part = R("XU", 128 + 64 * h, 192 + 64 * h), (1024 * h, 1024 * h + 1024)
+            up[0] = cf["up"][4] + 2 * S["so"] * (1 - h)
+            part = (1024 * h, 1024 * h + 1024)
+            if cf["xs"] == 3:
+                move(R(us, *part), cols[h], -1.0, hold=[xs])
+                add("v", lambda q, A, h=h, part=part: q.tensor_tensor(A(R(xs, *part)), A(own[h]), A(R(us, *part)), AL.add),
+                    [R(xs, *part)], [own[h], R(us, *part)], ("vg", 1024))
+                continue
+            move(R(us, *part), own[h], -1.0 if cf["xs"] == 2 else None, hold=[xs])
             if cf["xs"]:
-                move(R(xs, *part), IND(R(u_, OW, OE), lu))
+                move(R(xs, *part), cols[h])
+                if cf["xs"] == 2:
+                    acc([xs], part[0], part[1], 0, us)
             else:
-                tt(R(xs, *part), IND(R(u_, OW, OE), lu), R(us, *part), AL.subtract)
-        long = cf["tree"][4]
-        sb = [tile("P"), tile("P")] if long < 10 else [None, None]
+                tt(R(xs, *part), cols[h], R(us, *part), AL.subtract)
         pos, neg = ("IDB", "NIDB") if t == 0 else ("IDF", "NIDF")
-        for u in (0, 2, 1, 3):
-            up[0] = cf["up"][4] + S["so"] * (3, 1, 2, 0)[u]
+        for u in range(4):
+            up[0] = cf["up"][4] + S["so"] * (3 - u)
             b = tile("P", "s")
-            q0, q1 = R(Q[0], 512 * u, 512 * u + 512), R(Q[1], 512 * u, 512 * u + 512)
-            if cf["xs"]:
-                items = []
-                for kk in range(4):
-                    o = P(b, 128 * kk, 128 * kk + 128)
-                    items += group([(o, whole(pos), R(xs, 4 * u + kk, 2048, 16)), (o, whole(neg), R(us, 4 * u + kk, 2048, 16))])
-                mm(items)
+            part = (512 * u, 512 * u + 512)
+            q0, q1 = R(Q[0], *part), R(Q[1], *part)
+            if cf["xs"] == 1:
+                for x in range(0, 512, 512 if t == 0 else 128):
+                    w = (part[0] + x, part[0] + x + (512 if t == 0 else 128))
+                    o = P(b, x, x + w[1] - w[0])
+                    mm(group([(o, whole(pos), R(xs, *w)), (o, whole(neg), R(us, *w))]))
                 act(q0, P(b), AF.Abs, 0.0, PRE[t])
                 tt(q0 if cf["q0"] else P(b), P(b), q0, AL.mult)
             else:
-                for kk in range(4):
-                    act(P(b, 128 * kk, 128 * kk + 128), R(xs, 4 * u + kk, 2048, 16), AF.Abs, 0.0, PRE[t])
-                for kk in range(4):
-                    o = P(b, 128 * kk, 128 * kk + 128)
-                    tt(blk(Q[0], 4 * u + kk) if cf["q0"] else o, o, R(xs, 4 * u + kk, 2048, 16), AL.mult)
+                act(P(b), R(xs, *part), AF.Abs, 0.0, PRE[t])
+                tt(q0 if cf["q0"] else P(b), P(b), R(xs, *part), AL.mult)
             if cf["q0"]:
                 b = tile("P")
-                mm([(P(b, 128 * kk, 128 * kk + 128), idb, R("E", 4 * u + kk, 2048, 16), True, True) for kk in range(4)])
+                mm([(P(b), idb, R("E", *part), True, True)])
                 tt(q1, P(b), q0, AL.mult)
-                if u == 3:
-                    acc([Q[0]], 0, 2048, 0, Q[1])
-                    levels(Q, long, u, False)
-                continue
-            for kk in range(4):
-                tt(blk(Q[1], 4 * u + kk), P(b, 128 * kk, 128 * kk + 128), R("E", 4 * u + kk, 2048, 16), AL.mult)
-            tt(P(b) if (u == 1 and long in VA) else q0, P(b), q1, AL.add)
-            if long > 10:
-                levels(Q, long, u, cf["split"])
-            if long not in VA:
-                continue
-            if u == 1:
-                b1 = b
-            elif u == 3:
-                tt(q1, R(Q[1], 512, 1024), q1, AL.add)
-                tt(q0, P(b1), q0, AL.add)
-            elif long < 10:
-                tree_a(Q[1], sb[1], u, long)
-                tree_a(Q[0], sb[0], u, long)
-        for z in (1, 0):
-            tree(Q[z], sb[z], R("UW", OW + 2 * par + z, OE, 4), None, long, (-POST[t], POST[t])[z])
+                if u % 2:
+                    acc([Q[0]], part[0] - 512, part[1], 0, Q[1])
+            else:
+                tt(q1, P(b), R("E", *part), AL.mult)
+                tt(q0, P(b), q1, AL.add)
+            if u % 2:
+                for z in (1, 0):
+                    shock_tree(t, u // 2, z)
         up[0] = 0.0
+
+    def shock_tree(t, h, z):
+        lo, hi = 1024 * h, 1024 * h + 1024
+        q = lambda k: R("Q%d" % z, lo + k, hi, 16)
+        four = lambda k: ("Q%d" % z, lo, hi, 1, k)
+        b, B = tile("P"), tile("B")
+        if CFG[t]["a4"][h] == "v":
+            tt(four(4), four(4), four(12), AL.add)
+        else:
+            mm(group([(P(b, 256, 512), idf, four(4)), (P(b, 256, 512), idf, four(12))]))
+            move(four(4), P(b, 256, 512))
+        mm([x for k in (2, 3) for x in group([(P(b, 64 * k, 64 * k + 64), idf, q(j)) for j in (k, k + 8, k + 4)])])
+        move(R(B, 0, 128), P(b, 128, 256))
+        if CFG[t]["c1"] == "a":
+            mm(group([(P(b, 64, 128), idf, x) for x in (q(1), q(9), q(5), R(B, 64, 128))]))
+            move(R(B, 128, 192), P(b, 64, 128))
+        else:
+            mm(group([(P(b, 64, 128), idf, x) for x in (q(1), q(9), q(5))]))
+            tt(R(B, 128, 192), P(b, 64, 128), R(B, 64, 128), AL.add)
+        mm(group([(P(b, 0, 64), idf, x) for x in (q(0), q(8), q(4), R(B, 0, 64), R(B, 128, 192))]))
+        dst = R("UW", OW + 256 * h + 2 * (t % 2) + z, OW + 256 * h + 256, 4)
+        plus = z ^ (CFG[t]["xs"] == 3)
+        if POST[t] == 1.0:
+            tt(dst, dst, P(b, 0, 64), (AL.subtract, AL.add)[plus])
+        else:
+            move(P(b, 64, 128), P(b, 0, 64), (-POST[t], POST[t])[plus])
+            tt(dst, P(b, 64, 128), dst, AL.add)
 
     def claims(t):
         par = t % 2
@@ -669,7 +705,7 @@ def build():
                     [col("SM", 8 + c)], [a], ("v", 16 * c + 16))
         for z in (0, 1):
             tt(blk("MV", z), P(b, 128 * z, 128 * z + 128), w[z], AL.mult)
-        move(whole("AS"), P(b, 128, 256), 2048.0)
+        move(whole("AS"), P(b, 128, 256), 2048.0) if t < 2 else move(whole("KD"), P(b, 128, 256))
         tt(sm(4), kw, R("CC", 0, 8), AL.subtract)
         if CFG[t]["red"] == "a":
             ts(sm(5), sm(1), 0.001, AL.is_lt)
@@ -679,8 +715,11 @@ def build():
         tt(sm(7), sm(6), j0, AL.add)
         lu = R("LU", 8 * t, 8 * t + 8)
         i = cp(lu, sm(7))
-        cp(IND(R("SN", OS - 128, OS + 1024), lu), whole("AS"))
-        cp(IND(R("SN", ON - 128, ON + 1024), lu), blk("J4B", par))
+        if t < 2:
+            cp(IND(R("SN", OS - 128, OS + 1024), lu), whole("AS"))
+            cp(IND(R("SN", ON - 128, ON + 1024), lu), blk("J4B", par))
+        else:
+            tt(IND(R("VW1", 0, 1152), lu), blk("J4", par), whole("KD"), AL.add)
         tt(IND(R("UW", OE, OH), lu), blk("MV", 0), blk("MV", 1), AL.add)
         if late[t]:
             cp(IND(R("SN", OK_[t] - 128, OK_[t] + 1024), lu), whole("ZB"))
@@ -702,6 +741,7 @@ def build():
             store("yu", src, 256 * c, 256 * c + 256)
 
     for t in range(3):
+        now[0] = t
         up[0] = CFG[t]["up"][4] + BOOST
         shock_front(t)
         shock_main(t)
@@ -712,6 +752,12 @@ def build():
         for c in CFG[t]["early"]:
             up[0] = CFG[t]["up"][c]
             nodes_end(t, c, D[c], ())
+        if t == 2:
+            up[0] = CFG[t]["up"][6]
+            for x in (0, 512):
+                b = tile("P")
+                mm(group([(P(b), idb, R("SN", ON + x, ON + x + 512)), (P(b), whole("IDS"), R("SN", OS + x, OS + x + 512))]))
+                move(R("VW1", 128 + x, 640 + x), P(b))
         up[0] = CFG[t]["up"][5]
         gate = claims(t)
         if t < 2:
@@ -730,12 +776,8 @@ def build():
         else:
             store("ys", R("UW", OW, OE), 0, 512)
             done(t, 0)
-            b = tile("P")
-            mm(group([(P(b, 0, 64), blk("SEL", i), R("SN", ON + 64 * i, ON + 64 * i + 64)) for i in range(16)])
-               + group([(P(b, 64, 128), blk("SEL", i), R("SN", OS + 64 * i, OS + 64 * i + 64)) for i in range(16)]))
-            move(R("YC", 64, 128), P(b, 64, 128), 1.0 / 2048)
-            tt(R("YC", 0, 64), P(b, 0, 64), R("YC", 64, 128), AL.add)
-            dma("s", [(lambda A: A(("#hbm", "yc"))[:], lambda A: A(R("YC", 0, 64)))], [], [R("YC", 0, 64)], 32768)
+            dma("a", [(lambda A, c=c: A(("#hbm", "yc"))[c:c + 1, :], lambda A, c=c: A(("#hbm", "VW1"))[16 * c:16 * c + 1, 128:1152]) for c in range(8)],
+                [], [R("VW1", 128, 1152)], 32768)
             dma("s", [(lambda A, c=c: A(("#hbm", "yh"))[:, 32 * c:32 * c + 32], lambda A, c=c: A(R("HF", 2 * c, 2 * c + 2))) for c in range(8)],
                 [], [whole("HF")], 8192, rows=1024)
         for c in (1, 2, 3):
@@ -746,7 +788,7 @@ def build():
     return ops
 
 
-def schedule(ops, urge):
+def schedule(ops):
     n = len(ops)
     seen = {}
     users = {}
@@ -793,11 +835,13 @@ def schedule(ops, urge):
     open_ = {x: len(u) for x, u in users.items()}
     till = {x: 0.0 for x in users}
     place = {}
-    if urge is None:
-        urge = [prio[k] + ops[k]["up"] for k in range(n)]
-    key = lambda k: (urge[k], -k)
+    urge = [(prio[k] + ops[k]["up"], -k) for k in range(n)]
+    urge = S.get("urge") or urge
+    key = lambda k: urge[k]
 
     memo = {}
+    quota = [c["vg"] for c in CFG] + [S["vg"]]
+    busy_ = {"n": 0, "s": 0}
 
     def slots(p):
         if p not in memo:
@@ -806,14 +850,14 @@ def schedule(ops, urge):
 
     def when(k):
         r = ready[k]
-        if not ops[k]["tiles"]:
+        new = [x for x in ops[k]["tiles"] if x not in place]
+        if not new:
             return r
         need = {}
-        for x in ops[k]["tiles"]:
-            if x not in place:
-                need[x[0]] = need.get(x[0], 0) + 1
-                if x[-1] in "ns" and sum(y is not None and y[-1] == x[-1] and open_[y] > 0 for y in slot["P"]) >= S["c" + x[-1]]:
-                    return None
+        for x in new:
+            need[x[0]] = need.get(x[0], 0) + 1
+            if x[-1] in busy_ and busy_[x[-1]] >= S["c" + x[-1]]:
+                return None
         for p, m in need.items():
             f = slots(p)
             if len(f) < m + (S["res"] if p == "P" and ops[k]["e"] == "t" and ops[k]["c"] > 800 else 0):
@@ -832,15 +876,14 @@ def schedule(ops, urge):
                 i = max(now, key=key)
         return i
 
-    def pick(e):
-        own = {k: when(k) for k in cand[e]}
-        own = {k: r for k, r in own.items() if r is not None}
+    def pick(e, fl):
+        own = {k: r for k, r in ((k, when(k)) for k in cand[e]) if r is not None}
         if e in "va":
-            fl = {k: when(k) for k in cand["f"]}
-            fl = {k: r for k, r in fl.items() if r is not None}
             if e == "a":
                 own.update(fl)
-            elif fl:
+            else:
+                fl = {k: r for k, r in fl.items() if ops[k]["k"]["v"][0] != "vg" or quota[ops[k]["t"]] >= ops[k]["k"]["v"][1]}
+            if e == "v" and fl:
                 tf = max(free["v"], min(fl.values()))
                 to = max(free["v"], min(own.values())) if own else 1e18
                 busy = free["a"] - tf
@@ -859,10 +902,12 @@ def schedule(ops, urge):
         t0 = max(free[e], min(own.values()))
         return t0, choose(own, t0)
 
+    seq = []
     for step in range(n):
         best = None
+        fl = {k: r for k, r in ((k, when(k)) for k in cand["f"]) if r is not None}
         for e in "xavtgs":
-            p = pick(e)
+            p = pick(e, fl) if cand[e] or e in "av" else None
             if p is not None and (best is None or p[0] < best[0]):
                 best = (p[0], p[1], e)
         t0, i, e = best
@@ -870,19 +915,22 @@ def schedule(ops, urge):
         st = max(free[e], when(i))
         cand[o["e"]].remove(i)
         if o["e"] == "f":
+            o["alt"], o["fns"] = o["k"], o["fn"]
             o["e"], o["fn"], o["k"] = e, o["fn"][e], o["k"][e]
             o["c"], o["done"], o["dm"] = price(o["k"], M)
+            if o["k"][0] == "vg":
+                quota[o["t"]] -= o["k"][1]
         for x in o["tiles"]:
             if x not in place:
                 s = slots(x[0])[0][1]
                 old = slot[x[0]][s]
                 slot[x[0]][s] = x
                 memo.clear()
+                if x[-1] in busy_:
+                    busy_[x[-1]] += 1
                 place[x] = "%s%d" % (x[0], s)
                 if old is not None:
                     for k in users[x]:
-                        ops[k]["deps"] = ops[k]["deps"] | set(users[old])
-                        ops[k]["all"] = ops[k]["all"] | set(users[old])
                         ready[k] = max(ready[k], till[old] + M["lx"])
         free[e] = st + o["c"]
         end[i] = st + o["done"]
@@ -892,15 +940,24 @@ def schedule(ops, urge):
         for x in o["tiles"]:
             open_[x] -= 1
             till[x] = max(till[x], end[i])
-        memo.clear()
+            if open_[x] == 0:
+                memo.clear()
+                if x[-1] in busy_:
+                    busy_[x[-1]] -= 1
         o["st"] = st
-        o["seq"] = step
-        order[e].append(i)
+        seq.append(i)
         for k in succ[i]:
             ready[k] = max(ready[k], end[i] + lat(e, i, ops[k]["e"]))
             left[k] -= 1
             if left[k] == 0:
                 cand[ops[k]["e"]].append(k)
+    seq, before, place = refine(ops, seq, users)
+    for x, old in before.items():
+        for k in users[x]:
+            ops[k]["deps"] = ops[k]["deps"] | set(users[old])
+    for p, i in enumerate(seq):
+        ops[i]["seq"] = p
+        order[ops[i]["e"]].append(i)
     count = {}
     for e in "vatg":
         c = 0
@@ -931,34 +988,172 @@ def schedule(ops, urge):
     return order, count, max(end), place
 
 
+def refine(ops, seq, users):
+    n, E, GAP = len(ops), "vatgsx", 48
+    pos = [0] * n
+    for p, i in enumerate(seq):
+        pos[i] = p
+    reach, pre = [0] * n, [None] * n
+    for i in seq:
+        pre[i], r = [], 0
+        for j in sorted(ops[i]["all"] if ops[i]["e"] == "x" else ops[i]["deps"], key=lambda j: -pos[j]):
+            if not r >> j & 1:
+                pre[i].append(j)
+                r |= reach[j] | 1 << j
+        reach[i] = r
+    names = sorted(users)
+    tiles = [[names.index(x) for x in o["tiles"]] for o in ops]
+    first, base = {}, 0
+    for p in POOLS:
+        first[p] = range(base, base + POOLS[p][0])
+        base += POOLS[p][0]
+    pool = [first[x[0]] for x in names]
+    eng = [E.index(o["e"]) for o in ops]
+    alt = ["alt" in o for o in ops]
+    sem = [o["sem"] is not None for o in ops]
+    cost = [[{E.index(e): price(k, dict(M, **m)) for e, k in o.get("alt", {o["e"]: o["k"]}).items()} for o in ops] for m in MODELS]
+    for c_, m in zip(cost, MODELS):
+        c_.append((m["lx"], [m["ls"], m["ls"], 0.0, m["ls"], m["ls"], 0.0]))
+    nt = len(names)
+
+    post = [[] for _ in ops]
+    for i in seq:
+        for j in pre[i]:
+            post[j].append(i)
+
+    def run(c_, old, p0, far, given):
+        lx, same = c_[n]
+        end, why, marks = old[0][:], old[1][:], old[2][:p0 // GAP + 1]
+        free, last, dfree, ld, slot, left, till, got, by = [x[:] if isinstance(x, list) else x for x in marks[-1]]
+        for p in range(p0 // GAP * GAP, n):
+            if p % GAP == 0 and p > p0:
+                if p > far and old[2][p // GAP] == (free, last, dfree, ld, slot, left, till, got, by):
+                    return end, why, marks + old[2][p // GAP:], old[3]
+                marks.append((free[:], last[:], dfree, ld, slot[:], left[:], till[:], got[:], by[:]))
+            i = seq[p]
+            e = eng[i]
+            c, d, dm = c_[i][e]
+            r, w = free[e], -2 - last[e]
+            for j in pre[i]:
+                y = end[j] + (lx if (sem[j] or eng[j] != e) else same[e])
+                if y > r:
+                    r, w = y, j
+            for x in tiles[i]:
+                if got[x] is None:
+                    if given is None:
+                        s, y = -1, 1e18
+                        for k in pool[x]:
+                            h = slot[k]
+                            if h < 0:
+                                s, y = k, -1.0
+                                break
+                            if left[h] == 0 and till[h] < y:
+                                s, y = k, till[h]
+                        if s < 0:
+                            return None
+                        got[x] = (s, slot[s])
+                        slot[s] = x
+                    else:
+                        got[x] = given[x]
+                h = got[x][1]
+                if h >= 0 and till[h] + lx > r:
+                    r, w = till[h] + lx, by[h]
+            if e < 5:
+                free[e], last[e] = r + c, i
+            y = r + d
+            if dm:
+                if dfree + dm > y:
+                    y, w = dfree + dm, -2 - ld
+                dfree, ld = y, i
+            if y != end[i]:
+                end[i] = y
+                for j in post[i]:
+                    if pos[j] > far:
+                        far = pos[j]
+            why[i] = w
+            for x in tiles[i]:
+                left[x] -= 1
+                if y > till[x]:
+                    till[x], by[x] = y, i
+        return end, why, marks, got
+
+    def both(state, p0, far):
+        a = run(cost[0], state[0], p0, far, None)
+        if a and a[3] != state[0][3]:
+            far = n
+        return a and [a] + [run(c_, s, p0, far, a[3]) for c_, s in zip(cost[1:], state[1:])]
+
+    def path(s):
+        arcs, i = [], s[0].index(max(s[0]))
+        while i >= 0:
+            w = s[1][i]
+            if w < -1:
+                w = -2 - w
+                arcs.append((w, i))
+            i = w
+        return arcs
+    seed = [S["seed"]]
+
+    def rnd():
+        seed[0] = (seed[0] * 1664525 + 1013904223) % 4294967296
+        return seed[0] / 4294967296
+    start = ([0.0] * 6, [-1] * 6, 0.0, -1, [-1] * base, [len(users[x]) for x in names], [0.0] * nt, [None] * nt, [-1] * nt)
+    state = both([([0.0] * n, [-1] * n, [start], None)] * len(MODELS), 0, n)
+    worth = lambda st: sum(m["w"] * max(s[0]) for m, s in zip(MODELS, st))
+    cur, arcs = worth(state), [path(s) for s in state]
+    best = (cur, seq[:], eng[:], state[0][3])
+    for it in range(S["iters"]):
+        a = arcs[int(rnd() * len(arcs))]
+        w, i = a[int(rnd() * len(a))]
+        x, old = rnd(), None
+        if x < 0.12 and (alt[i] or alt[w]):
+            k = i if (alt[i] and (not alt[w] or rnd() < 0.5)) else w
+            eng[k] = 1 - eng[k]
+            lo, hi = pos[k], max([pos[j] for j in post[k]] + [pos[k]])
+        else:
+            lo, hi, early = pos[w], pos[i], x < 0.6
+            for _ in range(int(rnd() * rnd() * S["hop"])):
+                p, step = (lo - 1, -1) if early else (hi + 1, 1)
+                while 0 <= p < n and eng[seq[p]] != eng[i]:
+                    p += step
+                if not 0 <= p < n or (reach[i] >> seq[p] if early else reach[seq[p]] >> w) & 1:
+                    break
+                lo, hi = (p, hi) if early else (lo, p)
+            old = seq[lo:hi + 1]
+            tied = [k for k in old if (reach[i] >> k if early else reach[k] >> w) & 1]
+            if (w if early else i) in tied or len(tied) > 8:
+                continue
+            rest = [k for k in old if k not in tied and k != (i if early else w)]
+            seq[lo:hi + 1] = tied + [i] + rest if early else rest + [w] + tied
+        new = both(state, lo, hi)
+        c2 = worth(new) if new else 1e18
+        if c2 <= cur or rnd() < math.exp((cur - c2) / (S["temp"] * max(1 - it / S["iters"], 0.02))):
+            cur, state, arcs = c2, new, [path(s) for s in new]
+            for p in range(lo, lo + len(old or ())):
+                pos[seq[p]] = p
+            if cur < best[0]:
+                best = (cur, seq[:], eng[:], state[0][3])
+        elif old:
+            seq[lo:lo + len(old)] = old
+        else:
+            eng[k] = 1 - eng[k]
+    for i, o in enumerate(ops):
+        if alt[i]:
+            e = E[best[2][i]]
+            o["e"], o["k"], o["fn"] = e, o["alt"][e], o["fns"][e]
+    before = {names[x]: names[g[1]] for x, g in enumerate(best[3]) if g[1] >= 0}
+    return best[1], before, {names[x]: "%s%d" % (names[x][0], g[0] - pool[x][0]) for x, g in enumerate(best[3])}
+
+
 _PLAN = {}
 
 
 def plan():
     if not _PLAN:
-        urge = None
-        for _ in range(S["pass"]):
-            ops = build()
-            order, count, total, place = schedule(ops, urge)
-            if total < _PLAN.get("total", 1e18):
-                _PLAN.update(ops=ops, order=order, count=count, total=total, place=place)
-            new = latest(ops, order)
-            urge = new if urge is None else [S["mix"] * a + (1 - S["mix"]) * b for a, b in zip(new, urge)]
+        ops = build()
+        order, count, total, place = schedule(ops)
+        _PLAN.update(ops=ops, order=order, count=count, total=total, place=place)
     return _PLAN
-
-
-def latest(ops, order):
-    rest = [o["done"] for o in ops]
-    before = {}
-    for e in order:
-        before.update(zip(order[e][1:], order[e]))
-    for i in sorted(range(len(ops)), key=lambda k: -ops[k]["seq"]):
-        o = ops[i]
-        for j in o["all"]:
-            rest[j] = max(rest[j], rest[i] + ops[j]["done"] + (0.0 if o["e"] == ops[j]["e"] == "t" else M["lx"]))
-        if i in before and o["e"] != "x":
-            rest[before[i]] = max(rest[before[i]], rest[i] + S["q"] * ops[before[i]]["c"])
-    return rest
 
 
 def route(T, topo, src, dst):
@@ -989,10 +1184,11 @@ def binder(T, sem):
             return T[x[1]][:, :, x[2]:x[3]]
         if x[0] in ("U1", "U2"):
             return T[x[0]][:, x[1] // 512, x[1] % 512:(x[2] - 1) % 512 + 1]
-        if x[0] == "QQ":
-            return T["Q"][:, :, x[1]:x[2]]
         if x[0][0] == "Q":
-            return T["Q"][:, int(x[0][1]), x[1]:x[2]]
+            z, lo, hi = int(x[0][1]), x[1] // 16, x[2] // 16
+            if len(x) > 4:
+                return T["Q"][:, z, lo:hi, x[4]:x[4] + 4]
+            return T["Q"][:, z, lo:hi, x[1] % 16] if x[3] == 16 else T["Q"][:, z, lo:hi, :]
         buf = T[place.get(x[0], x[0])]
         if x[0][:2] == "P#":
             if len(x) > 4:
@@ -1027,7 +1223,7 @@ def rank_program(g, core, T, topo):
                     fn = ops[i]["fn"]
                     if isinstance(fn, tuple):
                         m, d = fn[1], fn[3][half]
-                        g.wait_ge(T.sem["rin%d" % m], HOP1)
+                        g.wait_ge(T.sem["rin%d" % m], len(topo.engines(src, core)) // 2)
                         g.remote_dma(A(d), A(d), T.sem["arr%d" % m], T.sem["rl"], pid, rid, bits(eng))
                         sent += len(eng)
                 g.wait_ge(T.sem["rl"], sent)
@@ -1036,7 +1232,8 @@ def rank_program(g, core, T, topo):
     dst, src = cores[(rank - 1) % n], cores[(rank + 1) % n]
     hops = route(T, topo, core, dst)
     back = route(T, topo, src, core)
-    val = {"#sent": 2 * HOP1, "#arr": sum(HOP1 if h == core else len(topo.engines(h, core)) for h in back)}
+    share = len(topo.engines(core, hops[0])) // 2
+    val = {"#sent": 2 * share, "#arr": sum(len(topo.engines(src, core)) // 2 if h == core else len(topo.engines(h, core)) for h in back)}
     queue = {"v": g.vector, "a": g.scalar, "t": g.tensor, "g": g, "s": g.sync}
     for e in "sagtv":
         q = queue[e]
@@ -1049,7 +1246,7 @@ def rank_program(g, core, T, topo):
                 tr = []
                 for half in (0, 1):
                     rid, pid = topo.addr(hops[half], core)
-                    eng = topo.engines(core, hops[half])[HOP1 * half:HOP1 * half + HOP1]
+                    eng = topo.engines(core, hops[half])[share * half:share * half + share]
                     tr.append(RemoteDMATransfer(dst_ids=[DstId(rid=rid, pnc=pid)], dma_engine_mask=bits(eng),
                                                 remote_sem=T.sem[("arr%d" if hops[half] == dst else "rin%d") % m], src=A(srcs[half]), dst=A(dsts[half])))
                 g.remote_dma_fused(tr, local_sem=T.sem[s])

import math
from concourse.bass import DstId, RemoteDMATransfer
from concourse.mybir import AluOpType, AxisListType, ActivationFunctionType

AL = AluOpType
AF = ActivationFunctionType
F32, BF, I32, U16 = "float32", "bfloat16", "int32", "uint16"

CFG = [
    {'tree': [12, 12, -1, -1], 'xs': 1, 'q0': 0, 'early': (0,), 'red': 'v', 'up': [20000, 10000, 2000, 2000, 15000, 30000, 15000],
     'sub': ['pppp', 'pppp', 'pppp', 'pppp'], 'rel': 10000, 'one': 4, 'split': 0, 'c1': 'v', 'vg': 3072, 'eh': 2, 'a4': 'vv'},
    {'tree': [0, 12, -1, 0], 'xs': 3, 'q0': 0, 'early': (0,), 'red': 'v', 'up': [5000, 20000, 0, 5000, 30000, 20000, 5000],
     'sub': ['ffdd', 'fddd', 'dddd', 'dddd'], 'rel': 0, 'one': 2, 'split': 1, 'c1': 'v', 'vg': 4096, 'eh': 2, 'a4': 'vv'},
    {'tree': [-1, 12, 12, 0], 'xs': 3, 'q0': 0, 'early': (0, 1, 2, 3), 'red': 'a', 'up': [2000, 2000, 0, 2000, 5000, 5000, 0],
     'sub': ['dpdp', 'dddd', 'ddff', 'ddff'], 'rel': 40000, 'one': 2, 'split': 1, 'c1': 'v', 'vg': 1024, 'eh': 2, 'a4': 'vv'},
]

OW, OE, OU, OH = 0, 512, 640, 1664
OK_ = (128, 1280, 2432)
ON, OS, OG = 3584, 4736, 5760

SCRATCH = {
    "TL": ("sbuf", [128, 1024], I32), "TL2": ("sbuf", [128, 1024], F32),
    "UB": ("sbuf", [128, 1920], BF), "UW": ("sbuf", [128, 1920], F32),
    "U1": ("sbuf", [128, 4, 512], F32), "U2": ("sbuf", [128, 4, 512], F32), "TT": ("sbuf", [128, 1024], F32), "LT": ("sbuf", [128, 896], F32), "SL": ("sbuf", [128, 64], BF),
    "SO0": ("sbuf", [128, 128], BF), "SO": ("sbuf", [128, 256], F32), "GO": ("sbuf", [128, 256], F32),
    "SN": ("sbuf", [128, 6016], BF),
    "VW0": ("sbuf", [128, 2560], BF), "VW1": ("sbuf", [128, 2560], F32), "VW2": ("sbuf", [128, 2560], F32),
    "SV0": ("sbuf", [128, 256], BF), "SV1": ("sbuf", [128, 256], F32), "SV2": ("sbuf", [128, 256], F32),
    "SS": ("sbuf", [128, 384], BF), "SG": ("sbuf", [128, 512], BF),
    "SBI": ("sbuf", [128, 128], I32), "SBB": ("sbuf", [128, 128], BF),
    "HI": ("sbuf", [128, 16], I32), "HF": ("sbuf", [128, 16], F32), "HL": ("sbuf", [128, 24], U16),
    "TH": ("sbuf", [128, 4], F32), "NTH": ("sbuf", [128, 4], F32),
    "PI": ("sbuf", [128, 4], I32), "PC": ("sbuf", [128, 4], F32),
    "PM": ("sbuf", [128, 128], F32), "J": ("sbuf", [128, 128], F32), "MH": ("sbuf", [128, 128], F32), "ML": ("sbuf", [128, 128], F32),
    "IDF": ("sbuf", [128, 128], F32), "NIDF": ("sbuf", [128, 128], F32), "IDB": ("sbuf", [128, 128], BF), "NIDB": ("sbuf", [128, 128], BF),
    "IDS": ("sbuf", [128, 128], BF), "SHF": ("sbuf", [128, 128], F32), "SHB": ("sbuf", [128, 128], BF),
    "ONB": ("sbuf", [128, 128], BF), "ONF": ("sbuf", [128, 128], F32), "TRM": ("sbuf", [128, 128], BF),
    "TMP": ("sbuf", [128, 512], F32), "SC": ("sbuf", [128, 16], F32),
    "SEL": ("sbuf", [128, 2048], BF), "BC": ("sbuf", [128, 2048], BF),
    "DG": ("sbuf", [128, 128], F32), "RS": ("sbuf", [128, 128], F32), "JK": ("sbuf", [128, 128], BF),
    "J4": ("sbuf", [128, 256], F32), "J4B": ("sbuf", [128, 256], BF), "ZB": ("sbuf", [128, 128], BF),
    "VC": ("sbuf", [128, 192], F32), "CC": ("sbuf", [128, 16], F32),
    "IX": ("sbuf", [128, 1536], U16), "LV": ("sbuf", [128, 384], U16), "LA": ("sbuf", [128, 128], F32), "LM": ("sbuf", [128, 128], F32),
    "NM2": ("sbuf", [128, 384], F32), "NMU": ("sbuf", [128, 384], U16), "OWN": ("sbuf", [128, 384], F32),
    "E": ("sbuf", [128, 2048], BF), "XF": ("sbuf", [128, 256], F32), "XU": ("sbuf", [128, 256], U16),
    "FIT": ("sbuf", [128, 256], BF), "FF": ("sbuf", [128, 256], F32), "CL": ("sbuf", [128, 256], F32),
    "VB": ("sbuf", [128, 256], BF), "MM": ("sbuf", [128, 128], F32), "MV": ("sbuf", [128, 256], F32),
    "AS": ("sbuf", [128, 128], BF), "KEY": ("sbuf", [128, 136], F32), "KD": ("sbuf", [128, 128], F32), "KS": ("sbuf", [128, 128], F32),
    "AB": ("sbuf", [128, 1088], F32), "SM": ("sbuf", [128, 96], F32), "LU": ("sbuf", [128, 24], U16),
}
POOLS = {"P": (8, "psum", 512, F32), "X": (4, "sbuf", 1024, F32), "Y": (2, "sbuf", 2048, F32), "H": (4, "sbuf", 2048, BF),
         "D": (4, "sbuf", 2048, F32), "B": (5, "sbuf", 384, F32)}
SCRATCH["Q"] = ("sbuf", [128, 2, 128, 16], F32)
for _p, (_k, _w, _c, _d) in POOLS.items():
    for _b in range(_k):
        SCRATCH["%s%d" % (_p, _b)] = (_w, [128, 4, 16, 8] if _p == "P" else [128, _c], _d)
PRE, POST = (0.015625, 0.015625, 1.0), (1.0, 1.0, 0.015625)

SEMAPHORES = (["ev", "ea", "et", "eg", "rl"] + ["d%d" % i for i in range(110)] + ["arr%d" % i for i in range(9)] + ["rin%d" % i for i in range(9)])
ESEM = {"v": "ev", "a": "ea", "t": "et", "g": "eg"}

M = {"cy": 1.0, "fv": 33, "fa": 33, "pe": 0.6, "ga": 1.56, "sc": 3.8, "lx": 170.0, "ls": 100.0, "comm": 1.2,
     "gi": 1000, "dl": 2000, "dr": 130, "ar": 200, "fm": 0}
S = {'slack': 30.0, 'boost': 10000, 'look': 200, 'tol': 300, 'far': 1000, 'th': 1500, 'res': 0, 'far2': 8000, 'frac': 0.2, 'tn': -10000, 'uo': 1500,
     'so': 1500, 'cn': 5, 'cs': 3, 'tn2': -10000, 'vg': 9999, 'hop': 6, 'iters': 24000, 'temp': 50, 'seed': 2}
MODELS = [{"w": 0.4, "cy": 0.87, "pe": 0.47, "ar": 220, "lx": 170, "ls": 100},
          {"w": 0.27, "cy": 1.22, "pe": 0.79, "ga": 1.9, "sc": 5.0, "comm": 1.2, "ar": 200, "lx": 150, "ls": 90, "fv": 40, "fa": 40},
          {"w": 0.33, "cy": 1.05, "pe": 0.64, "ga": 1.2, "sc": 2.5, "comm": 1.3, "ar": 155, "gi": 1300, "dl": 2800, "lx": 220, "ls": 120}]


def price(k, m):
    cy = m["cy"]
    if k[0] == "ns":
        return k[1], k[2], 500.0
    if k[0] == "comm":
        return 0.0, k[1] * m["comm"] - 2500, 0.0
    if k[0] == "dma":
        return (m["gi"] if k[1] == "g" else 70) * k[2], m["dl"] + k[3] / m["dr"] + k[4] * 3, (k[3] / m["ar"] if k[4] == 512 else 0.0)
    if k[0] == "acc":
        return m["gi"], m["dl"] + k[1] / m["ar"], k[1] / m["ar"]
    c = {"v": m["fv"] + cy * max(64, k[1]), "a": m["fa"] + cy * max(64, k[1]), "vg": 50 + m["ga"] * cy * k[1], "ag": 65 + m["ga"] * cy * k[1],
         "vs": 50 + m["sc"] * cy * k[1], "t": m["pe"] * k[1] + m["fm"] * k[-1], "g": 130 + 2 * cy * k[1]}[k[0]]
    return c, c, 0.0


def R(name, lo, hi, step=1):
    return (name, lo, hi, step)


def IND(win, off):
    return ("#ind", win, off)


def _n(r):
    if r[0] == "#ind":
        return 16 * _n(r[2])
    if len(r) > 4:
        return 256 if r[0][0] == "Q" else 32
    return (r[2] - r[1] + r[3] - 1) // r[3]


def _kind(name):
    if name[0] == "Q":
        return SCRATCH["D0"]
    return SCRATCH[name.split("#")[0] + "0" if "#" in name else name]


def _psum(r):
    return r[0] != "#ind" and _kind(r[0])[0] == "psum"


def _two(r):
    return _kind(r[0])[2] in (BF, U16)


def _flat(rs):
    out = []
    for r in rs:
        if isinstance(r, tuple):
            out += [r[1], r[2]] if r[0] == "#ind" else [r]
    return out


def build():
    ops = []
    nsem = [0]
    up = [0.0]
    ntile = [0]
    now = [3]

    def tile(pool, kind=""):
        ntile[0] += 1
        return "%s#%d%s" % (pool, ntile[0], kind)

    def add(eng, fn, wr, rd, cost, sem=None, after=(), hold=()):
        w, r = [], _flat(rd)
        for o in wr:
            if o[0] == "#ind":
                w.append(o[1]); r.append(o[2])
            else:
                w.append(o)
        tiles = sorted(set([x[0] for x in w + r if "#" in x[0]] + list(hold)))
        ops.append({"e": eng, "fn": fn, "w": w, "r": r, "k": cost, "sem": sem, "after": list(after), "up": up[0], "t": now[0], "tiles": tiles})
        return len(ops) - 1

    def vcost(out, a, b=None):
        if out[0] == "#ind":
            return ("vs", _n(out))
        if a[0] == "#ind":
            return ("vg", _n(a))
        n = _n(out)
        if b is not None:
            n = n if (_psum(a) or _psum(b)) else 2 * n
        elif _two(out) and _two(a):
            n = n / 2
        return ("v", n)

    def tt(out, a, b, op):
        return add("v", lambda q, A: q.tensor_tensor(A(out), A(a), A(b), op), [out], [a, b], vcost(out, a, b))

    def ts(out, a, s1, op0, s2=None, op1=None):
        if op1 is None:
            fn = lambda q, A: q.tensor_scalar(A(out), A(a), A(s1), None, op0)
        else:
            fn = lambda q, A: q.tensor_scalar(A(out), A(a), A(s1), A(s2), op0, op1)
        return add("v", fn, [out], [a, s1, s2], vcost(out, a))

    def cp(out, a):
        return add("v", lambda q, A: q.tensor_copy(A(out), A(a)), [out], [a], vcost(out, a))

    def fill(out, x):
        return add("v", lambda q, A: q.memset(A(out), x), [out], [], ("v", _n(out) / (2 if _two(out) else 1)))

    def acost(a):
        return ("ag", _n(a)) if a[0] == "#ind" else ("a", _n(a))

    def act(out, a, f, bias=0.0, scale=1.0):
        return add("a", lambda q, A: q.activation(A(out), A(a), f, bias=A(bias), scale=A(scale)), [out], [a, bias, scale], acost(a))

    def move(out, a, scale=None, hold=()):
        fa = lambda q, A: q.activation(A(out), A(a), AF.Identity, bias=0.0, scale=A(1.0 if scale is None else scale))
        if scale is None:
            fv = lambda q, A: q.tensor_copy(A(out), A(a))
        else:
            fv = lambda q, A: q.tensor_scalar(A(out), A(a), A(scale), None, AL.mult)
        return add("f", {"a": fa, "v": fv}, [out], [a, scale], {"a": acost(a), "v": vcost(out, a)}, hold=hold)

    def mm(items):
        def fn(q, A):
            for o, l, r, st, sp in items:
                ins = q.matmul(A(o), A(l), A(r), st, sp)
            return ins
        c = ("t", sum(max(64, _n(r)) * (1 if _two(r) else 4) for o, l, r, st, sp in items), len(items))
        return add("t", fn, [i[0] for i in items], [i[1] for i in items] + [i[2] for i in items], c)

    def group(parts):
        return [(o, l, r, i == 0, i == len(parts) - 1) for i, (o, l, r) in enumerate(parts)]

    def iota(out, pattern, base, cm):
        if SCRATCH[out[0]][2] == I32:
            fn = lambda q, A: q.iota(A(out), pattern, base, cm)
        else:
            fn = lambda q, A: q.iota(A(out), pattern, base, cm, allow_small_or_imprecise_dtypes=True)
        return add("g", fn, [out], [], ("g", _n(out)))

    def select(out, a, pattern, base, cm):
        return add("g", lambda q, A: q.affine_select(A(out), A(a), pattern, AL.is_equal, 0.0, base, cm), [out], [a], ("g", _n(out) + 24))

    def dma(eng, pairs, wr, rd, nbytes, after=(), rows=128):
        s = "d%d" % nsem[0]; nsem[0] += 1
        def fn(q, A):
            for o, i in pairs:
                q.dma_start(o(A), i(A)).then_inc(A(("#sem", s)), 16)
        return add(eng, fn, wr, rd, ("dma", eng, len(pairs), nbytes, rows), (s, 16 * len(pairs)), after)

    def acc(D, lo, hi, far, other=None):
        s = "d%d" % nsem[0]; nsem[0] += 1
        name = D[0] if len(D) == 1 else "QQ"
        out, a = R(name, lo, hi), R(other or name, lo + far, hi + far)
        fn = lambda q, A: q.dma_start(A(out), A(a), accum_op=AL.add).then_inc(A(("#sem", s)), 16)
        w = [R(x, lo, hi) for x in D]
        return add("g", fn, w, w + [R(other or x, lo + far, hi + far) for x in D], ("acc", 512 * (hi - lo) * len(D), 128 * len(D)), (s, 16))

    def load(eng, out, name, nbytes, after=()):
        return dma(eng, [(lambda A: A(out), lambda A: A(("#hbm", name))[:])], [out], [], nbytes, after)

    def send(m, srcs, dsts, lat):
        s = "d%d" % nsem[0]; nsem[0] += 1
        i = add("g", ("send", m, srcs, dsts, s), [], srcs, ("ns", 700, 2500), (s, "#sent"))
        add("x", None, dsts, [], ("comm", lat), ("arr%d" % m, "#arr"), [i])
        return i

    P = lambda b, lo=0, hi=512, st=1: R(b, lo, hi, st)
    byname = lambda b, k: (b, 0, 512, 1, k)
    whole = lambda n: R(n, 0, _kind(n)[1][1])
    col = lambda n, j: R(n, j, j + 1)
    blk = lambda n, i: R(n, 128 * i, 128 * i + 128)
    idf, idb = whole("IDF"), whole("IDB")
    BOOST = S["boost"]

    up[0] = 50000.0
    load("s", R("SBI", 0, 64), "sd", 32768)
    load("s", R("SBI", 64, 128), "nr", 32768)
    dma("a", [(lambda A: A(R("UB", OU, OU + 256)), lambda A: A(("#hbm", "u0"))[:, 0:256])], [R("UB", OU, OU + 256)], [], 65536)
    load("a", R("UB", OW, OE), "w0", 196608)
    up[0] = 45000.0
    i = load("s", whole("TL"), "tl", 780000)
    up[0] = 40000.0
    dma("s", [(lambda A: A(R("UB", OU + 256, OH)), lambda A: A(("#hbm", "u0"))[:, 256:1024])], [R("UB", OU + 256, OH)], [], 980000, [i])
    up[0] = 0.0
    load("s", col("TH", 0), "th", 512)
    dma("s", [(lambda A, c=c: A(R("HI", 2 * c, 2 * c + 2)), lambda A, c=c: A(("#hbm", "hs"))[:, 32 * c:32 * c + 32]) for c in range(8)],
        [whole("HI")], [], 500000, rows=1024)

    iota(col("PI", 0), [[0, 1]], 0, 1)
    iota(whole("MH"), [[1, 8], [0, 16]], 0, 0)
    iota(whole("J"), [[1, 128]], 0, 0)
    iota(whole("PM"), [[1, 128]], 0, -1)
    iota(whole("ML"), [[0, 8], [1, 16]], 0, 0)
    ts(col("PI", 1), col("PI", 0), 15, AL.bitwise_and)
    ts(col("PI", 2), col("PI", 0), 4, AL.arith_shift_right)
    cp(R("PC", 1, 3), R("PI", 1, 3))
    lane, grp = col("PC", 1), col("PC", 2)
    ts(whole("ONB"), whole("MH"), grp, AL.is_equal)
    ts(whole("SC"), R("J", 0, 16), lane, AL.is_equal)
    ts(idb, whole("PM"), 0.0, AL.is_equal)
    for i in range(16):
        move(blk("BC", i), whole("ONB"), col("SC", i))
        move(blk("SEL", i), idb, col("SC", i))
    ts(R("VC", 0, 64), R("J", 0, 64), 16.0, AL.mult, lane, AL.add)
    ts(R("VC", 64, 128), R("VC", 0, 64), float(OU), AL.add)
    ts(R("VC", 128, 192), R("VC", 0, 64), OU - 2049.0, AL.add)
    ts(blk("TMP", 0), whole("PM"), -16.0, AL.is_equal)
    ts(blk("TMP", 1), whole("PM"), 112.0, AL.is_equal)
    tt(whole("SHB"), blk("TMP", 0), blk("TMP", 1), AL.add)
    move(whole("SHF"), whole("SHB"))
    move(idf, idb)
    move(whole("NIDB"), idb, -1.0)
    move(whole("NIDF"), idb, -1.0)
    move(whole("IDS"), idb, 1.0 / 2048)
    move(whole("ONF"), whole("ONB"))
    ts(blk("TMP", 2), whole("PM"), 0.0, AL.is_gt, -8192.0, AL.mult)
    ts(blk("TMP", 3), whole("PM"), 0.0, AL.is_ge, 4096.0, AL.mult)
    tt(blk("TMP", 2), blk("TMP", 2), blk("TMP", 3), AL.add)
    tt(whole("TRM"), blk("TMP", 2), whole("ONB"), AL.mult)
    ts(whole("DG"), whole("ML"), lane, AL.is_equal)
    ts(whole("RS"), whole("ML"), 0.0, AL.not_equal)
    move(whole("JK"), whole("J"), 1.0 / 256)
    for par in (0, 1):
        ts(blk("J4", par), whole("J"), 4.0, AL.mult, 2.0 * par, AL.add)
    move(whole("J4B"), whole("J4"))
    fill(whole("ZB"), 0.0)
    j0 = R("VC", 0, 8)
    ts(R("CC", 0, 8), j0, 1.0 + 1.0 / 256, AL.mult, -127.0, AL.add)
    ts(R("CC", 8, 16), j0, 1.0 / 256, AL.mult, 1.0, AL.add)
    late = [[c for c in (1, 2, 3) if c not in CFG[t]["early"]] for t in range(3)]
    for t in range(3):
        if late[t]:
            fill(R("SN", OK_[t] + 256 * min(late[t]) + t % 2, OK_[t] + 256 * max(late[t]) + 256, 2), POST[t])
    ts(col("NTH", 0), col("TH", 0), -1.0, AL.mult)
    for name in ("UB", "UW"):
        fill(R(name, OE, OU), 0.0)
    fill(col("KEY", 7), -0.002)
    fill(col("NTH", 1), -2047.0)
    fill(col("NTH", 2), 0.25)

    ts(R("SBB", 0, 64), R("SBI", 0, 64), 2048.0, AL.mult)
    ts(R("SBB", 64, 128), R("SBI", 64, 128), 2.0, AL.mult)

    def spread(src, dst, i0, i1):
        b = tile("P")
        mm([(P(b, 64 * (i - i0), 64 * (i - i0) + 64), blk("BC", i), R("SBB", src, src + 64), True, True) for i in range(i0, i1)])
        move(R("SN", dst + 64 * i0, dst + 64 * i1), P(b, 0, 64 * (i1 - i0)))

    def lists(t, c0, c1):
        n = c1 - c0
        b = tile("P")
        mm(group([(P(b, 64, 64 + n), blk("SEL", i), R("SN", OS + 16 * c0 + i, OS + 16 * c1, 16)) for i in range(16)]))
        mm(group([(P(b, 0, n), blk("SEL", i), R("SN", ON + 16 * c0 + i, ON + 16 * c1, 16)) for i in range(16)]))
        for z in (0, 1):
            tt(R("LA", 64 * z + c0, 64 * z + c1), R("VC", 64 + 64 * z + c0, 64 + 64 * z + c1), P(b, 64, 64 + n), (AL.subtract, AL.add)[z])
        for z in (0, 1):
            tt(R("LM", 64 * z + c0, 64 * z + c1), P(b, 0, n), R("LA", 64 * z + c0, 64 * z + c1), AL.max)
        for z in (0, 1):
            o = 128 * t + 64 * z
            ts(R("LV", o + c0, o + c1), R("LM", 64 * z + c0, 64 * z + c1), float(z), AL.add)

    def views(t, c):
        win = R("UB" if t == 0 else "UW", 0, OU + 256 * c + 256)
        for z in (0, 1):
            o = 128 * t + 64 * z + 16 * c
            move(R("VW%d" % t, 512 * c + z, 512 * c + 512, 2), IND(win, R("LV", o, o + 16)))

    def send_sides(t):
        b = tile("P")
        mm([(P(b, 0, 128), whole("SHB"), R("SN", OS + 128, OS + 256), True, True)])
        move(blk("SS", t), P(b, 0, 128))
        name, o = ("SN", OG) if t == 0 else ("SG", 256 * (t - 1))
        return send(3 * t, [R("SN", OS, OS + 128), blk("SS", t)], [R(name, o, o + 128), R(name, o + 128, o + 256)], 5000)

    def send_own(t):
        b = tile("P")
        u, so, land, o = (("UB", whole("SO0"), "UB", OH), ("UW", blk("SO", 0), "UW", OH), ("UW", blk("SO", 1), "GO", 0))[t]
        mm([(P(b, 0, 128), whole("SHB" if t == 0 else "SHF"), R(u, OU + 128, OU + 256), True, True)])
        move(so, P(b, 0, 128))
        return send(3 * t + 1, [R(u, OU, OU + 128), so], [R(land, o, o + 128), R(land, o + 128, o + 256)], 5000 if t == 0 else 6000)

    def send_views(t):
        vw, sv = "VW%d" % t, "SV%d" % t
        b = tile("P")
        mm([(P(b, 0, 256), whole("SHB" if t == 0 else "SHF"), R(vw, 256, 512), True, True)])
        move(whole(sv), P(b, 0, 256))
        return send(3 * t + 2, [R(vw, 0, 256), whole(sv)], [R(vw, 2048, 2304), R(vw, 2304, 2560)], 6000 if t == 0 else 8000)

    def node_lists(t):
        par = t % 2
        b = tile("P")
        if t == 0:
            mm(group([(P(b), idf, R("TL2", par, 1024, 2)), (P(b), whole("IDS"), R("SN", OS + par, OS + 1024, 2))]))
        else:
            b2, sl = tile("P"), R("SL", 32 * par, 32 * par + 32)
            mm(group([(P(b2, 0, 32), blk("SEL", i), R("SN", OS + par + 2 * i, OS + 1024, 32)) for i in range(16)]))
            move(sl, P(b2, 0, 32))
            mm(group([(P(b), idf, R("TT", 512 * par, 512 * par + 512))] + [(byname(b, k), whole("IDS"), sl) for k in range(16)]))
        cp(R("IX", 512 * t, 512 * t + 512), P(b))

    def turned_names(par, gate):
        y = "VW2"
        if par:
            add("v", lambda q, A: q.transpose(A(R(y, 0, 1024)), A(whole("TL2"))), [R(y, 0, 1024)], [whole("TL2")], ("v", 1024))
            ops[iota(blk("LT", 6), [[0, 128]], 1, 0)]["after"].append(last)
            for p in (1, 0):
                select(blk("LT", 4 + p), blk("LT", 6), [[-32, 4], [0, 2], [-2, 16]], -p, 1)
                for a in (0, 1):
                    select(blk("LT", 2 * p + a), blk("LT", 4 + p), [[0, 4], [1, 2], [0, 16]], -a, 0)
        b = tile("P")
        for k0 in range(0, 16, 2):
            i = mm([x for k in (k0, k0 + 1) for x in group([(byname(b, k), blk("LT", 2 * par + a), R(y, 16 * a + k, 1024, 32)) for a in (0, 1)])])
            ops[i]["after"] += gate
        move(R("TT", 512 * par, 512 * par + 512), P(b))

    def copies(t):
        name, src = "U%d" % t, R("UW", OU + t % 2, OH, 2)
        part = lambda lo, hi: [R(name, 512 * c + lo, 512 * c + hi) for c in range(4)]
        add("a", lambda q, A: q.activation(A(("#all", name, 0, 128)), A(src), AF.Identity, bias=0.0, scale=-1.0), part(0, 128), [src], ("a", 512))
        for w in (128, 256):
            dma("s", [(lambda A, w=w: A(("#all", name, w, 2 * w)), lambda A, w=w: A(("#all", name, 0, w)))], part(w, 2 * w), part(0, w), 2048 * w, rows=512)

    def names(t):
        par = t % 2
        cp(R("HL", 8 * t, 8 * t + 8), R("HF", par, 16, 2))
        move(blk("NM2", t), IND(whole("TL2"), R("HL", 8 * t, 8 * t + 8)))
        ts(blk("NMU", t), blk("NM2", t), 0.5, AL.mult)
        ts(blk("OWN", t), blk("NM2", t), 2048.0, AL.is_lt, -1.0, AL.mult)

    spread(0, OS, 0, 4)
    spread(64, ON, 0, 4)
    send_sides(0)
    send_own(0)
    lists(0, 0, 16)
    views(0, 0)
    last = send_views(0)
    spread(0, OS, 4, 12)
    spread(64, ON, 4, 12)
    spread(0, OS, 12, 16)
    spread(64, ON, 12, 16)
    lists(0, 16, 64)
    for c in (1, 2, 3):
        views(0, c)
    move(R("TL2", 0, 1024), whole("TL"), 2.0) if False else ts(R("TL2", 0, 1024), whole("TL"), 2.0, AL.mult)
    cp(whole("HF"), whole("HI"))
    names(0)
    node_lists(0)
    load("g", R("UW", OW, OE), "w0", 262144, [last])
    load("g", R("UW", OU, OH), "u0", 524288, [last])
    names(1)
    up[0] = S["tn"]
    turned_names(1, [])

    def tree_a(D, b, u, long):
        lo = 128 if long > 0 else 0
        if long >= 0:
            mm([(P(b, lo, 512), idf, R(D, 512 * u + lo, 512 * u + 512), u == 0, False)])
        elif u == 2:
            tt(P(b), P(b), R(D, 1024, 1536), AL.add)

    VA = (-1, 0, 1, 2, 21)

    def levels(D, long, u, split):
        if u == 2 and (split or long == 21):
            acc(D, 0, 512, 1024)
        if u == 3 and long != 21:
            acc(D, 512, 1024, 1024) if split else acc(D, 0, 1024, 1024)
            for lv in range(1, long - 10):
                acc(D, 0, 1024 >> lv, 1024 >> lv)

    def tree(D, b, dst, keep, long, scale, c1, gate=()):
        B = tile("B")
        tb = lambda lo, hi: R(B, lo, hi)
        if long > 10:
            b = tile("P")

            def third(parts):
                if c1 == "a":
                    mm(group([(P(b, 128, 256), idf, x) for x in parts + [tb(128, 256)]]))
                    move(tb(256, 384), P(b, 128, 256))
                else:
                    mm(group([(P(b, 128, 256), idf, x) for x in parts]))
                    tt(tb(256, 384), P(b, 128, 256), tb(128, 256), AL.add)
            if long == 21:
                mm(group([(P(b, 256, 512), idf, R(D, 256, 512)), (P(b, 256, 512), idf, R(D, 1792, 2048))]))
                move(tb(0, 256), P(b, 256, 512))
                third([blk(D, 1), blk(D, 13)])
                fin = [blk(D, 0), blk(D, 12), tb(0, 128), tb(256, 384)]
            elif long == 11:
                mm(group([(P(b, 256, 512), idf, R(D, 256, 512)), (P(b, 256, 512), idf, R(D, 768, 1024))]))
                move(tb(0, 256), P(b, 256, 512))
                third([blk(D, 1), blk(D, 5)])
                fin = [blk(D, 0), blk(D, 4), tb(0, 128), tb(256, 384)]
            elif long == 12:
                mm(group([(P(b, 128, 256), idf, blk(D, 1)), (P(b, 128, 256), idf, blk(D, 3))]))
                move(tb(0, 128), P(b, 128, 256))
                fin = [blk(D, 0), blk(D, 2), tb(0, 128)]
            else:
                fin = [blk(D, 0), blk(D, 1)]
            if gate and long != 13:
                b = tile("P")
            i = mm(group([(P(b, 0, 128), idf, x) for x in fin]))
            ops[i]["after"] += list(gate)
        else:
            lo = 128 if long > 0 else 0
            hi = 512 if long == 2 else 256
            if long >= 0:
                mm([(P(b, lo, hi), idf, R(D, 1536 + lo, 1536 + hi), False, True)])
            else:
                tt(P(b, 0, 256), P(b, 0, 256), R(D, 1536, 1792), AL.add)
            if long == 2:
                move(tb(0, 256), P(b, 256, 512))
            else:
                tt(tb(0, 256), P(b, 256, 512), R(D, 1792, 2048), AL.add)
            tt(tb(256, 384), P(b, 128, 256), tb(128, 256), AL.add)
            if long > 0:
                if gate:
                    b = tile("P")
                i = mm(group([(P(b, 0, 128), idf, x) for x in (blk(D, 0), blk(D, 8), blk(D, 12), tb(0, 128), tb(256, 384))]))
                ops[i]["after"] += list(gate)
            else:
                tt(P(b, 0, 128), P(b, 0, 128), tb(0, 128), AL.add)
                tt(P(b, 0, 128), P(b, 0, 128), tb(256, 384), AL.add)
        if keep is None and abs(scale) == 1.0:
            tt(dst, dst, P(b, 0, 128), AL.add if scale > 0 else AL.subtract)
            return
        if keep is None:
            move(P(b, 128, 256), P(b, 0, 128), scale)
        else:
            tt(P(b, 128, 256), P(b, 0, 128), keep, AL.mult)
        tt(dst, P(b, 128, 256), dst, AL.add)

    def nodes(t, c):
        par = t % 2
        D = tile("D")
        vw, o = whole("VW%d" % t), 512 * t + 128 * c
        mode = CFG[t]["sub"][c]
        xu = {}
        if t == 0:
            X = tile("H")
            for h in (0, 1):
                move(R(X, 1024 * h, 1024 * h + 1024), IND(vw, R("IX", o + 64 * h, o + 64 * h + 64)), hold=[D])
        else:
            u = 0
            while u < 4:
                if mode[u] == "f":
                    u += 1
                    continue
                w = 2 if u < 3 and mode[u + 1] != "f" and (mode[u] == "d") == (mode[u + 1] == "d") and c >= CFG[t]["one"] else 1
                X, x0 = (D, 512 * u) if mode[u] == "d" else (tile("X"), 0)
                i = move(R(X, x0, x0 + 512 * w), IND(vw, R("IX", o + 32 * u, o + 32 * (u + w))), hold=[D])
                for j in range(w):
                    xu[u + j] = R(X, x0 + 512 * j, x0 + 512 * j + 512)
                u += w
        long = CFG[t]["tree"][c]
        old = R("U%d" % t, 512 * c, 512 * c + 512)
        if "v" in mode:
            pu = tile("P")
            j = mm([(P(pu), idf, old, True, True)])
            ops[j]["after"].append(i)
        sb = tile("P") if long < 10 else None
        for u in (0, 2, 1, 3):
            up[0] = CFG[t]["up"][c] + S["uo"] * (3, 1, 2, 0)[u]
            stay = long in VA and (u == 1 or (u == 0 and long < 0))
            b = sb if (u == 0 and long < 0) else tile("P", "n")
            du = R(D, 512 * u, 512 * u + 512)
            if t == 0:
                un = R("UB", OU + 256 * c, OU + 256 * c + 256, 2)
                mm([x for kk in range(4) for x in group([(P(b, 128 * kk, 128 * kk + 128), idb, R(X, 4 * u + kk, 2048, 16)),
                                                         (P(b, 128 * kk, 128 * kk + 128), whole("NIDB"), un)])])
            elif mode[u] == "p":
                for x in range(0, 512, 128):
                    mm(group([(P(b, x, x + 128), idf, R(xu[u][0], xu[u][1] + x, xu[u][1] + x + 128)),
                              (P(b, x, x + 128), idf, R(old[0], old[1], old[1] + 128))]))
            elif mode[u] == "v":
                tt(du, xu[u], P(pu), AL.add)
            elif mode[u] == "d":
                acc([D], 512 * u, 512 * u + 512, 512 * (c - u), old[0])
            else:
                tt(du, IND(vw, R("IX", o + 32 * u, o + 32 * u + 32)), old, AL.add)
            if mode[u] == "p":
                up[0] += CFG[t]["rel"]
                act(du, P(b), AF.Abs, 0.0, PRE[t])
            else:
                act(P(b), du, AF.Abs, 0.0, PRE[t])
            tt(P(b) if stay else du, P(b), du, AL.mult)
            up[0] = CFG[t]["up"][c]
            if long > 10:
                levels([D], long, u, CFG[t]["split"])
            if long not in VA:
                continue
            if u == 1:
                b1 = b
            elif u == 3:
                tt(du, P(b1), du, AL.add)
            elif long < 10:
                tree_a(D, sb, u, long)
        return D, sb

    def nodes_end(t, c, D, gate):
        par = t % 2
        keep = R("SN", OK_[t] + 256 * c + par, OK_[t] + 256 * c + 256, 2) if c in late[t] else None
        tree(D[0], D[1], R("UW", OU + 256 * c + par, OU + 256 * c + 256, 2), keep, CFG[t]["tree"][c], POST[t], CFG[t]["c1"], gate)

    def shock_front(t):
        par = t % 2
        if t > 0:
            move(R("SN", OG, OG + 256), R("SG", 256 * (t - 1), 256 * t))
        for h in (0, 1):
            o = 128 * t + 64 * h
            move(R("E", 1024 * h, 1024 * h + 1024), IND(R("SN", OS, OS + 1280), R("NMU", o, o + 64)), -1.0 / 2048)
        w = 128 // CFG[t]["eh"]
        for x in range(0, 128, w):
            e = P(tile("P"), 0, w)
            part = lambda name, o: R(name, o + x, o + x + w)
            up[0] = CFG[t]["up"][4] + BOOST
            mm(group([(e, blk("SEL", k), R("E", 16 * x + k, 16 * (x + w), 16)) for k in range(16)]))
            tt(part("XF", 128), part("J4", 128 * par), e, AL.subtract)
            cp(part("XU", 128), part("XF", 128))
            up[0] = CFG[t]["up"][5]
            tt(part("FIT", 0), part("OWN", 128 * t), e, AL.mult)
            tt(part("FIT", 128), part("OWN", 128 * t), e, AL.is_lt)
        b = tile("P")
        mm(group([(P(b, 0, 256), whole("TRM"), whole("FIT")), (P(b, 0, 128), idf, blk("NM2", t)), (P(b, 128, 256), idf, blk("NM2", t))]))
        act(whole("FF"), P(b, 0, 256), AF.Relu, col("NTH", 1), 0.5)
        mm(group([(P(b, 256, 512), whole("ONF"), whole("FF")), (P(b, 256, 384), idb, whole("JK")), (P(b, 384, 512), idb, whole("JK"))]))
        move(whole("CL"), P(b, 256, 512))

    def shock_main(t):
        par = t % 2
        cf = CFG[t]
        pool = "H" if t == 0 and cf["xs"] else "Y"
        xs, us, Q = tile(pool), tile(pool), ["Q0", "Q1"]
        u_ = "UB" if t == 0 else "UW"
        up[0] = cf["up"][4]
        if t == 2:
            move(R("UW", OH, OH + 256), whole("GO"))
        own = [IND(R(u_, OU, OH + 256), R("NMU", 128 * t + 64 * h, 128 * t + 64 * h + 64)) for h in (0, 1)]
        cols = [IND(R(u_, OW, OE), R("XU", 128 + 64 * h, 192 + 64 * h)) for h in (0, 1)]
        for h in (0, 1):
            up[0] = cf["up"][4] + 2 * S["so"] * (1 - h)
            part = (1024 * h, 1024 * h + 1024)
            if cf["xs"] == 3:
                move(R(us, *part), cols[h], -1.0, hold=[xs])
                add("v", lambda q, A, h=h, part=part: q.tensor_tensor(A(R(xs, *part)), A(own[h]), A(R(us, *part)), AL.add),
                    [R(xs, *part)], [own[h], R(us, *part)], ("vg", 1024))
                continue
            move(R(us, *part), own[h], -1.0 if cf["xs"] == 2 else None, hold=[xs])
            if cf["xs"]:
                move(R(xs, *part), cols[h])
                if cf["xs"] == 2:
                    acc([xs], part[0], part[1], 0, us)
            else:
                tt(R(xs, *part), cols[h], R(us, *part), AL.subtract)
        pos, neg = ("IDB", "NIDB") if t == 0 else ("IDF", "NIDF")
        for u in range(4):
            up[0] = cf["up"][4] + S["so"] * (3 - u)
            b = tile("P", "s")
            part = (512 * u, 512 * u + 512)
            q0, q1 = R(Q[0], *part), R(Q[1], *part)
            if cf["xs"] == 1:
                for x in range(0, 512, 512 if t == 0 else 128):
                    w = (part[0] + x, part[0] + x + (512 if t == 0 else 128))
                    o = P(b, x, x + w[1] - w[0])
                    mm(group([(o, whole(pos), R(xs, *w)), (o, whole(neg), R(us, *w))]))
                act(q0, P(b), AF.Abs, 0.0, PRE[t])
                tt(q0 if cf["q0"] else P(b), P(b), q0, AL.mult)
            else:
                act(P(b), R(xs, *part), AF.Abs, 0.0, PRE[t])
                tt(q0 if cf["q0"] else P(b), P(b), R(xs, *part), AL.mult)
            if cf["q0"]:
                b = tile("P")
                mm([(P(b), idb, R("E", *part), True, True)])
                tt(q1, P(b), q0, AL.mult)
                if u % 2:
                    acc([Q[0]], part[0] - 512, part[1], 0, Q[1])
            else:
                tt(q1, P(b), R("E", *part), AL.mult)
                tt(q0, P(b), q1, AL.add)
            if u % 2:
                for z in (1, 0):
                    shock_tree(t, u // 2, z)
        up[0] = 0.0

    def shock_tree(t, h, z):
        lo, hi = 1024 * h, 1024 * h + 1024
        q = lambda k: R("Q%d" % z, lo + k, hi, 16)
        four = lambda k: ("Q%d" % z, lo, hi, 1, k)
        b, B = tile("P"), tile("B")
        if CFG[t]["a4"][h] == "v":
            tt(four(4), four(4), four(12), AL.add)
        else:
            mm(group([(P(b, 256, 512), idf, four(4)), (P(b, 256, 512), idf, four(12))]))
            move(four(4), P(b, 256, 512))
        mm([x for k in (2, 3) for x in group([(P(b, 64 * k, 64 * k + 64), idf, q(j)) for j in (k, k + 8, k + 4)])])
        move(R(B, 0, 128), P(b, 128, 256))
        if CFG[t]["c1"] == "a":
            mm(group([(P(b, 64, 128), idf, x) for x in (q(1), q(9), q(5), R(B, 64, 128))]))
            move(R(B, 128, 192), P(b, 64, 128))
        else:
            mm(group([(P(b, 64, 128), idf, x) for x in (q(1), q(9), q(5))]))
            tt(R(B, 128, 192), P(b, 64, 128), R(B, 64, 128), AL.add)
        mm(group([(P(b, 0, 64), idf, x) for x in (q(0), q(8), q(4), R(B, 0, 64), R(B, 128, 192))]))
        dst = R("UW", OW + 256 * h + 2 * (t % 2) + z, OW + 256 * h + 256, 4)
        plus = z ^ (CFG[t]["xs"] == 3)
        if POST[t] == 1.0:
            tt(dst, dst, P(b, 0, 64), (AL.subtract, AL.add)[plus])
        else:
            move(P(b, 64, 128), P(b, 0, 64), (-POST[t], POST[t])[plus])
            tt(dst, P(b, 64, 128), dst, AL.add)

    def claims(t):
        par = t % 2
        w = [R("UW", OW + 2 * par + z, OE, 4) for z in (0, 1)]
        b = tile("P")
        mm(group([(P(b, 0, 128), idf, w[0]), (P(b, 0, 128), whole("NIDF"), w[1])]))
        ts(blk("VB", 0), P(b, 0, 128), col("TH", 0), AL.is_gt)
        ts(blk("VB", 1), P(b, 0, 128), col("NTH", 0), AL.is_lt)
        mm([(P(b, 0, 256), whole("ONB"), whole("VB"), True, True)])
        ts(P(b, 0, 256), P(b, 0, 256), 9.0, AL.is_ge)
        tt(P(b, 256, 384), P(b, 0, 128), blk("CL", 0), AL.mult)
        tt(whole("MM"), P(b, 128, 256), blk("CL", 1), AL.mult)
        tt(R("KEY", 8, 136), P(b, 256, 384), whole("MM"), AL.add)
        tt(whole("KD"), R("KEY", 8, 136), whole("DG"), AL.mult)
        add("v", lambda q, A: q.tensor_tensor_scan(A(whole("KS")), A(whole("RS")), A(whole("KD")), 0.0, AL.mult, AL.add),
            [whole("KS")], [whole("RS"), whole("KD")], ("v", 128))
        kw = R("KS", 15, 128, 16)
        sm = lambda i: R("SM", 8 * i, 8 * i + 8)
        ts(sm(0), kw, -1.0, AL.mult, 0.25, AL.add)
        for c in range(7, -1, -1):
            a = R("AB", 136 * c, 136 * c + 16 * c + 17)
            act(a, R("KEY", 7, 16 * c + 24), AF.Abs, col("SM", c))
            if CFG[t]["red"] == "a":
                add("a", lambda q, A, a=a, c=c: q.activation(A(a), A(a), AF.Relu, bias=A(col("NTH", 2)), scale=-1.0, accum_out=A(col("SM", 8 + c))),
                    [a, col("SM", 8 + c)], [a, col("NTH", 2)], ("a", 20 + max(64, 16 * c + 16)))
            else:
                add("v", lambda q, A, a=a, c=c: q.tensor_reduce(A(col("SM", 8 + c)), A(a), AxisListType.X, AL.min),
                    [col("SM", 8 + c)], [a], ("v", 16 * c + 16))
        for z in (0, 1):
            tt(blk("MV", z), P(b, 128 * z, 128 * z + 128), w[z], AL.mult)
        move(whole("AS"), P(b, 128, 256), 2048.0) if t < 2 else move(whole("KD"), P(b, 128, 256))
        tt(sm(4), kw, R("CC", 0, 8), AL.subtract)
        if CFG[t]["red"] == "a":
            ts(sm(5), sm(1), 0.001, AL.is_lt)
        else:
            ts(sm(5), sm(1), 0.25, AL.is_ge)
        tt(sm(6), sm(5), sm(4), AL.mult)
        tt(sm(7), sm(6), j0, AL.add)
        lu = R("LU", 8 * t, 8 * t + 8)
        i = cp(lu, sm(7))
        if t < 2:
            cp(IND(R("SN", OS - 128, OS + 1024), lu), whole("AS"))
            cp(IND(R("SN", ON - 128, ON + 1024), lu), blk("J4B", par))
        else:
            tt(IND(R("VW1", 0, 1152), lu), blk("J4", par), whole("KD"), AL.add)
        tt(IND(R("UW", OE, OH), lu), blk("MV", 0), blk("MV", 1), AL.add)
        if late[t]:
            cp(IND(R("SN", OK_[t] - 128, OK_[t] + 1024), lu), whole("ZB"))
        h = R("HF", par, 16, 2)
        tt(sm(8), kw, R("CC", 8, 16), AL.subtract)
        tt(sm(9), sm(8), h, AL.subtract)
        tt(sm(11), sm(5), sm(9), AL.mult)
        tt(h, h, sm(11), AL.add)
        return i

    def store(name, src, lo, hi):
        dma("s", [(lambda A: A(("#hbm", name))[:, lo:hi], lambda A: A(src))], [], [src], 512 * (hi - lo))

    def done(t, c):
        src = R("UW", OU + 256 * c, OU + 256 * c + 256)
        if t < 2:
            views(t + 1, c)
        else:
            store("yu", src, 256 * c, 256 * c + 256)

    for t in range(3):
        now[0] = t
        up[0] = CFG[t]["up"][4] + BOOST
        shock_front(t)
        shock_main(t)
        D = {}
        for c in range(4):
            up[0] = CFG[t]["up"][c]
            D[c] = nodes(t, c)
        for c in CFG[t]["early"]:
            up[0] = CFG[t]["up"][c]
            nodes_end(t, c, D[c], ())
        if t == 2:
            up[0] = CFG[t]["up"][6]
            for x in (0, 512):
                b = tile("P")
                mm(group([(P(b), idb, R("SN", ON + x, ON + x + 512)), (P(b), whole("IDS"), R("SN", OS + x, OS + x + 512))]))
                move(R("VW1", 128 + x, 640 + x), P(b))
        up[0] = CFG[t]["up"][5]
        gate = claims(t)
        if t < 2:
            send_sides(t + 1)
            send_own(t + 1)
            lists(t + 1, 0, 64)
            done(t, 0)
            sent = send_views(t + 1)
            up[0] = CFG[t]["up"][6]
            node_lists(t + 1)
            copies(t + 1)
            if t == 0:
                names(2)
                up[0] = S["tn2"]
                turned_names(0, [sent])
        else:
            store("ys", R("UW", OW, OE), 0, 512)
            done(t, 0)
            dma("a", [(lambda A, c=c: A(("#hbm", "yc"))[c:c + 1, :], lambda A, c=c: A(("#hbm", "VW1"))[16 * c:16 * c + 1, 128:1152]) for c in range(8)],
                [], [R("VW1", 128, 1152)], 32768)
            dma("s", [(lambda A, c=c: A(("#hbm", "yh"))[:, 32 * c:32 * c + 32], lambda A, c=c: A(R("HF", 2 * c, 2 * c + 2))) for c in range(8)],
                [], [whole("HF")], 8192, rows=1024)
        for c in (1, 2, 3):
            up[0] = CFG[t]["up"][c]
            if c in late[t]:
                nodes_end(t, c, D[c], [gate])
            done(t, c)
    return ops


def schedule(ops):
    n = len(ops)
    seen = {}
    users = {}
    for i, o in enumerate(ops):
        o["c"], o["done"], o["dm"] = price(o["k"]["a"] if o["e"] == "f" else o["k"], M)
        deps = set()
        for kind in ("r", "w"):
            for r in o[kind]:
                ps = _psum(r)
                for j, k2, lo, hi, st in seen.get(r[0], ()):
                    if ps and (ops[j]["e"] != o["e"] or o["e"] == "f"):
                        deps.add(j)
                    elif (kind == "w" or k2 == "w") and lo < r[2] and r[1] < hi and (st != r[3] or (lo - r[1]) % st == 0):
                        deps.add(j)
        for kind in ("r", "w"):
            for r in o[kind]:
                seen.setdefault(r[0], []).append((i, kind, r[1], r[2], r[3]))
        o["deps"] = deps
        o["all"] = deps | set(o["after"])
        for x in o["tiles"]:
            users.setdefault(x, []).append(i)
    succ = [[] for _ in range(n)]
    for i, o in enumerate(ops):
        for j in o["all"]:
            succ[j].append(i)

    def lat(ej, j, e):
        if ej == e and ops[j]["sem"] is None:
            return 0.0 if e == "t" else M["ls"]
        return M["lx"]
    prio = [0.0] * n
    for i in range(n - 1, -1, -1):
        prio[i] = ops[i]["done"] + max([prio[k] + lat(ops[i]["e"], i, ops[k]["e"]) for k in succ[i]], default=0.0)
    left = [len(o["all"]) for o in ops]
    ready = [0.0] * n
    cand = {e: [] for e in "vatgsxf"}
    free = {e: 0.0 for e in "vatgsxd"}
    order = {e: [] for e in "vatgsx"}
    for i in range(n):
        if left[i] == 0:
            cand[ops[i]["e"]].append(i)
    end = [0.0] * n
    slot = {p: [None] * POOLS[p][0] for p in POOLS}
    open_ = {x: len(u) for x, u in users.items()}
    till = {x: 0.0 for x in users}
    place = {}
    urge = [(prio[k] + ops[k]["up"], -k) for k in range(n)]
    urge = S.get("urge") or urge
    key = lambda k: urge[k]

    memo = {}
    quota = [c["vg"] for c in CFG] + [S["vg"]]
    busy_ = {"n": 0, "s": 0}

    def slots(p):
        if p not in memo:
            memo[p] = sorted((0.0 if x is None else till[x] + M["lx"], s) for s, x in enumerate(slot[p]) if x is None or open_[x] == 0)
        return memo[p]

    def when(k):
        r = ready[k]
        new = [x for x in ops[k]["tiles"] if x not in place]
        if not new:
            return r
        need = {}
        for x in new:
            need[x[0]] = need.get(x[0], 0) + 1
            if x[-1] in busy_ and busy_[x[-1]] >= S["c" + x[-1]]:
                return None
        for p, m in need.items():
            f = slots(p)
            if len(f) < m + (S["res"] if p == "P" and ops[k]["e"] == "t" and ops[k]["c"] > 800 else 0):
                return None
            r = max(r, f[m - 1][0])
        return r

    def choose(c, t0):
        i = max((k for k in c if c[k] <= t0 + S["look"]), key=key)
        if c[i] > t0 + S["slack"]:
            now = [k for k in c if c[k] <= t0 + S["slack"]]
            short = [k for k in now if ops[k]["c"] <= c[i] - t0 + S["tol"]]
            if short:
                i = max(short, key=key)
            elif key(i)[0] - key(max(now, key=key))[0] < S["far"]:
                i = max(now, key=key)
        return i

    def pick(e, fl):
        own = {k: r for k, r in ((k, when(k)) for k in cand[e]) if r is not None}
        if e in "va":
            if e == "a":
                own.update(fl)
            else:
                fl = {k: r for k, r in fl.items() if ops[k]["k"]["v"][0] != "vg" or quota[ops[k]["t"]] >= ops[k]["k"]["v"][1]}
            if e == "v" and fl:
                tf = max(free["v"], min(fl.values()))
                to = max(free["v"], min(own.values())) if own else 1e18
                busy = free["a"] - tf
                now = {k: r for k, r in fl.items() if r <= tf + S["slack"]}
                if busy > S["th"] or len(now) > 1:
                    if len(now) > 1 and busy <= S["th"]:
                        now.pop(max(now, key=key))
                    k = max(now, key=key)
                    if to - tf > S["frac"] * ops[k]["c"]:
                        return tf, k
                    mine = [j for j, r in own.items() if r <= to + S["slack"]]
                    if busy > S["th"] and key(k)[0] - key(max(mine, key=key))[0] > S["far2"]:
                        return tf, k
        if not own:
            return None
        t0 = max(free[e], min(own.values()))
        return t0, choose(own, t0)

    seq = []
    for step in range(n):
        best = None
        fl = {k: r for k, r in ((k, when(k)) for k in cand["f"]) if r is not None}
        for e in "xavtgs":
            p = pick(e, fl) if cand[e] or e in "av" else None
            if p is not None and (best is None or p[0] < best[0]):
                best = (p[0], p[1], e)
        t0, i, e = best
        o = ops[i]
        st = max(free[e], when(i))
        cand[o["e"]].remove(i)
        if o["e"] == "f":
            o["alt"], o["fns"] = o["k"], o["fn"]
            o["e"], o["fn"], o["k"] = e, o["fn"][e], o["k"][e]
            o["c"], o["done"], o["dm"] = price(o["k"], M)
            if o["k"][0] == "vg":
                quota[o["t"]] -= o["k"][1]
        for x in o["tiles"]:
            if x not in place:
                s = slots(x[0])[0][1]
                old = slot[x[0]][s]
                slot[x[0]][s] = x
                memo.clear()
                if x[-1] in busy_:
                    busy_[x[-1]] += 1
                place[x] = "%s%d" % (x[0], s)
                if old is not None:
                    for k in users[x]:
                        ready[k] = max(ready[k], till[old] + M["lx"])
        free[e] = st + o["c"]
        end[i] = st + o["done"]
        if o["dm"]:
            end[i] = max(end[i], free["d"] + o["dm"])
            free["d"] = end[i]
        for x in o["tiles"]:
            open_[x] -= 1
            till[x] = max(till[x], end[i])
            if open_[x] == 0:
                memo.clear()
                if x[-1] in busy_:
                    busy_[x[-1]] -= 1
        o["st"] = st
        seq.append(i)
        for k in succ[i]:
            ready[k] = max(ready[k], end[i] + lat(e, i, ops[k]["e"]))
            left[k] -= 1
            if left[k] == 0:
                cand[ops[k]["e"]].append(k)
    seq, before, place = refine(ops, seq, users)
    for x, old in before.items():
        for k in users[x]:
            ops[k]["deps"] = ops[k]["deps"] | set(users[old])
    for p, i in enumerate(seq):
        ops[i]["seq"] = p
        order[ops[i]["e"]].append(i)
    count = {}
    for e in "vatg":
        c = 0
        for i in order[e]:
            if ops[i]["sem"] is None:
                c += 1
                ops[i]["sig"] = (ESEM[e], c)
        count[ESEM[e]] = c
    for o in ops:
        if o["sem"] is not None:
            o["sig"] = o["sem"]
            count[o["sem"][0]] = o["sem"][1]
    for e in "vatgs":
        had = {}
        for i in order[e]:
            need = {}
            for j in ops[i]["deps"]:
                if e == "t" and ops[j]["e"] == "t":
                    continue
                s, v = ops[j]["sig"]
                if isinstance(v, str):
                    if s not in had:
                        need[s] = v
                elif v > had.get(s, 0) and v > need.get(s, 0):
                    need[s] = v
            had.update(need)
            ops[i]["waits"] = sorted(need.items())
    return order, count, max(end), place


def refine(ops, seq, users):
    n, E, GAP = len(ops), "vatgsx", 48
    pos = [0] * n
    for p, i in enumerate(seq):
        pos[i] = p
    reach, pre = [0] * n, [None] * n
    for i in seq:
        pre[i], r = [], 0
        for j in sorted(ops[i]["all"] if ops[i]["e"] == "x" else ops[i]["deps"], key=lambda j: -pos[j]):
            if not r >> j & 1:
                pre[i].append(j)
                r |= reach[j] | 1 << j
        reach[i] = r
    names = sorted(users)
    tiles = [[names.index(x) for x in o["tiles"]] for o in ops]
    first, base = {}, 0
    for p in POOLS:
        first[p] = range(base, base + POOLS[p][0])
        base += POOLS[p][0]
    pool = [first[x[0]] for x in names]
    eng = [E.index(o["e"]) for o in ops]
    alt = ["alt" in o for o in ops]
    sem = [o["sem"] is not None for o in ops]
    cost = [[{E.index(e): price(k, dict(M, **m)) for e, k in o.get("alt", {o["e"]: o["k"]}).items()} for o in ops] for m in MODELS]
    for c_, m in zip(cost, MODELS):
        c_.append((m["lx"], [m["ls"], m["ls"], 0.0, m["ls"], m["ls"], 0.0]))
    nt = len(names)

    post = [[] for _ in ops]
    for i in seq:
        for j in pre[i]:
            post[j].append(i)

    def run(c_, old, p0, far, given):
        lx, same = c_[n]
        end, why, marks = old[0][:], old[1][:], old[2][:p0 // GAP + 1]
        free, last, dfree, ld, slot, left, till, got, by = [x[:] if isinstance(x, list) else x for x in marks[-1]]
        for p in range(p0 // GAP * GAP, n):
            if p % GAP == 0 and p > p0:
                if p > far and old[2][p // GAP] == (free, last, dfree, ld, slot, left, till, got, by):
                    return end, why, marks + old[2][p // GAP:], old[3]
                marks.append((free[:], last[:], dfree, ld, slot[:], left[:], till[:], got[:], by[:]))
            i = seq[p]
            e = eng[i]
            c, d, dm = c_[i][e]
            r, w = free[e], -2 - last[e]
            for j in pre[i]:
                y = end[j] + (lx if (sem[j] or eng[j] != e) else same[e])
                if y > r:
                    r, w = y, j
            for x in tiles[i]:
                if got[x] is None:
                    if given is None:
                        s, y = -1, 1e18
                        for k in pool[x]:
                            h = slot[k]
                            if h < 0:
                                s, y = k, -1.0
                                break
                            if left[h] == 0 and till[h] < y:
                                s, y = k, till[h]
                        if s < 0:
                            return None
                        got[x] = (s, slot[s])
                        slot[s] = x
                    else:
                        got[x] = given[x]
                h = got[x][1]
                if h >= 0 and till[h] + lx > r:
                    r, w = till[h] + lx, by[h]
            if e < 5:
                free[e], last[e] = r + c, i
            y = r + d
            if dm:
                if dfree + dm > y:
                    y, w = dfree + dm, -2 - ld
                dfree, ld = y, i
            if y != end[i]:
                end[i] = y
                for j in post[i]:
                    if pos[j] > far:
                        far = pos[j]
            why[i] = w
            for x in tiles[i]:
                left[x] -= 1
                if y > till[x]:
                    till[x], by[x] = y, i
        return end, why, marks, got

    def both(state, p0, far):
        a = run(cost[0], state[0], p0, far, None)
        if a and a[3] != state[0][3]:
            far = n
        return a and [a] + [run(c_, s, p0, far, a[3]) for c_, s in zip(cost[1:], state[1:])]

    def path(s):
        arcs, i = [], s[0].index(max(s[0]))
        while i >= 0:
            w = s[1][i]
            if w < -1:
                w = -2 - w
                arcs.append((w, i))
            i = w
        return arcs
    seed = [S["seed"]]

    def rnd():
        seed[0] = (seed[0] * 1664525 + 1013904223) % 4294967296
        return seed[0] / 4294967296
    start = ([0.0] * 6, [-1] * 6, 0.0, -1, [-1] * base, [len(users[x]) for x in names], [0.0] * nt, [None] * nt, [-1] * nt)
    state = both([([0.0] * n, [-1] * n, [start], None)] * len(MODELS), 0, n)
    worth = lambda st: sum(m["w"] * max(s[0]) for m, s in zip(MODELS, st))
    cur, arcs = worth(state), [path(s) for s in state]
    best = (cur, seq[:], eng[:], state[0][3])
    for it in range(S["iters"]):
        a = arcs[int(rnd() * len(arcs))]
        w, i = a[int(rnd() * len(a))]
        x, old = rnd(), None
        if x < 0.12 and (alt[i] or alt[w]):
            k = i if (alt[i] and (not alt[w] or rnd() < 0.5)) else w
            eng[k] = 1 - eng[k]
            lo, hi = pos[k], max([pos[j] for j in post[k]] + [pos[k]])
        else:
            lo, hi, early = pos[w], pos[i], x < 0.6
            for _ in range(int(rnd() * rnd() * S["hop"])):
                p, step = (lo - 1, -1) if early else (hi + 1, 1)
                while 0 <= p < n and eng[seq[p]] != eng[i]:
                    p += step
                if not 0 <= p < n or (reach[i] >> seq[p] if early else reach[seq[p]] >> w) & 1:
                    break
                lo, hi = (p, hi) if early else (lo, p)
            old = seq[lo:hi + 1]
            tied = [k for k in old if (reach[i] >> k if early else reach[k] >> w) & 1]
            if (w if early else i) in tied or len(tied) > 8:
                continue
            rest = [k for k in old if k not in tied and k != (i if early else w)]
            seq[lo:hi + 1] = tied + [i] + rest if early else rest + [w] + tied
        new = both(state, lo, hi)
        c2 = worth(new) if new else 1e18
        if c2 <= cur or rnd() < math.exp((cur - c2) / (S["temp"] * max(1 - it / S["iters"], 0.02))):
            cur, state, arcs = c2, new, [path(s) for s in new]
            for p in range(lo, lo + len(old or ())):
                pos[seq[p]] = p
            if cur < best[0]:
                best = (cur, seq[:], eng[:], state[0][3])
        elif old:
            seq[lo:lo + len(old)] = old
        else:
            eng[k] = 1 - eng[k]
    for i, o in enumerate(ops):
        if alt[i]:
            e = E[best[2][i]]
            o["e"], o["k"], o["fn"] = e, o["alt"][e], o["fns"][e]
    before = {names[x]: names[g[1]] for x, g in enumerate(best[3]) if g[1] >= 0}
    return best[1], before, {names[x]: "%s%d" % (names[x][0], g[0] - pool[x][0]) for x, g in enumerate(best[3])}


_PLAN = {}


def plan():
    if not _PLAN:
        ops = build()
        order, count, total, place = schedule(ops)
        _PLAN.update(ops=ops, order=order, count=count, total=total, place=place)
    return _PLAN


def route(T, topo, src, dst):
    if topo.may_write(src, dst):
        return [dst, dst]
    ok = [c for c in topo.cores_of(src) if c != src and T.rank_of(c) is None and topo.may_write(c, dst)]
    ok.sort(key=lambda c: topo.die(c) != topo.die(src))
    return ok[:2]


def bits(engines):
    return sum(1 << e for e in engines)


def binder(T, sem):
    place = plan()["place"]

    def A(x):
        if not isinstance(x, tuple):
            return x
        if x[0] == "#ind":
            return A(x[1]).indirect(A(x[2]))
        if x[0] == "#sem":
            return sem[x[1]] if sem is not None else None
        if x[0] == "#hbm":
            return T[x[1]]
        if x[0] == "#all":
            return T[x[1]][:, :, x[2]:x[3]]
        if x[0] in ("U1", "U2"):
            return T[x[0]][:, x[1] // 512, x[1] % 512:(x[2] - 1) % 512 + 1]
        if x[0][0] == "Q":
            z, lo, hi = int(x[0][1]), x[1] // 16, x[2] // 16
            if len(x) > 4:
                return T["Q"][:, z, lo:hi, x[4]:x[4] + 4]
            return T["Q"][:, z, lo:hi, x[1] % 16] if x[3] == 16 else T["Q"][:, z, lo:hi, :]
        buf = T[place.get(x[0], x[0])]
        if x[0][:2] == "P#":
            if len(x) > 4:
                return buf[:, :, x[4], :]
            if x[1] % 128 == 0 and x[2] % 128 == 0:
                return buf[:, x[1] // 128:x[2] // 128, :, :]
            return buf[:, x[1] // 128, x[1] % 128 // 8:(x[2] - 1) % 128 // 8 + 1, :]
        if x[3] == 1:
            return buf[:, x[1]:x[2]]
        return buf[:, x[1]:x[2]:x[3]]
    return A


def rank_program(g, core, T, topo):
    pl = plan()
    ops = pl["ops"]
    cores = list(T.cores)
    n = len(cores)
    A = binder(T, T.sem)

    rank = T.rank_of(core)
    if rank is None:
        for r in range(n):
            src, dst = cores[r], cores[(r - 1) % n]
            hops = route(T, topo, src, dst)
            if core in hops:
                half = hops.index(core)
                eng = topo.engines(core, dst)
                rid, pid = topo.addr(dst, core)
                sent = 0
                for i in pl["order"]["g"]:
                    fn = ops[i]["fn"]
                    if isinstance(fn, tuple):
                        m, d = fn[1], fn[3][half]
                        g.wait_ge(T.sem["rin%d" % m], len(topo.engines(src, core)) // 2)
                        g.remote_dma(A(d), A(d), T.sem["arr%d" % m], T.sem["rl"], pid, rid, bits(eng))
                        sent += len(eng)
                g.wait_ge(T.sem["rl"], sent)
        return

    dst, src = cores[(rank - 1) % n], cores[(rank + 1) % n]
    hops = route(T, topo, core, dst)
    back = route(T, topo, src, core)
    share = len(topo.engines(core, hops[0])) // 2
    val = {"#sent": 2 * share, "#arr": sum(len(topo.engines(src, core)) // 2 if h == core else len(topo.engines(h, core)) for h in back)}
    queue = {"v": g.vector, "a": g.scalar, "t": g.tensor, "g": g, "s": g.sync}
    for e in "sagtv":
        q = queue[e]
        for i in pl["order"][e]:
            o = ops[i]
            for s, v in o["waits"]:
                q.wait_ge(T.sem[s], val.get(v, v))
            if isinstance(o["fn"], tuple):
                m, srcs, dsts, s = o["fn"][1:]
                tr = []
                for half in (0, 1):
                    rid, pid = topo.addr(hops[half], core)
                    eng = topo.engines(core, hops[half])[share * half:share * half + share]
                    tr.append(RemoteDMATransfer(dst_ids=[DstId(rid=rid, pnc=pid)], dma_engine_mask=bits(eng),
                                                remote_sem=T.sem[("arr%d" if hops[half] == dst else "rin%d") % m], src=A(srcs[half]), dst=A(dsts[half])))
                g.remote_dma_fused(tr, local_sem=T.sem[s])
            elif o["sem"] is None:
                o["fn"](q, A).then_inc(T.sem[o["sig"][0]], 1)
            else:
                o["fn"](q, A)
    for s, v in sorted(pl["count"].items()):
        g.wait_ge(T.sem[s], val.get(v, v))
